import numpy as np, ml_dtypes
CORES = [66,74,82,90,194,202,210,218]
N = 8
BF = ml_dtypes.bfloat16
V, L, T, RO, MIN = 4096, 128, 16, 4, 6
B, S = T // 16, V // L
def place(n, u, kk):
    return (((n * (2 * u + 1)) >> 5) + n + kk) & (V - 1)
def pack(X, A, z, w):
    a = np.ascontiguousarray(A.reshape(N, 8, B, 16, L).transpose(0, 1, 3, 2, 4)).reshape(N, 128, B * L)
    return {"xt": np.ascontiguousarray(X.reshape(N, 128, V)).astype(np.float32).astype(BF), "am": a.astype(np.int32),
            "zv": np.ascontiguousarray(z.reshape(N, 128, L)).astype(np.float32).astype(BF), "wt": np.ascontiguousarray(w.reshape(N, 128, 1)).astype(np.int32)}
def pools(rng, sizes):
    m = rng.choice(np.array(sizes), (N, 8, 1, L)); pool = rng.integers(0, V, (N, 8, T, L))
    return np.take_along_axis(pool, rng.integers(0, m, (N, 8, T, L)), 2)
def setup_inputs(rng):
    base = rng.integers(0, 256, (N, 8, 16, 1)).astype(np.int16); share = rng.choice(np.array([0.3, 0.5, 0.7], np.float32), (N, 8, 1, 1))
    X = np.where(rng.random((N, 8, 16, V), dtype=np.float32) < share, base, rng.integers(0, 256, (N, 8, 16, V), dtype=np.int16))
    return pack(X, pools(rng, [1, 2, 3, T, T, T, T, T]), rng.integers(0, 256, (N, 8, 16, L)), rng.integers(0, 16, (N, 8, 16)))
def setup_inputs_spread(rng):
    X = np.minimum(np.exp2(8 * rng.random((N, 8, 1, V))) * rng.random((N, 8, 16, V)), 255).astype(np.int16)
    A = np.exp2((V.bit_length() - 1) * rng.random((N, 8, T, L))).astype(np.int64) - 1
    A = np.where(rng.random((N, 8, T, L)) < rng.random((N, 8, 1, L)), V - 1 - A, A)
    z = np.minimum(np.exp2(8 * rng.random((N, 8, 1, L))) * rng.random((N, 8, 16, L)), 255).astype(np.int64)
    w = np.minimum(np.exp2(4 * rng.random((N, 8, 1))) * rng.random((N, 8, 16)), 15).astype(np.int64)
    return pack(X, A, z, w)
def setup_inputs_ends(rng):
    kd = rng.integers(0, 8, (N, 8, 1, V)); X = 255 * rng.integers(0, 2, (N, 8, 16, V), dtype=np.int16)
    kd[N - 1] = np.maximum(kd[N - 1], 2)
    X = np.where(kd == 0, 0, np.where(kd == 1, 255, X))
    full = np.all(X[N - 1] == 255, axis=1); X[N - 1, :, 15] = np.where(full, 0, X[N - 1, :, 15])
    X[::2, :, :, 0] = 255; X[1::2, :, :, 0] = 0; X[N - 1, :, :, 0] = 255
    c1 = place(V - 1, 1023, 0); X[:, 7, :, c1] = 255; X[::2, 7, :, c1] = 0; X[N - 1, 7, :, c1] = 0
    A = (V - 1) * (rng.random((N, 8, T, L)) < rng.choice(np.array([0.1, 0.5, 0.9]), (N, 8, 1, L))).astype(np.int64)
    A[:, :, 0, L - 1] = V - 1; A[:, :, T - 1, L - 1] = V - 1; A[:, :, T - 2, L - 1] = 0
    one = (V - 1) * rng.integers(0, 2, (8, 1, L)); one[:, :, 0] = 0; one[:, :, L - 1] = V - 1
    A[N - 2] = one; A[N - 1] = V - 1; A[N - 1, :, T - 1] = 0
    zk = rng.integers(0, 4, (N, 8, 1, L)); zk[..., 0] = 1; zk[..., 1] = 0; zk[..., L - 2] = 1
    z = np.where(zk == 0, 0, np.where(zk == 1, 255, 255 * rng.integers(0, 2, (N, 8, 16, L))))
    vec = np.array([255] * 13 + [30, 0, 0]); o = np.argsort(rng.random((N, 16, L)), axis=1)
    hit = rng.random((N, 1, L)) < 0.125; hit[..., L - 1] = True; hit[..., 0] = False; hit[..., 1] = False; hit[..., L - 2] = False
    z[:, 7] = np.where(hit, vec[o], z[:, 7])
    w = 15 * rng.integers(0, 2, (N, 8, 16)); w[:, 7] = 15; w[::2, 0] = 0
    return pack(X, A, z, w)
def setup_inputs_corners(rng):
    X = rng.integers(0, 256, (N, 8, 16, V), dtype=np.int16); c = np.arange(V); base = rng.choice(np.array([0, 1, 100, 255]), (N, 8, 16))
    prs = [(0, 1), (14, 15), (0, 15), (7, 8), (3, 4), (6, 9), (2, 12), (8, 15)]
    for q in range(N):
        o = rng.permutation(8)
        for g in range(8):
            p0, p1 = prs[int(o[g])]
            X[q, g, :p1] = base[q, g, :p1, None]
            X[q, g, p0] = (c >> 8) + (0 if rng.random() < 0.5 else 256 - (V >> 8)); X[q, g, p1] = c & 255
    zk = rng.integers(0, 4, (N, 8, 1, L))
    z = np.where(zk == 0, 0, np.where(zk == 1, 255, rng.integers(0, 256, (N, 8, 16, L))))
    wk = rng.integers(0, 4, (N, 8, 1)); w = np.where(wk == 0, 0, np.where(wk == 1, 15, rng.integers(0, 16, (N, 8, 16))))
    r = rng.permutation(N); z[r[0]] = 0; w[r[0]] = rng.integers(1, 16, (8, 16)); w[r[1]] = 0
    s = rng.choice(np.array([1, 2, T // 2, T // 2 + 1, T - 1, T]), (N, 8, 1, L))
    s[r[0]] = 1; s[r[1]] = 1; s[r[1], 7, 0, L - 1] = 2; s[r[2]] = T
    k = np.arange(T).reshape(1, 1, T, 1); h = V // 16 * 15 // T
    nm = k * h + rng.integers(0, h, (N, 8, T, L))
    u = np.sum(w[..., None] * z, axis=2, keepdims=True) & 1023
    nm = np.take_along_axis(nm, np.argsort(place(nm, u, 0), axis=2, kind="stable"), 2)
    A = np.take_along_axis(nm, np.where(k < T - s, k, 2 * T - 1 - s - k), 2)
    return pack(X, A, z, w)
def setup_inputs_ties(rng):
    base = rng.integers(1, 255, (N, 8, 16, 1)); base[:, 1::2] = rng.choice(np.array([1, 254]), (N, 4, 16, 1)); base = base.astype(np.int16)
    X = base + np.where(rng.random((N, 8, 16, V), dtype=np.float32) < 0.03, rng.integers(-1, 2, (N, 8, 16, V), dtype=np.int16), 0)
    A = pools(rng, [1, 2, T, T]); A[:, 0] = A[:, 0, :, :1]
    n = rng.choice(np.array([0, MIN - 1, MIN, MIN, MIN + 1, 16]), (N, 8, 1, L)); o = np.argsort(np.argsort(rng.random((N, 8, 16, L)), axis=2), axis=2)
    return pack(X, A, base.astype(np.int64) - (o >= n), rng.integers(0, 16, (N, 8, 16)))
def setup_inputs_few(rng):
    base = rng.integers(0, 256, (N, 8, 16, 1)).astype(np.int16)
    X = np.where(rng.random((N, 8, 16, V), dtype=np.float32) < 0.4, base, rng.integers(0, 256, (N, 8, 16, V), dtype=np.int16))
    A = pools(rng, [1, 2, 3, T, T, T, T, T]); w = rng.integers(0, 16, (N, 8, 16))
    q = int(rng.integers(0, N)); p = (q + 1) % N; a = rng.permutation(3) + 1
    near = [(q - d) % N for d in range((RO - 2) * (RO - 1) // 2 + 1)]
    A[near] = rng.integers(0, V, (8, 1, L)); A[p] = rng.integers(0, V, (8, 1, L))
    w[q] = 0; w[p] = 0
    nm = np.arange(V); rest = place(nm, 0, 0) % S; ok = (rest >= 1) & (rest <= S - 4)
    lows, highs = nm[ok & (nm < V // 4)], nm[ok & (nm >= V // 2) & (nm < 3 * V // 4)]
    for r, rs, kinds in ((q, near, np.repeat(np.arange(RO - 1), a[:RO - 1])), (p, [p], np.zeros(int(a[2]), np.int64))):
        for g, t in zip(rng.permutation(8), kinds):
            i = int(rng.integers(0, L)); n, m = int(rng.choice(lows)), int(rng.choice(highs))
            if rng.random() < 0.5: n, m = m, n
            for v in rs: A[v, g, :, i] = n
            A[r, g, 0, i] = m
            for j in range(int(t) + 1):
                k = 0 if j == 0 else int(a[j - 1])
                X[r, g, 0, place(n, 0, k)] = 0 if j < t else 255
                X[r, g, 0, place(m, 0, k)] = 255 if j < t else 0
    return pack(X, A, rng.integers(0, 256, (N, 8, 16, L)), w)
def check_inputs(d):
    bad = []
    for k, lo, hi in (("xt", 0, 255), ("am", 0, V - 1), ("zv", 0, 255), ("wt", 0, 15)):
        v = np.asarray(d[k]).astype(np.float64)
        if not (np.min(v) >= lo and np.max(v) <= hi and np.all(v == np.floor(v))): bad.append("range of " + k)
    return bad
def pick(X, c):
    return np.take_along_axis(X, c.reshape(N, 8, 1, T * L), 3).reshape(N, 8, 16, T, L)
def keys(v):
    out = []
    for b in (0, 8):
        h = np.zeros((N, 8, T, L), np.uint64)
        for p in range(b, b + 8): h = (h << np.uint64(8)) | v[:, :, p].astype(np.uint64)
        out.append(h)
    return out
def below(h, l, h0, l0):
    return (h < h0) | ((h == h0) & (l < l0))
def close(n, keep):
    o = np.argsort(~keep, axis=2, kind="stable")
    return np.where(np.take_along_axis(keep, o, 2), np.take_along_axis(n, o, 2), -1)
def reference(xt, am, zv, wt):
    X = xt.astype(np.float32).astype(np.int32).reshape(N, 8, 16, V)
    A = am.astype(np.int64).reshape(N, 8, 16, B, L).transpose(0, 1, 3, 2, 4).reshape(N, 8, T, L)
    z = zv.astype(np.float32).astype(np.int64).reshape(N, 8, 16, L); w = wt.astype(np.int64).reshape(N, 8, 16, 1)
    kk = np.zeros((N, 1, 1, 1), np.int64); lane = np.arange(L).reshape(1, 1, 1, L); row = np.arange(T).reshape(1, 1, T, 1)
    for t in range(RO):
        u = np.sum(w * z, axis=2, keepdims=True) & 1023
        x = pick(X, place(A, u, kk)); ha, la = keys(x)
        live = np.ones((N, 8, T, L), bool); mh, ml = ha[:, :, T - 1], la[:, :, T - 1]
        for k in range(T - 2, -1, -1):
            less = below(ha[:, :, k], la[:, :, k], mh, ml); live[:, :, k] = ~less
            mh = np.where(less, mh, ha[:, :, k]); ml = np.where(less, ml, la[:, :, k])
        alpha = close(A, live)
        first = np.argmax(live, axis=2)
        M = np.take_along_axis(x, first[:, :, None, None, :], 3)[:, :, :, 0]
        beta = np.stack([alpha[(q - 1 - t % (N - 1)) % N] for q in range(N)]); has = beta >= 0
        y = pick(X, place(np.maximum(beta, 0), u, kk)); hy, ly = keys(y)
        front = np.sum(z >= M, axis=2, keepdims=True) >= MIN
        ka = live & ~below(ha, la, hy[:, :, :1], ly[:, :, :1]); kb = has & ~below(hy, ly, mh[:, :, None], ml[:, :, None])
        names = np.where(front, np.concatenate([A, beta], axis=2), np.concatenate([beta, A], axis=2))
        keep = np.where(front, np.concatenate([ka, has], axis=2), np.concatenate([kb, live], axis=2))
        new = close(names, keep)[:, :, :T]
        A = np.where(new >= 0, new, (((A * u) >> 5) + 37 * row + u) & (V - 1))
        col = np.broadcast_to(S * lane + (u & (S - 1)), (N, 8, 16, L))
        np.put_along_axis(X, col, ((np.take_along_axis(X, col, 3) + M) >> 1).astype(np.int32), 3)
        z = np.abs(z - y[:, :, :, 0])
        kk = np.sum(~live, axis=(1, 2, 3)).reshape(N, 1, 1, 1)
    yx = np.sum(X.reshape(N, 128, 4, V // 4), axis=2)
    ya = A.reshape(N, 8, B, 16, L).transpose(0, 1, 3, 2, 4).reshape(N, 128, B * L)
    return {"yx": yx.astype(np.float32), "ya": np.ascontiguousarray(ya).astype(np.float32), "yz": z.reshape(N, 128, L).astype(np.float32)}

@@ -1,0 +1,575 @@
+from concourse.mybir import AluOpType, ActivationFunctionType
+
+RO = 4
+BIG = float(2 ** 26)
+MAGIC = 0x1111 << 11
+EMASK = (1 << 14) | (1 << 17) | (1 << 20) | (1 << 23)
+RND = float(3 << 22)
+SPLIT = 1
+M_ACT = False
+SLOT, GAP = 0, 3
+TFIRST, YCUT, REF_FIRST = True, 128, False
+CUT = 60
+
+
+def _sb(n, d):
+    return ("sbuf", [128, n], d)
+
+
+F, BF, I32, U16 = "float32", "bfloat16", "int32", "uint16"
+SCRATCH = {
+    "X": _sb(4096, BF), "xb": _sb(2048, BF), "yb": _sb(2048, BF),
+    "am_i": _sb(128, I32), "am_f": _sb(128, F), "Zb": _sb(128, BF), "Zf": _sb(128, F), "w_i": _sb(4, I32),
+    "cols": _sb(16, F), "coli": _sb(8, I32),
+    "ioj": _sb(128, F), "iog": _sb(128, F), "tvec": _sb(128, F), "tvb": _sb(128, BF), "c0": _sb(128, F), "c0b": _sb(128, BF),
+    "ETi": _sb(128, I32),
+    "If": _sb(128, F), "Rf": _sb(128, F), "Is": _sb(128 * 7, BF),
+    "Blk": _sb(128, BF), "Wblk": _sb(128, BF), "mask": _sb(128, F), "mask16": _sb(128, BF), "Lin": _sb(128, BF),
+    "l1": _sb(128, F), "l2": _sb(128, F),
+    "Sel": _sb(8, BF), "nSel": _sb(8, BF), "Sel2": _sb(8, BF), "ones": _sb(400, BF),
+    "wv": _sb(96, F), "wg": _sb(96, F), "wa": _sb(96, F), "wb": _sb(96, F), "Wp": _sb(432, BF), "Wn": _sb(384, BF),
+    "hc": _sb(384, F),
+    "oend": _sb(8, U16), "ohor": _sb(8, U16), "omA": _sb(8, U16), "omB": _sb(8, U16), "orev": _sb(8, U16),
+    "K32": _sb(4, F), "junk": _sb(128, F),
+    "P1": _sb(128, F), "P2": _sb(128, I32), "P3": _sb(128, I32), "offx": _sb(128, U16), "offy": _sb(128, U16),
+    "q1": _sb(128, F), "q2": _sb(128, F), "q3": _sb(128, BF), "c33": _sb(128, BF), "Wblk2": _sb(128, BF), "Wblk64": _sb(128, BF),
+    "r1": _sb(128, F), "r2": _sb(128, F), "kc": _sb(256, BF), "ab": _sb(128, F),
+    "ZA": _sb(128, F), "cN": _sb(128, BF), "Gu": _sb(128, BF), "offc": _sb(8, U16),
+    "f2": _sb(128, F), "f3": _sb(128, I32), "f4": _sb(128, I32), "fil": _sb(128, F),
+    "d0": _sb(136, F), "d1": _sb(136, F), "h1": _sb(128, F), "eq": _sb(128, F), "cont": _sb(128, F), "nl": _sb(128, BF),
+    "ks": _sb(128, BF), "G": _sb(128, BF), "M": _sb(128, BF), "ge": _sb(128, BF), "y0": _sb(128, BF),
+    "Ha": _sb(768, F), "Hb": _sb(768, F),
+    "thrA": _sb(128, F), "thrB": _sb(128, F), "sg": _sb(128, BF), "sg2": _sb(128, BF),
+    "nfk": _sb(128, BF),
+    "lT": _sb(128, BF), "kT": _sb(128, BF), "ZB": _sb(128, F),
+    "gea": _sb(128, BF), "keepB": _sb(128, BF), "vA": _sb(128, F),
+    "e1": _sb(128, I32), "e2": _sb(128, I32), "e3": _sb(128, I32), "e4": _sb(128, I32),
+    "a1": _sb(128, I32), "a2": _sb(128, I32), "a3": _sb(128, I32), "a4": _sb(128, I32),
+    "geF": _sb(128, BF), "cG": _sb(128, BF),
+    "O0": _sb(128, F), "O1": _sb(128, F), "Y": _sb(256, F), "m1": _sb(128, F), "m2": _sb(128, I32),
+    "xs": _sb(128, I32), "xh": _sb(128, I32),
+    "yaf": _sb(128, F), "yao": _sb(128, F), "yxo": _sb(1024, F),
+    "A": _sb(128 * (RO + 1), I32), "B": _sb(128 * RO, I32),
+    "live": _sb(128 * RO, BF), "liveB": _sb(128 * RO, BF), "offm": _sb(16 * RO, U16), "offb": _sb(16 * RO, U16),
+    "pKA": ("psum", [128, 512], F), "pKB": ("psum", [128, 512], F), "pD0": ("psum", [128, 512], F), "pD1": ("psum", [128, 512], F),
+    "pH": ("psum", [128, 512], F), "pH2": ("psum", [128, 512], F), "pT": ("psum", [128, 512], F), "pS": ("psum", [128, 512], F),
+}
+SEMAPHORES = (["cv", "ca", "cp", "cg", "ls", "ldx", "lda", "ldz", "ldw", "sta", "stz", "stx0", "stx1", "stx2", "stx3"]
+              + ["rn%d" % t for t in range(RO)] + ["rl%d" % t for t in range(RO)] + ["ro%d" % t for t in range(RO)])
+
+
+def rank_program(g, core, T, topo):
+    rank = T.rank_of(core)
+    if rank is None:
+        return
+    N = len(T.cores)
+    A_ = AluOpType
+    AF = ActivationFunctionType
+    Q = {"v": g.vector, "a": g.scalar, "p": g.tensor, "g": g, "s": g.sync}
+    own = {"v": "cv", "a": "ca", "p": "cp", "g": "cg"}
+    total = {}
+    known = {e: {} for e in Q}
+    clock = {}
+    lastw, readers, bank = {}, {}, {}
+
+    def wait(e, ev):
+        s, n = ev
+        if known[e].get(s, 0) >= n:
+            return
+        Q[e].wait_ge(T.sem[s], n)
+        known[e][s] = n
+        for s2, n2 in clock.get(ev, {}).items():
+            if known[e].get(s2, 0) < n2:
+                known[e][s2] = n2
+
+    def op(e, fn, r, w, inc=True, sem=None, by=1):
+        me = own.get(e) if sem is None else sem
+        need = {}
+
+        def add(ev, same_ok):
+            if ev is None:
+                return
+            if ev[0] == me and sem is None and (same_ok or e == "p"):
+                return
+            if need.get(ev[0], 0) < ev[1]:
+                need[ev[0]] = ev[1]
+        for k in r:
+            add(lastw.get(k), False)
+        for k in w:
+            add(lastw.get(k), False)
+            for s, n in readers.get(k, {}).items():
+                add((s, n), False)
+        banks = set(k.split(":")[0] for k in list(r) + list(w) if ":" in k)
+        for b in banks:
+            for s, n in bank.get(b, {}).items():
+                add((s, n), True)
+        for s, n in sorted(need.items(), key=lambda x: x[0] == me):
+            wait(e, (s, n))
+        ins = fn()
+        ev = (me, total.get(me, 0) + by)
+        if inc:
+            if ins is not None:
+                ins.then_inc(T.sem[me], by)
+            total[me] = ev[1]
+            clock[ev] = dict(known[e])
+        for k in r:
+            readers.setdefault(k, {})[me] = ev[1]
+        for k in w:
+            lastw[k] = ev
+            readers[k] = {}
+        for b in banks:
+            bank.setdefault(b, {})[me] = ev[1]
+
+    V, S_, PE = g.vector, g.scalar, g.tensor
+
+    def tt(out, a, b, o, r, w):
+        op("v", lambda: V.tensor_tensor(out, a, b, o), r, w)
+
+    def ts(out, a, s1, o1, r, w, s2=None, o2=None):
+        if o2 is None:
+            op("v", lambda: V.tensor_scalar(out, a, s1, None, o1), r, w)
+        else:
+            op("v", lambda: V.tensor_scalar(out, a, s1, s2, o1, o2), r, w)
+
+    def cp(out, a, r, w):
+        op("v", lambda: V.tensor_copy(out, a), r, w)
+
+    def scan(out, a, b, o1, o2, r, w):
+        op("v", lambda: V.tensor_tensor_scan(out, a, b, 0.0, o1, o2), r, w)
+
+    def ms(out, c, w):
+        op("v", lambda: V.memset(out, c), [], w)
+
+    def act(out, a, f, r, w, bias=0.0, scale=1.0, acc=None):
+        if acc is None:
+            op("a", lambda: S_.activation(out, a, f, bias=bias, scale=scale), r, w)
+        else:
+            op("a", lambda: S_.activation(out, a, f, bias=bias, scale=scale, accum_out=acc), r, w)
+
+    def mm(out, l, rh, st, sp, r, w, inc=True):
+        op("p", lambda: PE.matmul(out, l, rh, st, sp), r, w, inc=inc)
+
+    def lin(out, w, terms, first=True, final=True):
+        for j, (l, rh, r) in enumerate(terms):
+            end = j == len(terms) - 1
+            mm(out, l, rh, first and j == 0, final and end, r, [w], inc=end)
+
+    def iota(out, pat, base, cm, w, fl=True):
+        if fl:
+            op("g", lambda: g.iota(out, pat, base, cm, allow_small_or_imprecise_dtypes=True), [], w)
+        else:
+            op("g", lambda: g.iota(out, pat, base, cm), [], w)
+
+    def dma(e, out, a, sem, r, w):
+        op(e, lambda: Q[e].dma_start(out, a), r, w, sem=sem, by=16)
+
+    def peer(t, sign):
+        return T.cores[(rank + sign * (1 + t % (N - 1))) % N]
+
+    def width(src, dst):
+        return len(topo.engines(src, dst))
+
+    def send(t, src, dst, sem, r):
+        d = peer(t, 1)
+        rid, pid = topo.addr(d, core)
+
+        def fn():
+            g.remote_dma(dst, src, T.sem[sem], T.sem.ls, pid, rid, topo.mask(core, d))
+            return None
+        op("g", fn, r, [], sem="ls", by=width(core, d))
+
+    def landed(t, key, sem):
+        n = width(peer(t, -1), core)
+        total[sem] = n
+        lastw[key] = (sem, n)
+
+    def blk(buf, t, n=128):
+        return buf[:, n * t:n * t + n]
+
+    dma("s", T.am_i[:], T.am[:], "lda", [], ["am_i"])
+    dma("a", T.Zb[:], T.zv[:], "ldz", [], ["Zb"])
+    dma("a", T.w_i[:, 0:1], T.wt[:], "ldw", [], ["w_i"])
+    dma("s", T.X[:], T.xt[:], "ldx", [], ["X"])
+    for t in range(RO):
+        landed(t, "B%d" % t, "rn%d" % t)
+        landed(t, "liveB%d" % t, "rl%d" % t)
+        landed(t, "offb%d" % t, "ro%d" % t)
+
+    col = lambda j: T.cols[:, j:j + 1]
+    iota(T.coli[:, 0:1], [[0, 1]], 0, 1, ["coli0"], fl=False)
+    iota(T.ioj[:], [[1, 128]], 0, 0, ["ioj"])
+    iota(T.tvec[:], [[0, 8], [1, 16]], 0, 0, ["tvec"])
+    iota(T.iog[:], [[1, 8], [0, 16]], 0, 0, ["iog"])
+    iota(T.wv[:, 0:48], [[-3, 6], [-16, 8]], 0, 1, ["wv0"])
+    iota(T.wv[:, 48:96], [[-16, 8], [3, 6]], -15, 1, ["wv1"])
+    iota(T.wg[:, 0:48], [[0, 6], [1, 8]], 0, 0, ["wg0"])
+    iota(T.wg[:, 48:96], [[1, 8], [0, 6]], 0, 0, ["wg1"])
+    iota(T.ETi[:], [[0, 8], [-1, 16]], 15, 0, ["ETi"], fl=False)
+
+    U = T.pD1[:, 384:512]
+    KB_ = [T.pKA, T.pKB]
+    kname = ["pKA:k", "pKB:k"]
+    DX = [T.pD0, T.pD1]
+    xname = ["pD0:k", "pD1:k"]
+
+    ms(T.ones[:], 1.0, ["ones"])
+    ts(T.coli[:, 1:2], T.coli[:, 0:1], 15, A_.bitwise_and, ["coli0"], ["coli1"])
+    ts(T.coli[:, 2:3], T.coli[:, 0:1], 4, A_.arith_shift_right, ["coli0"], ["coli2"])
+    ms(T.K32[:], 0.0, ["K32"])
+    cp(T.cols[:, 0:3], T.coli[:, 0:3], ["coli0", "coli1", "coli2"], ["cols"])
+    ms(T.d0[:, 0:8], 0.0, ["d0_0"])
+    ts(col(3), col(1), -2.0, A_.mult, ["cols"], ["col3a"], 15.0, A_.add)
+    ts(T.If[:], T.ioj[:], col(0), A_.is_equal, ["ioj", "cols"], ["If"])
+    tt(col(4), col(3), col(0), A_.add, ["col3a", "cols"], ["col4"])
+    ms(T.hc[:], 2.0 ** -25, ["hc"])
+    ts(T.Rf[:], T.ioj[:], col(4), A_.is_equal, ["ioj", "col4"], ["Rf"])
+    ms(T.hc[:, 0:384:6], 0.0, ["hc"])
+    ms(T.d1[:, 0:8], 0.0, ["d1_0"])
+    ms(T.c33[:], 33.0, ["c33"])
+    ms(T.offm[:], 0, ["offm%d" % t for t in range(RO)])
+    ts(T.mask[:], T.tvec[:], col(1), A_.is_equal, ["tvec", "cols"], ["mask"])
+    ts(T.Sel[:], T.ioj[:, 0:8], col(2), A_.is_equal, ["ioj", "cols"], ["Sel"])
+    ts(T.l1[:], T.tvec[:], col(1), A_.is_lt, ["tvec", "cols"], ["l1"])
+    ts(T.Blk[:], T.iog[:], col(2), A_.is_equal, ["iog", "cols"], ["Blk"])
+
+    SC = [1.0, -1.0, 32.0, -64.0, 4096.0, 8192.0, 12288.0]
+    Id = {x: blk(T.Is, j) for j, x in enumerate(SC)}
+    act(Id[1.0], T.If[:], AF.Copy, ["If"], ["Is"])
+    act(col(6), col(0), AF.Identity, ["cols"], ["col6"], scale=16.0)
+    act(col(7), col(1), AF.Identity, ["cols"], ["col7"], scale=48.0, bias=5.0)
+    act(col(8), col(1), AF.Identity, ["cols"], ["col8"], scale=-16.0, bias=240.0)
+    act(col(9), col(1), AF.Identity, ["cols"], ["col9"], scale=-1.0, bias=15.0)
+    act(T.l2[:], T.If[:], AF.Identity, ["If", "cols"], ["l2"], scale=col(1))
+    for x in SC[1:]:
+        act(Id[x], T.If[:], AF.Identity, ["If"], ["I%d" % x], scale=x)
+
+    cp(T.am_f[:], T.am_i[:], ["am_i"], ["am_f"])
+    cp(col(5), T.w_i[:, 0:1], ["w_i"], ["col5"])
+    mm(T.pT[:, 0:128], T.am_f[:], T.Rf[:], True, True, ["am_f", "Rf"], ["pT:a"])
+    act(T.Wblk[:], T.Blk[:], AF.Identity, ["Blk", "col5"], ["Wblk"], scale=col(5))
+    ts(T.wa[:], T.wv[:], 0.0, A_.is_equal, ["wv0", "wv1"], ["wa"], 65536.0, A_.mult)
+    ts(T.wb[:], T.wv[:], 1.0, A_.is_equal, ["wv0", "wv1"], ["wb"], 256.0, A_.mult)
+    ts(T.wv[:], T.wv[:], 2.0, A_.is_equal, ["wv0", "wv1"], ["wv"])
+    cp(blk(T.A, 0), T.pT[:, 0:128], ["pT:a"], ["A0"])
+    send(0, blk(T.A, 0), blk(T.B, 0), "rn0", ["A0"])
+
+    def init_keys():
+        for b in range(2):
+            mm(KB_[b][:, 0:400], Id[1.0], T.ones[:], True, False, ["Is", "ones"], [kname[b]], inc=False)
+
+    def u1():
+        mm(T.pS[:, 0:128], T.Zb[:], T.Wblk[:], True, True, ["Zb", "Wblk"], ["pS:a"])
+        act(T.q1[:], T.pS[:, 0:128], AF.Identity, ["pS:a"], ["q1"], scale=2.0 ** -10, bias=2.0 ** -11 - 0.5)
+        act(T.q2[:], T.q1[:], AF.Identity, ["q1"], ["q2"], bias=RND)
+        act(T.q3[:], T.q2[:], AF.Identity, ["q2"], ["q3"], scale=-2048.0, bias=2048.0 * RND)
+
+        act(T.r1[:], T.pS[:, 0:128], AF.Identity, ["pS:a"], ["r1"], scale=2.0 ** -5, bias=2.0 ** -6 - 0.5)
+        act(T.r2[:], T.r1[:], AF.Identity, ["r1"], ["r2"], bias=RND)
+        act(T.r1[:], T.r2[:], AF.Identity, ["r2"], ["r1"], scale=-32.0, bias=32.0 * RND)
+
+    def u2():
+        z2, q = (T.Zb[:], T.Wblk2[:], ["Zb", "Wblk2"]), (Id[1.0], T.q3[:], ["Is", "q3"])
+        lin(U, "pD1:U", [z2, (Id[1.0], T.c33[:], ["Is", "c33"]), q])
+
+    def u3():
+        z2, q = (T.Zb[:], T.Wblk2[:], ["Zb", "Wblk2"]), (Id[1.0], T.q3[:], ["Is", "q3"])
+        lin(T.pD1[:, 0:128], "pD1:V", [z2, q])
+        lin(T.pD1[:, 128:256], "pD1:C", [(T.Zb[:], T.Wblk64[:], ["Zb", "Wblk64"]), (Id[32.0], T.q3[:], ["I32", "q3"]),
+                                         (Id[1.0], T.kc[:, 0:128], ["kc"]), (Id[1.0], T.kc[:, 128:256], ["kc2"])])
+        lin(T.pD1[:, 256:384], "pD1:u", [(T.Zb[:], T.Wblk[:], ["Zb", "Wblk"]), (T.If[:], T.r1[:], ["If", "r1"])])
+
+    act(T.Wblk2[:], T.Wblk[:], AF.Identity, ["Wblk"], ["Wblk2"], scale=2.0)
+    u1()
+    init_keys()
+    u2()
+    act(T.Wblk64[:], T.Wblk[:], AF.Identity, ["Wblk"], ["Wblk64"], scale=64.0)
+    act(T.kc[:, 0:128], T.tvec[:], AF.Identity, ["tvec"], ["kc"], scale=-2048.0, bias=15 * 2048.0)
+    act(T.kc[:, 128:256], T.tvec[:], AF.Identity, ["tvec"], ["kc2"], scale=-320.0, bias=15 * 320.0)
+    tt(T.wa[:], T.wa[:], T.wb[:], A_.add, ["wa", "wb"], ["wa"])
+    ts(T.wg[:], T.wg[:], col(2), A_.is_equal, ["wg0", "wg1", "cols"], ["wg"])
+    tt(T.wa[:], T.wa[:], T.wv[:], A_.add, ["wa", "wv"], ["wa"])
+    tt(T.Wp[:, 0:96], T.wa[:], T.wg[:], A_.mult, ["wa", "wg"], ["Wp"])
+    ts(T.c0[:], T.tvec[:], 1.0, A_.min, ["tvec"], ["c0"])
+    ts(T.e1[:], T.ETi[:], float(MAGIC), A_.mult, ["ETi"], ["e1"])
+    ts(T.oend[:], T.ioj[:, 0:8], 16.0, A_.mult, ["ioj"], ["oend"], 15.0, A_.add)
+    ts(T.e2[:], T.e1[:], EMASK, A_.bitwise_and, ["e1"], ["e2"])
+    tt(T.l1[:], T.l1[:], T.Blk[:], A_.mult, ["l1", "Blk"], ["l1"])
+    ts(T.pH2[:, 256:384], T.e2[:], 4096.0, A_.add, ["e2"], ["pH2:ET"])
+
+    def more_constants():
+        act(T.mask16[:], T.mask[:], AF.Identity, ["mask", "col6"], ["mask16"], scale=col(6))
+        act(T.nSel[:], T.Sel[:], AF.Identity, ["Sel"], ["nSel"], scale=-1.0)
+        act(T.Sel2[:], T.Sel[:], AF.Identity, ["Sel"], ["Sel2"], scale=2.0)
+        act(T.tvb[:], T.tvec[:], AF.Copy, ["tvec"], ["tvb"])
+        act(T.Wp[:, 96:144], T.Wp[:, 48:96], AF.Copy, ["Wp"], ["Wp1"])
+        act(T.c0b[:], T.c0[:], AF.Copy, ["c0"], ["c0b"])
+        act(T.Wp[:, 144:240], T.Wp[:, 48:144], AF.Copy, ["Wp", "Wp1"], ["Wp2"])
+        act(T.Wp[:, 240:432], T.Wp[:, 48:240], AF.Copy, ["Wp", "Wp1", "Wp2"], ["Wp3"])
+
+    def late_constants():
+        ts(T.ohor[:], T.ioj[:, 0:8], 6.0, A_.mult, ["ioj", "col7"], ["ohor"], col(7), A_.add)
+        ts(T.omA[:], T.ioj[:, 0:8], col(8), A_.add, ["ioj", "col8"], ["omA"])
+        ts(T.omB[:], T.ioj[:, 0:8], col(8), A_.add, ["ioj", "col8"], ["omB"], 8.0, A_.add)
+        ts(T.orev[:], T.ioj[:, 0:8], 16.0, A_.mult, ["ioj", "col9"], ["orev"], col(9), A_.add)
+        act(T.Wn[:], T.Wp[:, 48:432], AF.Identity, ["Wp", "Wp1", "Wp2", "Wp3"], ["Wn"], scale=-1.0)
+        tt(T.Lin[:], T.l1[:], T.l2[:], A_.subtract, ["l1", "l2"], ["Lin"])
+
+    h = T.pH[:, 0:128]
+    Eb = [256, 384]
+    O = [T.O0, T.O1]
+    dd = [T.d0, T.d1]
+    WT = ["Wp", "Wp1", "Wp2", "Wp3"]
+    W_ = 128 // SPLIT
+    parts = [(j, W_ * j, W_ * j + W_) for j in range(SPLIT)]
+    allp = lambda n: [n + "_%d" % j for j in range(SPLIT)]
+
+    for t in range(RO):
+        last = t == RO - 1
+        A, B = blk(T.A, t), blk(T.B, t)
+        kA, kB = "A%d" % t, "B%d" % t
+        live, liveB = blk(T.live, t), blk(T.liveB, t)
+        klive, kliveB = "live%d" % t, "liveB%d" % t
+        offm, offb = T.offm[:, 16 * t:16 * t + 8], T.offb[:, 16 * t:16 * t + 8]
+        koffm, koffb = "offm%d" % t, "offb%d" % t
+        Xw = T.X[:, 0:4096]
+
+        tt(T.P1[:], A, U, A_.mult, [kA, "pD1:U"], ["P1"])
+        mm(T.pT[:, 0:128 - CUT], T.P1[:], T.If[:, CUT:128], True, True, ["P1", "If"], ["pT:a"])
+        mm(T.pS[:, 0:CUT], T.P1[:], T.If[:, 0:CUT], True, True, ["P1", "If"], ["pS:a"])
+        if t == 0:
+            u3()
+        else:
+            tt(T.f2[:], A, T.pD1[:, 0:128], A_.mult, [kA, "pD1:V"], ["f2"])
+        ts(T.P2[:, CUT:128], T.pT[:, 0:128 - CUT], T.K32[:, 0:1], A_.add, ["pT:a", "K32"], ["P2b"])
+        ts(T.P3[:, CUT:128], T.P2[:, CUT:128], 5, A_.arith_shift_right, ["P2b"], ["P3b"], 4095, A_.bitwise_and)
+        ts(T.P2[:, 0:CUT], T.pS[:, 0:CUT], T.K32[:, 0:1], A_.add, ["pS:a", "K32"], ["P2a"])
+        cp(T.offx[:, CUT:128], T.P3[:, CUT:128], ["P3b"], ["offx1"])
+        ts(T.P3[:, 0:CUT], T.P2[:, 0:CUT], 5, A_.arith_shift_right, ["P2a"], ["P3a"], 4095, A_.bitwise_and)
+        cp(T.offx[:, 0:CUT], T.P3[:, 0:CUT], ["P3a"], ["offx0"])
+        if t == 0:
+            more_constants()
+        act(T.xb[:, 16 * CUT:2048], Xw.indirect(T.offx[:, CUT:128]), AF.Copy, ["X", "offx1"], ["xb1"])
+        cp(T.xb[:, 0:16 * CUT], Xw.indirect(T.offx[:, 0:CUT]), ["X", "offx0"], ["xb0"])
+        for j in range(16):
+            mm(T.pKA[:, 8 + j:8 + j + 369:16], T.xb[:, j:2048:16], T.Wp[:, 0:24], False, j == 15, ["xb0", "xb1", "Wp"], ["pKA:k"], inc=j == 15)
+        if t == 0:
+            tt(T.f2[:], A, T.pD1[:, 0:128], A_.mult, [kA, "pD1:V"], ["f2"])
+        tt(T.Gu[:], T.pD1[:, 256:384], T.mask[:], A_.mult, ["pD1:u", "mask"], ["Gu"])
+        tt(T.f3[:], T.f2[:], T.pD1[:, 128:256], A_.add, ["f2", "pD1:C"], ["f3"])
+        if t == 0:
+            late_constants()
+        ts(T.f4[:], T.f3[:], 6, A_.arith_shift_right, ["f3"], ["f4"], 4095, A_.bitwise_and)
+        tt(T.fil[:], T.f4[:], T.pH2[:, 256:384], A_.add, ["f4", "pH2:ET"], ["fil"])
+        def keys_b():
+            for j in range(16):
+                mm(T.pKB[:, 8 + j:8 + j + 369:16], T.xb[:, j:2048:16], T.Wp[:, 24:48], False, j == 15,
+                   ["xb0", "xb1", "Wp"], ["pKB:k"], inc=j == 15)
+
+        if not TFIRST:
+            keys_b()
+
+        def b1():
+            tt(T.P1[:], B, U, A_.mult, [kB, "pD1:U"], ["P1"])
+            mm(T.pT[:, 0:128], T.P1[:], T.If[:], True, True, ["P1", "If"], ["pT:a"])
+            if TFIRST:
+                keys_b()
+            lin(T.pS[:, 256:264], "pS:c", [(T.mask16[:], T.Sel2[:], ["mask16", "Sel2"]), (T.Gu[:], T.Sel[:], ["Gu", "Sel"])])
+            for j in range(16):
+                mm(DX[j // 8][:, 48 * (j % 8):48 * (j % 8) + 48], T.xb[:, j:2048:16], T.Wp[:, 48:96], j % 8 == 0, False,
+                   ["xb0", "xb1", "Wp"], [xname[j // 8]], inc=False)
+
+        def b2():
+            ts(T.P2[:], T.pT[:, 0:128], T.K32[:, 0:1], A_.add, ["pT:a", "K32"], ["P2a", "P2b"])
+            mm(T.pT[:, 264:272], T.mask16[:], T.Sel[:], True, False, ["mask16", "Sel"], ["pT:m"], inc=False)
+
+        def b3():
+            ts(T.P3[:], T.P2[:], 5, A_.arith_shift_right, ["P2a", "P2b"], ["P3a", "P3b"], 4095, A_.bitwise_and)
+
+        def b4():
+            cp(T.offy[:], T.P3[:], ["P3a", "P3b"], ["offy"])
+            act(T.yb[:, 0:16 * YCUT], Xw.indirect(T.offy[:, 0:YCUT]), AF.Copy, ["X", "offy"], ["yb"])
+
+        def b5():
+            cp(T.offc[:], T.pS[:, 256:264], ["pS:c"], ["offc"])
+
+        slots = {SLOT: b1, SLOT + GAP: b2, SLOT + GAP + 1: b3, SLOT + GAP + 2: b4, 12: b5}
+
+        def slot(n):
+            if n in slots:
+                slots[n]()
+
+        slot(0)
+
+        for l in range(6):
+            kb, kn = KB_[l // 3], kname[l // 3]
+            c = 8 + 128 * (l % 3)
+            if l == 0:
+                for j, a, b in parts:
+                    scan(T.h1[:, a:b], kb[:, c - 1 + a:c - 1 + b], T.c0[:, a:b], A_.max, A_.mult, [kn, "c0"], ["h1_%d" % j])
+                slot(1)
+                for j, a, b in parts:
+                    tt(T.eq[:, a:b], kb[:, c + a:c + b], T.h1[:, a:b], A_.is_ge, [kn, "h1_%d" % j], ["eq_%d" % j])
+                for j, a, b in parts:
+                    tt(T.cont[:, a:b], kb[:, c + a:c + b], T.h1[:, a:b], A_.is_le, [kn, "h1_%d" % j], ["cont_%d" % j])
+                slot(2)
+                continue
+            d, kd = dd[l % 2], "d%d" % (l % 2)
+            for j, a, b in parts:
+                tt(d[:, 8 + a:8 + b], kb[:, c + a:c + b], T.eq[:, a:b], A_.mult, [kn, "eq_%d" % j], [kd + "_%d" % j])
+            slot(3 * l)
+            for j, a, b in parts:
+                scan(T.pH[:, a:b], d[:, 7 + a:7 + b], T.cont[:, a:b], A_.max, A_.mult,
+                     [kd + "_%d" % j, kd + "_%d" % max(j - 1, 0), "cont_%d" % j], ["pH:h_%d" % j])
+            slot(3 * l + 1)
+            if l < 5:
+                for j, a, b in parts:
+                    tt(T.eq[:, a:b], d[:, 8 + a:8 + b], T.pH[:, a:b], A_.is_ge, [kd + "_%d" % j, "pH:h_%d" % j], ["eq_%d" % j])
+                for j, a, b in parts:
+                    tt(T.cont[:, a:b], d[:, 8 + a:8 + b], T.pH[:, a:b], A_.is_le, [kd + "_%d" % j, "pH:h_%d" % j], ["cont_%d" % j])
+                slot(3 * l + 2)
+            else:
+                dk = allp(kd) + allp("pH:h")
+                tt(T.nl[:], d[:, 8:136], h, A_.is_lt, dk, ["nl"])
+                tt(live, d[:, 8:136], h, A_.is_ge, dk, [klive])
+                scan(T.ks[:], T.nl[:], T.nl[:], A_.mult, A_.add, ["nl"], ["ks"])
+        send(t, live, liveB, "rl%d" % t, [klive])
+
+        tt(T.G[:], T.ks[:].indirect(T.oend[:]), T.mask[:], A_.mult, ["ks", "oend", "mask"], ["G"])
+        lin(T.pS[:, 384:512], "pS:d", [(live, Id[1.0], [klive])])
+        mm(T.pT[:, 264:272], T.G[:], T.nSel[:], False, True, ["G", "nSel"], ["pT:m"])
+        ts(offm, T.pT[:, 264:272], 15.0, A_.add, ["pT:m"], [koffm])
+        send(t, T.offm[:, 16 * t:16 * t + 16], T.offb[:, 16 * t:16 * t + 16], "ro%d" % t, [koffm])
+        act(T.lT[:], T.pS[:, 384:512], AF.Copy, ["pS:d"], ["lT"])
+        if M_ACT:
+            act(T.M[:], T.xb[:, 0:2048].indirect(offm), AF.Copy, ["xb0", "xb1", koffm], ["M"])
+        else:
+            cp(T.M[:], T.xb[:, 0:2048].indirect(offm), ["xb0", "xb1", koffm], ["M"])
+        if YCUT < 128:
+            cp(T.yb[:, 16 * YCUT:2048], Xw.indirect(T.offy[:, YCUT:128]), ["X", "offy"], ["yb2"])
+        tt(T.ge[:], T.Zb[:], T.M[:], A_.is_ge, ["Zb", "M"], ["ge"])
+        tt(T.xs[:], Xw.indirect(T.offc[:]), T.M[:], A_.add, ["X", "offc", "M"], ["xs"])
+
+        def ykeys(b, first):
+            for j in range(8):
+                mm(KB_[b][:, 48 * j:48 * j + 48], T.yb[:, 8 * b + j:2048:16], T.Wn[:, 0:48], first and j == 0, not first and j == 7,
+                   ["yb", "yb2", "Wn"], [kname[b]], inc=not first and j == 7)
+
+        def yref(b, first):
+            mm(KB_[b][:, 0:384], T.M[:], T.Wp[:, 48:432], first, not first, ["M"] + WT, [kname[b]], inc=not first)
+
+        gb = (T.ge[:], T.Blk[:], ["ge", "Blk"])
+        tv = (Id[1.0], T.tvb[:], ["tvb"])
+        if REF_FIRST:
+            yref(0, True)
+            yref(1, True)
+            ykeys(0, False)
+            lin(T.pS[:, 0:128], "pS:a", [gb])
+            ykeys(1, False)
+        else:
+            ykeys(0, True)
+            yref(0, False)
+            lin(T.pS[:, 0:128], "pS:a", [gb])
+            ykeys(1, True)
+            yref(1, False)
+        act(T.thrB[:], T.pS[:, 0:128], AF.Relu, ["pS:a"], ["thrB"], bias=-5.0 * BIG, scale=BIG)
+        act(T.sg[:], T.pS[:, 0:128], AF.Sign, ["pS:a"], ["sg"], bias=5.5, scale=-1.0)
+        lin(T.pS[:, 256:384], "pS:c", [gb, (Id[-64.0], live, [klive, "I-64"])])
+        lin(T.pT[:, 0:128], "pT:a", [tv, (T.lT[:], T.Lin[:], ["lT", "Lin"])])
+        act(T.pH[:, 128:256], T.sg[:], AF.Identity, ["sg"], ["pH:nf"], bias=0.5, scale=0.5)
+        act(T.sg2[:], T.pS[:, 256:384], AF.Sign, ["pS:c"], ["sg2"], bias=-58.5, scale=-1.0)
+        act(T.ab[:], T.pS[:, 256:384], AF.Abs, ["pS:c"], ["ab"], bias=53.0)
+        act(T.pH[:, 256:384], T.sg2[:], AF.Identity, ["sg2"], ["pH:E0a", "pH:E0b"], bias=4096.0, scale=4096.0)
+        act(T.ZA[:], T.pT[:, 0:128], AF.Copy, ["pT:a"], ["ZA"])
+        act(T.thrA[:], T.ab[:], AF.Relu, ["ab"], ["thrA"], bias=-5.5 * BIG, scale=BIG)
+        ts(T.xh[:], T.xs[:], 1, A_.arith_shift_right, ["xs"], ["xh"])
+        scan(T.Ha[:, 0:384], T.hc[:], KB_[0][:, 0:384], A_.mult, A_.add, ["hc", kname[0]], ["Ha0"])
+        cp(Xw.indirect(T.offc[:]), T.xh[:], ["xh", "offc"], ["X"])
+        scan(T.Ha[:, 384:768], T.hc[:], KB_[1][:, 0:384], A_.mult, A_.add, ["hc", kname[1]], ["Ha1"])
+        tt(T.gea[:], T.Ha[:].indirect(T.ohor[:]), T.thrB[:], A_.is_le, ["Ha0", "Ha1", "ohor", "thrB"], ["gea"])
+
+        def yx_sum(c, ps, key):
+            for q in range(4):
+                mm(ps, Id[1.0], T.X[:, 1024 * q + 256 * c:1024 * q + 256 * c + 256], q == 0, q == 3, ["X"], [key], inc=q == 3)
+
+        def yx_out(c, ps, key):
+            act(T.yxo[:, 256 * c:256 * c + 256], ps, AF.Copy, [key], ["yxo%d" % c])
+            dma("s", T.yx[:, 256 * c:256 * c + 256], T.yxo[:, 256 * c:256 * c + 256], "stx%d" % c, ["yxo%d" % c], [])
+
+        tt(T.keepB[:], T.gea[:], liveB, A_.mult, ["gea", kliveB], ["keepB"])
+        tt(h, A, T.pH[:, 256:384], A_.add, [kA, "pH:E0a", "pH:E0b"], allp("pH:h"))
+        tt(T.nfk[:], T.keepB[:], T.pH[:, 128:256], A_.mult, ["keepB", "pH:nf"], ["nfk"])
+        scan(T.cN[:], T.c0b[:], T.nfk[:], A_.mult, A_.add, ["c0b", "nfk"], ["cN"])
+        lin(T.pKA[:, 0:128], "pKA:k", [(T.keepB[:], Id[1.0], ["keepB"])])
+        lin(T.pKB[:, 0:128], "pKB:k", [(Id[8192.0], T.keepB[:], ["keepB", "I8192"]), (Id[4096.0], T.nfk[:], ["nfk", "I4096"])])
+        act(T.y0[:], T.yb[:, 0:2048].indirect(offb), AF.Copy, ["yb", "yb2", koffb], ["y0"])
+        act(T.kT[:], T.pKA[:, 0:128], AF.Copy, ["pKA:k"], ["kT"])
+        tt(T.a1[:], T.cN[:].indirect(T.oend[:]), T.ZA[:], A_.add, ["cN", "oend", "ZA"], ["a1"])
+        tt(T.pH2[:, 384:512], T.pKB[:, 0:128], B, A_.add, ["pKB:k", kB], ["pH2:nB"])
+        ts(T.a2[:], T.a1[:], 15, A_.bitwise_and, ["a1"], ["a2"])
+        mm(DX[0][:, 0:384], T.y0[:], T.Wn[:], False, True, ["y0", "Wn"], [xname[0]])
+        mm(DX[1][:, 0:384], T.y0[:], T.Wn[:], False, True, ["y0", "Wn"], [xname[1]])
+        lin(T.pKA[:, 256:384], "pKA:k", [tv, (T.kT[:], T.Lin[:], ["kT", "Lin"])])
+        lin(T.pS[:, 256:384], "pS:c", [(Id[1.0], T.Zb[:], ["Zb"]), (Id[-1.0], T.y0[:], ["y0", "I-1"])])
+        ts(T.a3[:], T.a2[:], float(MAGIC), A_.mult, ["a2"], ["a3"])
+        scan(T.Hb[:, 0:384], T.hc[:], DX[0][:, 0:384], A_.mult, A_.add, ["hc", xname[0]], ["Hb0"])
+        ts(T.a4[:], T.a3[:], EMASK, A_.bitwise_and, ["a3"], ["a4"])
+        scan(T.Hb[:, 384:768], T.hc[:], DX[1][:, 0:384], A_.mult, A_.add, ["hc", xname[1]], ["Hb1"])
+        act(T.ZB[:], T.pKA[:, 256:384], AF.Copy, ["pKA:k"], ["ZB"])
+        if last:
+            act(T.Zf[:], T.pS[:, 256:384], AF.Abs, ["pS:c"], ["Zf"])
+            dma("s", T.yz[:], T.Zf[:], "stz", ["Zf"], [])
+            yx_sum(0, T.pKB[:, 0:256], kname[1])
+            yx_out(0, T.pKB[:, 0:256], kname[1])
+        else:
+            act(T.Zb[:], T.pS[:, 256:384], AF.Abs, ["pS:c"], ["Zb"])
+        tt(T.geF[:], T.Hb[:].indirect(T.ohor[:]), T.thrA[:], A_.is_ge, ["Hb0", "Hb1", "ohor", "thrA"], ["geF"])
+        if not last:
+            u1()
+        lin(T.pT[:, 384:512], "pT:p", [(Id[12288.0], T.geF[:], ["geF", "I12288"])])
+        scan(T.cG[:], T.c0b[:], T.geF[:], A_.mult, A_.add, ["c0b", "geF"], ["cG"])
+        tt(T.vA[:], T.a4[:], h, A_.add, ["a4"] + allp("pH:h"), ["vA"])
+        tt(T.e1[:], T.cG[:].indirect(T.oend[:]), T.ZB[:], A_.add, ["cG", "oend", "ZB"], ["e1"])
+        ts(T.e2[:], T.e1[:], 15, A_.bitwise_and, ["e1"], ["e2"])
+        if last:
+            for x in [(1, T.pD0[:, 0:256], xname[0]), (2, T.pD1[:, 0:256], xname[1]), (3, T.pKA[:, 0:256], kname[0])]:
+                yx_sum(*x)
+                yx_out(*x)
+        else:
+            mm(T.pD0[:, 0:128], T.ones[:, 0:128], T.nl[:], True, True, ["ones", "nl"], [xname[0]])
+            act(T.junk[:], T.pD0[:, 0:128], AF.Identity, [xname[0]], ["junk", "K32"], scale=32.0, acc=T.K32[:, 0:1])
+            init_keys()
+            u2()
+            u3()
+        tt(T.pH[:, 256:320], T.vA[:, 0:128:2], T.pT[:, 384:512:2], A_.add, ["vA", "pT:p"], ["pH:E0a"])
+        ts(T.e3[:], T.e2[:], float(MAGIC), A_.mult, ["e2"], ["e3"])
+        tt(T.O0[:, 0:64], T.vA[:, 1:128:2], T.pT[:, 385:512:2], A_.add, ["vA", "pT:p"], ["O0a"])
+        ts(T.e4[:], T.e3[:], EMASK, A_.bitwise_and, ["e3"], ["e4"])
+        tt(T.pH[:, 320:384], T.e4[:, 0:128:2], T.pH2[:, 384:512:2], A_.add, ["e4", "pH2:nB"], ["pH:E0b"])
+        tt(T.O0[:, 64:128], T.e4[:, 1:128:2], T.pH2[:, 385:512:2], A_.add, ["e4", "pH2:nB"], ["O0b"])
+
+        for s in range(3):
+            i, o = s % 2, 1 - s % 2
+            rk = ["pH:E%da" % i, "pH:E%db" % i, "O%da" % i, "O%db" % i]
+            e0, e1 = T.pH[:, Eb[i]:Eb[i] + 128:2], T.pH[:, Eb[i] + 1:Eb[i] + 128:2]
+            o0, o1 = O[i][:, 0:128:2], O[i][:, 1:128:2]
+            tt(T.pH[:, Eb[o]:Eb[o] + 64], e0, o0, A_.min, rk, ["pH:E%da" % o])
+            tt(O[o][:, 0:64], e1, o1, A_.min, rk, ["O%da" % o])
+            tt(T.pH[:, Eb[o] + 64:Eb[o] + 128], e0, o0, A_.max, rk, ["pH:E%db" % o])
+            tt(O[o][:, 64:128], e1, o1, A_.max, rk, ["O%db" % o])
+        rk = ["pH:E1a", "pH:E1b", "O1a", "O1b"]
+        tt(T.Y[:, 0:128], T.pH[:, 384:512], T.O1[:], A_.min, rk, ["Ya"])
+        tt(T.Y[:, 128:256], T.pH[:, 384:512], T.O1[:], A_.max, rk, ["Yb"])
+        tt(T.m1[:], T.Y[:].indirect(T.omA[:]), T.fil[:], A_.max, ["Ya", "Yb", "omA", "fil"], ["m1"])
+        tt(T.m2[:], T.Y[:].indirect(T.omB[:]), T.m1[:], A_.max, ["Ya", "Yb", "omB", "m1"], ["m2"])
+        An, kAn = blk(T.A, t + 1), "A%d" % (t + 1)
+        ts(An, T.m2[:], 4095, A_.bitwise_and, ["m2"], [kAn])
+        if not last:
+            send(t + 1, An, blk(T.B, t + 1), "rn%d" % (t + 1), [kAn])
+        else:
+            cp(T.yaf[:], An.indirect(T.orev[:]), [kAn, "orev"], ["yaf"])
+            mm(T.pT[:, 0:128], T.yaf[:], T.If[:], True, True, ["yaf", "If"], ["pT:a"])
+            cp(T.yao[:], T.pT[:, 0:128], ["pT:a"], ["yao"])
+            dma("a", T.ya[:], T.yao[:], "sta", ["yao"], [])
+
+    for s in sorted(total):
+        wait("g", (s, total[s]))

@@ -5,11 +5,12 @@ BIG = float(2 ** 26)
 MAGIC = 0x1111 << 11
 EMASK = (1 << 14) | (1 << 17) | (1 << 20) | (1 << 23)
 RND = float(3 << 22)
-SPLIT = 1
+SPLIT = 2
 M_ACT = False
+KT_FIRST = True
 SLOT, GAP = 0, 3
 TFIRST, YCUT, REF_FIRST = True, 128, False
-CUT = 60
+CUT = 58
 
 
 def _sb(n, d):
@@ -290,11 +291,11 @@ def rank_program(g, core, T, topo):
     tt(T.wa[:], T.wa[:], T.wv[:], A_.add, ["wa", "wv"], ["wa"])
     tt(T.Wp[:, 0:96], T.wa[:], T.wg[:], A_.mult, ["wa", "wg"], ["Wp"])
     ts(T.c0[:], T.tvec[:], 1.0, A_.min, ["tvec"], ["c0"])
-    ts(T.e1[:], T.ETi[:], float(MAGIC), A_.mult, ["ETi"], ["e1"])
+    ts(T.a1[:], T.ETi[:], float(MAGIC), A_.mult, ["ETi"], ["a1"])
     ts(T.oend[:], T.ioj[:, 0:8], 16.0, A_.mult, ["ioj"], ["oend"], 15.0, A_.add)
-    ts(T.e2[:], T.e1[:], EMASK, A_.bitwise_and, ["e1"], ["e2"])
+    ts(T.a2[:], T.a1[:], EMASK, A_.bitwise_and, ["a1"], ["a2"])
     tt(T.l1[:], T.l1[:], T.Blk[:], A_.mult, ["l1", "Blk"], ["l1"])
-    ts(T.pH2[:, 256:384], T.e2[:], 4096.0, A_.add, ["e2"], ["pH2:ET"])
+    ts(T.pH2[:, 256:384], T.a2[:], 4096.0, A_.add, ["a2"], ["pH2:ET"])
 
     def more_constants():
         act(T.mask16[:], T.mask[:], AF.Identity, ["mask", "col6"], ["mask16"], scale=col(6))
@@ -321,6 +322,7 @@ def rank_program(g, core, T, topo):
     WT = ["Wp", "Wp1", "Wp2", "Wp3"]
     W_ = 128 // SPLIT
     parts = [(j, W_ * j, W_ * j + W_) for j in range(SPLIT)]
+    oend = T.oend[:, 0:W_ // 16]
     allp = lambda n: [n + "_%d" % j for j in range(SPLIT)]
 
     for t in range(RO):
@@ -429,14 +431,17 @@ def rank_program(g, core, T, topo):
                 slot(3 * l + 2)
             else:
                 dk = allp(kd) + allp("pH:h")
-                tt(T.nl[:], d[:, 8:136], h, A_.is_lt, dk, ["nl"])
+                for j, a, b in parts:
+                    tt(T.nl[:, a:b], d[:, 8 + a:8 + b], T.pH[:, a:b], A_.is_lt, [kd + "_%d" % j, "pH:h_%d" % j], ["nl_%d" % j])
                 tt(live, d[:, 8:136], h, A_.is_ge, dk, [klive])
-                scan(T.ks[:], T.nl[:], T.nl[:], A_.mult, A_.add, ["nl"], ["ks"])
+                for j, a, b in parts:
+                    scan(T.ks[:, a:b], T.nl[:, a:b], T.nl[:, a:b], A_.mult, A_.add, ["nl_%d" % j], ["ks_%d" % j])
         send(t, live, liveB, "rl%d" % t, [klive])
 
-        tt(T.G[:], T.ks[:].indirect(T.oend[:]), T.mask[:], A_.mult, ["ks", "oend", "mask"], ["G"])
+        for j, a, b in parts:
+            tt(T.G[:, a:b], T.ks[:, a:b].indirect(oend), T.mask[:, a:b], A_.mult, ["ks_%d" % j, "oend", "mask"], ["G_%d" % j])
         lin(T.pS[:, 384:512], "pS:d", [(live, Id[1.0], [klive])])
-        mm(T.pT[:, 264:272], T.G[:], T.nSel[:], False, True, ["G", "nSel"], ["pT:m"])
+        mm(T.pT[:, 264:272], T.G[:], T.nSel[:], False, True, allp("G") + ["nSel"], ["pT:m"])
         ts(offm, T.pT[:, 264:272], 15.0, A_.add, ["pT:m"], [koffm])
         send(t, T.offm[:, 16 * t:16 * t + 16], T.offb[:, 16 * t:16 * t + 16], "ro%d" % t, [koffm])
         act(T.lT[:], T.pS[:, 384:512], AF.Copy, ["pS:d"], ["lT"])
@@ -467,9 +472,9 @@ def rank_program(g, core, T, topo):
             ykeys(1, False)
         else:
             ykeys(0, True)
+            ykeys(1, True)
             yref(0, False)
             lin(T.pS[:, 0:128], "pS:a", [gb])
-            ykeys(1, True)
             yref(1, False)
         act(T.thrB[:], T.pS[:, 0:128], AF.Relu, ["pS:a"], ["thrB"], bias=-5.0 * BIG, scale=BIG)
         act(T.sg[:], T.pS[:, 0:128], AF.Sign, ["pS:a"], ["sg"], bias=5.5, scale=-1.0)
@@ -481,11 +486,11 @@ def rank_program(g, core, T, topo):
         act(T.pH[:, 256:384], T.sg2[:], AF.Identity, ["sg2"], ["pH:E0a", "pH:E0b"], bias=4096.0, scale=4096.0)
         act(T.ZA[:], T.pT[:, 0:128], AF.Copy, ["pT:a"], ["ZA"])
         act(T.thrA[:], T.ab[:], AF.Relu, ["ab"], ["thrA"], bias=-5.5 * BIG, scale=BIG)
-        ts(T.xh[:], T.xs[:], 1, A_.arith_shift_right, ["xs"], ["xh"])
         scan(T.Ha[:, 0:384], T.hc[:], KB_[0][:, 0:384], A_.mult, A_.add, ["hc", kname[0]], ["Ha0"])
-        cp(Xw.indirect(T.offc[:]), T.xh[:], ["xh", "offc"], ["X"])
         scan(T.Ha[:, 384:768], T.hc[:], KB_[1][:, 0:384], A_.mult, A_.add, ["hc", kname[1]], ["Ha1"])
+        ts(T.xh[:], T.xs[:], 1, A_.arith_shift_right, ["xs"], ["xh"])
         tt(T.gea[:], T.Ha[:].indirect(T.ohor[:]), T.thrB[:], A_.is_le, ["Ha0", "Ha1", "ohor", "thrB"], ["gea"])
+        cp(Xw.indirect(T.offc[:]), T.xh[:], ["xh", "offc"], ["X"])
 
         def yx_sum(c, ps, key):
             for q in range(4):
@@ -495,57 +500,71 @@ def rank_program(g, core, T, topo):
             act(T.yxo[:, 256 * c:256 * c + 256], ps, AF.Copy, [key], ["yxo%d" % c])
             dma("s", T.yx[:, 256 * c:256 * c + 256], T.yxo[:, 256 * c:256 * c + 256], "stx%d" % c, ["yxo%d" % c], [])
 
+        tt(T.pH2[:, 0:128], T.gea[:], T.pH[:, 128:256], A_.mult, ["gea", "pH:nf"], ["pH2:gn"])
         tt(T.keepB[:], T.gea[:], liveB, A_.mult, ["gea", kliveB], ["keepB"])
+        tt(T.nfk[:], T.pH2[:, 0:128], liveB, A_.mult, ["pH2:gn", kliveB], ["nfk"])
         tt(h, A, T.pH[:, 256:384], A_.add, [kA, "pH:E0a", "pH:E0b"], allp("pH:h"))
-        tt(T.nfk[:], T.keepB[:], T.pH[:, 128:256], A_.mult, ["keepB", "pH:nf"], ["nfk"])
         scan(T.cN[:], T.c0b[:], T.nfk[:], A_.mult, A_.add, ["c0b", "nfk"], ["cN"])
-        lin(T.pKA[:, 0:128], "pKA:k", [(T.keepB[:], Id[1.0], ["keepB"])])
-        lin(T.pKB[:, 0:128], "pKB:k", [(Id[8192.0], T.keepB[:], ["keepB", "I8192"]), (Id[4096.0], T.nfk[:], ["nfk", "I4096"])])
+
+        def k_turn():
+            lin(T.pKA[:, 0:128], "pKA:k", [(T.keepB[:], Id[1.0], ["keepB"])])
+
+        if KT_FIRST:
+            k_turn()
         act(T.y0[:], T.yb[:, 0:2048].indirect(offb), AF.Copy, ["yb", "yb2", koffb], ["y0"])
-        act(T.kT[:], T.pKA[:, 0:128], AF.Copy, ["pKA:k"], ["kT"])
-        tt(T.a1[:], T.cN[:].indirect(T.oend[:]), T.ZA[:], A_.add, ["cN", "oend", "ZA"], ["a1"])
-        tt(T.pH2[:, 384:512], T.pKB[:, 0:128], B, A_.add, ["pKB:k", kB], ["pH2:nB"])
-        ts(T.a2[:], T.a1[:], 15, A_.bitwise_and, ["a1"], ["a2"])
         mm(DX[0][:, 0:384], T.y0[:], T.Wn[:], False, True, ["y0", "Wn"], [xname[0]])
+        if not KT_FIRST:
+            k_turn()
+        act(T.kT[:], T.pKA[:, 0:128], AF.Copy, ["pKA:k"], ["kT"])
         mm(DX[1][:, 0:384], T.y0[:], T.Wn[:], False, True, ["y0", "Wn"], [xname[1]])
         lin(T.pKA[:, 256:384], "pKA:k", [tv, (T.kT[:], T.Lin[:], ["kT", "Lin"])])
+        lin(T.pKB[:, 0:128], "pKB:k", [(Id[8192.0], T.keepB[:], ["keepB", "I8192"]), (Id[4096.0], T.nfk[:], ["nfk", "I4096"])])
         lin(T.pS[:, 256:384], "pS:c", [(Id[1.0], T.Zb[:], ["Zb"]), (Id[-1.0], T.y0[:], ["y0", "I-1"])])
-        ts(T.a3[:], T.a2[:], float(MAGIC), A_.mult, ["a2"], ["a3"])
+        tt(T.a1[:], T.cN[:].indirect(T.oend[:]), T.ZA[:], A_.add, ["cN", "oend", "ZA"], ["a1"])
         scan(T.Hb[:, 0:384], T.hc[:], DX[0][:, 0:384], A_.mult, A_.add, ["hc", xname[0]], ["Hb0"])
-        ts(T.a4[:], T.a3[:], EMASK, A_.bitwise_and, ["a3"], ["a4"])
+        ts(T.a2[:], T.a1[:], 15, A_.bitwise_and, ["a1"], ["a2"])
         scan(T.Hb[:, 384:768], T.hc[:], DX[1][:, 0:384], A_.mult, A_.add, ["hc", xname[1]], ["Hb1"])
+        ts(T.a3[:], T.a2[:], float(MAGIC), A_.mult, ["a2"], ["a3"])
         act(T.ZB[:], T.pKA[:, 256:384], AF.Copy, ["pKA:k"], ["ZB"])
         if last:
             act(T.Zf[:], T.pS[:, 256:384], AF.Abs, ["pS:c"], ["Zf"])
             dma("s", T.yz[:], T.Zf[:], "stz", ["Zf"], [])
-            yx_sum(0, T.pKB[:, 0:256], kname[1])
-            yx_out(0, T.pKB[:, 0:256], kname[1])
+            yx_sum(0, T.pS[:, 0:256], "pS:a")
+            yx_out(0, T.pS[:, 0:256], "pS:a")
         else:
             act(T.Zb[:], T.pS[:, 256:384], AF.Abs, ["pS:c"], ["Zb"])
-        tt(T.geF[:], T.Hb[:].indirect(T.ohor[:]), T.thrA[:], A_.is_ge, ["Hb0", "Hb1", "ohor", "thrA"], ["geF"])
+        for j, a, b in parts:
+            tt(T.geF[:, a:b], T.Hb[:].indirect(T.ohor[:, a // 16:b // 16]), T.thrA[:, a:b], A_.is_ge, ["Hb0", "Hb1", "ohor", "thrA"], ["geF_%d" % j])
+        lin(T.pT[:, 384:512], "pT:p", [(Id[12288.0], T.geF[:], allp("geF") + ["I12288"])])
         if not last:
             u1()
-        lin(T.pT[:, 384:512], "pT:p", [(Id[12288.0], T.geF[:], ["geF", "I12288"])])
-        scan(T.cG[:], T.c0b[:], T.geF[:], A_.mult, A_.add, ["c0b", "geF"], ["cG"])
+        ts(T.a4[:], T.a3[:], EMASK, A_.bitwise_and, ["a3"], ["a4"])
+        for j, a, b in parts:
+            scan(T.cG[:, a:b], T.c0b[:, a:b], T.geF[:, a:b], A_.mult, A_.add, ["c0b", "geF_%d" % j], ["cG_%d" % j])
         tt(T.vA[:], T.a4[:], h, A_.add, ["a4"] + allp("pH:h"), ["vA"])
-        tt(T.e1[:], T.cG[:].indirect(T.oend[:]), T.ZB[:], A_.add, ["cG", "oend", "ZB"], ["e1"])
-        ts(T.e2[:], T.e1[:], 15, A_.bitwise_and, ["e1"], ["e2"])
+        for j, a, b in parts:
+            tt(T.e1[:, a:b], T.cG[:, a:b].indirect(oend), T.ZB[:, a:b], A_.add, ["cG_%d" % j, "oend", "ZB"], ["e1_%d" % j])
+        tt(T.pH2[:, 384:512], T.pKB[:, 0:128], B, A_.add, ["pKB:k", kB], ["pH2:nB"])
+        for j, a, b in parts:
+            ts(T.e2[:, a:b], T.e1[:, a:b], 15, A_.bitwise_and, ["e1_%d" % j], ["e2_%d" % j])
         if last:
             for x in [(1, T.pD0[:, 0:256], xname[0]), (2, T.pD1[:, 0:256], xname[1]), (3, T.pKA[:, 0:256], kname[0])]:
                 yx_sum(*x)
                 yx_out(*x)
         else:
-            mm(T.pD0[:, 0:128], T.ones[:, 0:128], T.nl[:], True, True, ["ones", "nl"], [xname[0]])
+            mm(T.pD0[:, 0:128], T.ones[:, 0:128], T.nl[:], True, True, ["ones"] + allp("nl"), [xname[0]])
             act(T.junk[:], T.pD0[:, 0:128], AF.Identity, [xname[0]], ["junk", "K32"], scale=32.0, acc=T.K32[:, 0:1])
             init_keys()
             u2()
             u3()
         tt(T.pH[:, 256:320], T.vA[:, 0:128:2], T.pT[:, 384:512:2], A_.add, ["vA", "pT:p"], ["pH:E0a"])
-        ts(T.e3[:], T.e2[:], float(MAGIC), A_.mult, ["e2"], ["e3"])
+        for j, a, b in parts:
+            ts(T.e3[:, a:b], T.e2[:, a:b], float(MAGIC), A_.mult, ["e2_%d" % j], ["e3_%d" % j])
         tt(T.O0[:, 0:64], T.vA[:, 1:128:2], T.pT[:, 385:512:2], A_.add, ["vA", "pT:p"], ["O0a"])
-        ts(T.e4[:], T.e3[:], EMASK, A_.bitwise_and, ["e3"], ["e4"])
-        tt(T.pH[:, 320:384], T.e4[:, 0:128:2], T.pH2[:, 384:512:2], A_.add, ["e4", "pH2:nB"], ["pH:E0b"])
-        tt(T.O0[:, 64:128], T.e4[:, 1:128:2], T.pH2[:, 385:512:2], A_.add, ["e4", "pH2:nB"], ["O0b"])
+        for j, a, b in parts:
+            ts(T.e4[:, a:b], T.e3[:, a:b], EMASK, A_.bitwise_and, ["e3_%d" % j], ["e4_%d" % j])
+        tt(T.pH[:, 320:384], T.e4[:, 0:128:2], T.pH2[:, 384:512:2], A_.add, allp("e4") + ["pH2:nB"], ["pH:E0b"])
+        tt(T.O0[:, 64:128], T.e4[:, 1:128:2], T.pH2[:, 385:512:2], A_.add, allp("e4") + ["pH2:nB"], ["O0b"])
 
         for s in range(3):
             i, o = s % 2, 1 - s % 2
@@ -559,10 +578,12 @@ def rank_program(g, core, T, topo):
         rk = ["pH:E1a", "pH:E1b", "O1a", "O1b"]
         tt(T.Y[:, 0:128], T.pH[:, 384:512], T.O1[:], A_.min, rk, ["Ya"])
         tt(T.Y[:, 128:256], T.pH[:, 384:512], T.O1[:], A_.max, rk, ["Yb"])
-        tt(T.m1[:], T.Y[:].indirect(T.omA[:]), T.fil[:], A_.max, ["Ya", "Yb", "omA", "fil"], ["m1"])
-        tt(T.m2[:], T.Y[:].indirect(T.omB[:]), T.m1[:], A_.max, ["Ya", "Yb", "omB", "m1"], ["m2"])
+        for j, a, b in parts:
+            tt(T.m1[:, a:b], T.Y[:].indirect(T.omA[:, a // 16:b // 16]), T.fil[:, a:b], A_.max, ["Ya", "Yb", "omA", "fil"], ["m1_%d" % j])
+        for j, a, b in parts:
+            tt(T.m2[:, a:b], T.Y[:].indirect(T.omB[:, a // 16:b // 16]), T.m1[:, a:b], A_.max, ["Ya", "Yb", "omB", "m1_%d" % j], ["m2_%d" % j])
         An, kAn = blk(T.A, t + 1), "A%d" % (t + 1)
-        ts(An, T.m2[:], 4095, A_.bitwise_and, ["m2"], [kAn])
+        ts(An, T.m2[:], 4095, A_.bitwise_and, allp("m2"), [kAn])
         if not last:
             send(t + 1, An, blk(T.B, t + 1), "rn%d" % (t + 1), [kAn])
         else:

@@ -1,16 +1,19 @@
 from concourse.mybir import AluOpType, ActivationFunctionType
 
 RO = 4
-BIG = float(2 ** 26)
-MAGIC = 0x1111 << 11
-EMASK = (1 << 14) | (1 << 17) | (1 << 20) | (1 << 23)
-RND = float(3 << 22)
-SPLIT = 2
-M_ACT = False
-KT_FIRST = True
-SLOT, GAP = 0, 3
-TFIRST, YCUT, REF_FIRST = True, 128, False
+MAGIC = 0x1111 << 12
+EMASK = (1 << 15) | (1 << 18) | (1 << 21) | (1 << 24)
+TOP = float(1 << 24)
 CUT = 58
+SLOTS = (2, 3, 5)
+KQ = 129.5 * 2 ** 17 - 8.0
+TFIRST = True
+HA_ACT = True
+K_EARLY = True
+EARLY = 1
+YX0 = 1
+LEAD = 6
+ORDER = [1, 0, 2, 3, 4, 5]
 
 
 def _sb(n, d):
@@ -18,44 +21,38 @@ def _sb(n, d):
 
 
 F, BF, I32, U16 = "float32", "bfloat16", "int32", "uint16"
+CUBE = [128, 16, 2, 2, 2, 2]
 SCRATCH = {
-    "X": _sb(4096, BF), "xb": _sb(2048, BF), "yb": _sb(2048, BF),
+    "X": _sb(4112, BF), "CQ": _sb(256, BF), "qp": _sb(128, BF), "LN": _sb(256, BF), "BN": _sb(256, BF), "xb": _sb(2048, BF), "yb": _sb(2048, BF),
     "am_i": _sb(128, I32), "am_f": _sb(128, F), "Zb": _sb(128, BF), "Zf": _sb(128, F), "w_i": _sb(4, I32),
     "cols": _sb(16, F), "coli": _sb(8, I32),
-    "ioj": _sb(128, F), "iog": _sb(128, F), "tvec": _sb(128, F), "tvb": _sb(128, BF), "c0": _sb(128, F), "c0b": _sb(128, BF),
-    "ETi": _sb(128, I32),
-    "If": _sb(128, F), "Rf": _sb(128, F), "Is": _sb(128 * 7, BF),
-    "Blk": _sb(128, BF), "Wblk": _sb(128, BF), "mask": _sb(128, F), "mask16": _sb(128, BF), "Lin": _sb(128, BF),
-    "l1": _sb(128, F), "l2": _sb(128, F),
-    "Sel": _sb(8, BF), "nSel": _sb(8, BF), "Sel2": _sb(8, BF), "ones": _sb(400, BF),
-    "wv": _sb(96, F), "wg": _sb(96, F), "wa": _sb(96, F), "wb": _sb(96, F), "Wp": _sb(432, BF), "Wn": _sb(384, BF),
-    "hc": _sb(384, F),
-    "oend": _sb(8, U16), "ohor": _sb(8, U16), "omA": _sb(8, U16), "omB": _sb(8, U16), "orev": _sb(8, U16),
+    "ioj": _sb(128, F), "iog": _sb(128, F), "tvec": _sb(128, F), "c0": _sb(128, F), "ETi": _sb(128, I32),
+    "If": _sb(128, F), "Rf": _sb(128, F), "Is": _sb(128 * 14, BF), "CT": _sb(128 * 4, BF),
+    "Blk": _sb(128, BF), "Wblk": _sb(128, BF), "Wblk2": _sb(128, BF), "mask": _sb(128, F), "mask16": _sb(128, BF),
+    "l1": _sb(128, F), "l2": _sb(128, F), "Lin": _sb(128, BF), "LM": _sb(256, BF), "BM": _sb(256, BF),
+    "Sel": _sb(8, BF), "nSel": _sb(8, BF), "Sel2": _sb(8, BF), "ones": _sb(128, BF), "c33": _sb(128, BF),
+    "wv": _sb(48, F), "wg": _sb(48, F), "wa": _sb(48, F), "wb": _sb(48, F), "Wp": _sb(48, BF),
+    "oend": _sb(8, U16), "orev": _sb(8, U16), "Cf": _sb(128, F), "c1": _sb(128, F),
     "K32": _sb(4, F), "junk": _sb(128, F),
-    "P1": _sb(128, F), "P2": _sb(128, I32), "P3": _sb(128, I32), "offx": _sb(128, U16), "offy": _sb(128, U16),
-    "q1": _sb(128, F), "q2": _sb(128, F), "q3": _sb(128, BF), "c33": _sb(128, BF), "Wblk2": _sb(128, BF), "Wblk64": _sb(128, BF),
-    "r1": _sb(128, F), "r2": _sb(128, F), "kc": _sb(256, BF), "ab": _sb(128, F),
-    "ZA": _sb(128, F), "cN": _sb(128, BF), "Gu": _sb(128, BF), "offc": _sb(8, U16),
-    "f2": _sb(128, F), "f3": _sb(128, I32), "f4": _sb(128, I32), "fil": _sb(128, F),
-    "d0": _sb(136, F), "d1": _sb(136, F), "h1": _sb(128, F), "eq": _sb(128, F), "cont": _sb(128, F), "nl": _sb(128, BF),
+    "P1": _sb(128, F), "offx": _sb(128, U16), "offy": _sb(128, U16),
+    "q1": _sb(128, BF), "q2": _sb(128, BF), "r1": _sb(128, BF), "r2": _sb(128, BF),
+    "Gu": _sb(128, BF), "offc": _sb(8, U16), "f2": _sb(128, I32), "f4": _sb(128, I32),
+    "D": _sb(256, F), "I0": _sb(260, F), "I1": _sb(260, F), "Qr": _sb(128, F), "Wk": _sb(48, BF), "Kc": _sb(768, BF),
+    "B25": _sb(128, BF), "Ck": _sb(128, BF),
     "ks": _sb(128, BF), "G": _sb(128, BF), "M": _sb(128, BF), "ge": _sb(128, BF), "y0": _sb(128, BF),
-    "Ha": _sb(768, F), "Hb": _sb(768, F),
-    "thrA": _sb(128, F), "thrB": _sb(128, F), "sg": _sb(128, BF), "sg2": _sb(128, BF),
-    "nfk": _sb(128, BF),
-    "lT": _sb(128, BF), "kT": _sb(128, BF), "ZB": _sb(128, F),
-    "gea": _sb(128, BF), "keepB": _sb(128, BF), "vA": _sb(128, F),
-    "e1": _sb(128, I32), "e2": _sb(128, I32), "e3": _sb(128, I32), "e4": _sb(128, I32),
-    "a1": _sb(128, I32), "a2": _sb(128, I32), "a3": _sb(128, I32), "a4": _sb(128, I32),
-    "geF": _sb(128, BF), "cG": _sb(128, BF),
-    "O0": _sb(128, F), "O1": _sb(128, F), "Y": _sb(256, F), "m1": _sb(128, F), "m2": _sb(128, I32),
+    "sX": ("sbuf", [128, 6, 8, 2, 8], BF), "sY": ("sbuf", [128, 6, 8, 2, 8], BF), "Wy": _sb(384, BF), "orep8": _sb(24, U16),
+    "fT": _sb(128, BF), "lsT": _sb(128, BF), "nlf": _sb(128, BF), "kT": _sb(128, BF), "nfT": _sb(128, BF), "gT": _sb(128, BF),
+    "a1": _sb(128, F), "a3": _sb(128, I32), "a4": _sb(128, I32),
+    "e1": _sb(128, F), "e3": _sb(128, I32), "e4": _sb(128, I32),
+    "W0": ("sbuf", CUBE, F), "W1": ("sbuf", CUBE, F), "m2": _sb(128, I32),
     "xs": _sb(128, I32), "xh": _sb(128, I32),
     "yaf": _sb(128, F), "yao": _sb(128, F), "yxo": _sb(1024, F),
     "A": _sb(128 * (RO + 1), I32), "B": _sb(128 * RO, I32),
-    "live": _sb(128 * RO, BF), "liveB": _sb(128 * RO, BF), "offm": _sb(16 * RO, U16), "offb": _sb(16 * RO, U16),
-    "pKA": ("psum", [128, 512], F), "pKB": ("psum", [128, 512], F), "pD0": ("psum", [128, 512], F), "pD1": ("psum", [128, 512], F),
-    "pH": ("psum", [128, 512], F), "pH2": ("psum", [128, 512], F), "pT": ("psum", [128, 512], F), "pS": ("psum", [128, 512], F),
+    "nl": _sb(128 * RO, BF), "nlB": _sb(128 * RO, BF), "offm": _sb(16 * RO, U16), "offb": _sb(16 * RO, U16),
+    "pKA": ("psum", [128, 512], F), "pKB": ("psum", [128, 512], F), "pYA": ("psum", [128, 512], F), "pYB": ("psum", [128, 512], F),
+    "pH": ("psum", [128, 512], F), "pU": ("psum", [128, 512], F), "pT": ("psum", [128, 512], F), "pS": ("psum", [128, 512], F),
 }
-SEMAPHORES = (["cv", "ca", "cp", "cg", "ls", "ldx", "lda", "ldz", "ldw", "sta", "stz", "stx0", "stx1", "stx2", "stx3"]
+SEMAPHORES = (["cv", "ca", "cp", "cg", "ls", "ldx", "lda", "ldz", "ldw", "ldp", "sta", "stz", "stx0", "stx1", "stx2", "stx3"]
               + ["rn%d" % t for t in range(RO)] + ["rl%d" % t for t in range(RO)] + ["ro%d" % t for t in range(RO)])
 
 
@@ -190,211 +187,230 @@ def rank_program(g, core, T, topo):
     dma("s", T.am_i[:], T.am[:], "lda", [], ["am_i"])
     dma("a", T.Zb[:], T.zv[:], "ldz", [], ["Zb"])
     dma("a", T.w_i[:, 0:1], T.wt[:], "ldw", [], ["w_i"])
-    dma("s", T.X[:], T.xt[:], "ldx", [], ["X"])
+    dma("s", T.X[:, 0:4096], T.xt[:], "ldx", [], ["X"])
+    dma("a", T.X[:, 4096:4112], T.xt[:, 0:16], "ldp", [], ["Xpad"])
     for t in range(RO):
         landed(t, "B%d" % t, "rn%d" % t)
-        landed(t, "liveB%d" % t, "rl%d" % t)
+        landed(t, "nlB%d" % t, "rl%d" % t)
         landed(t, "offb%d" % t, "ro%d" % t)
 
     col = lambda j: T.cols[:, j:j + 1]
     iota(T.coli[:, 0:1], [[0, 1]], 0, 1, ["coli0"], fl=False)
     iota(T.ioj[:], [[1, 128]], 0, 0, ["ioj"])
-    iota(T.tvec[:], [[0, 8], [1, 16]], 0, 0, ["tvec"])
     iota(T.iog[:], [[1, 8], [0, 16]], 0, 0, ["iog"])
-    iota(T.wv[:, 0:48], [[-3, 6], [-16, 8]], 0, 1, ["wv0"])
-    iota(T.wv[:, 48:96], [[-16, 8], [3, 6]], -15, 1, ["wv1"])
-    iota(T.wg[:, 0:48], [[0, 6], [1, 8]], 0, 0, ["wg0"])
-    iota(T.wg[:, 48:96], [[1, 8], [0, 6]], 0, 0, ["wg1"])
-    iota(T.ETi[:], [[0, 8], [-1, 16]], 15, 0, ["ETi"], fl=False)
+    iota(T.tvec[:], [[0, 8], [1, 16]], 0, 0, ["tvec"])
+    iota(T.wv[:], [[-3, 6], [-16, 8]], 0, 1, ["wv"])
+    iota(T.wg[:], [[0, 6], [1, 8]], 0, 0, ["wg"])
+    iota(T.ETi[:], [[0, 8], [1, 16]], 0, 0, ["ETi"], fl=False)
 
-    U = T.pD1[:, 384:512]
-    KB_ = [T.pKA, T.pKB]
-    kname = ["pKA:k", "pKB:k"]
-    DX = [T.pD0, T.pD1]
-    xname = ["pD0:k", "pD1:k"]
+    U, Uu, Cst, Um = (blk(T.pU, j) for j in range(4))
+    KB_, kname = [T.pKA, T.pKB], ["pKA:k", "pKB:k"]
+    YB_, yname = [T.pYA, T.pYB], ["pYA:k", "pYB:k"]
+    SC = [1.0, 2.0, -131072.0, 4.0, 8.0, 16.0, 32.0, 64.0, -256.0, 24576.0, 8192.0, -4096.0, -1.0, -2.0 ** 31]
+    Id = {x: blk(T.Is, j) for j, x in enumerate(SC)}
+    In = lambda x: "I%d" % x
+    ones = T.ones[:, 0:128]
+    LB, lname = [T.pKA, T.pKB, T.pYA], ["pKA:k", "pKB:k", "pYA:k"]
+    unit = lambda l: 2.0 ** (60 - 25 * l)
 
     ms(T.ones[:], 1.0, ["ones"])
     ts(T.coli[:, 1:2], T.coli[:, 0:1], 15, A_.bitwise_and, ["coli0"], ["coli1"])
     ts(T.coli[:, 2:3], T.coli[:, 0:1], 4, A_.arith_shift_right, ["coli0"], ["coli2"])
-    ms(T.K32[:], 0.0, ["K32"])
+    ms(T.K32[:, 0:1], -15.5, ["K32"])
+    ms(T.K32[:, 1:2], KQ, ["Kq"])
+    ms(T.CQ[:, 0:128], 62.0 * 1024, ["CQ0"])
+    ms(T.CQ[:, 128:256], 68.0 * 1024, ["CQ1"])
     cp(T.cols[:, 0:3], T.coli[:, 0:3], ["coli0", "coli1", "coli2"], ["cols"])
-    ms(T.d0[:, 0:8], 0.0, ["d0_0"])
+    ms(T.D[:], 0.0, ["D_0", "D_1"])
     ts(col(3), col(1), -2.0, A_.mult, ["cols"], ["col3a"], 15.0, A_.add)
     ts(T.If[:], T.ioj[:], col(0), A_.is_equal, ["ioj", "cols"], ["If"])
     tt(col(4), col(3), col(0), A_.add, ["col3a", "cols"], ["col4"])
-    ms(T.hc[:], 2.0 ** -25, ["hc"])
+    ts(T.Blk[:], T.iog[:], col(2), A_.is_equal, ["iog", "cols"], ["Blk"])
     ts(T.Rf[:], T.ioj[:], col(4), A_.is_equal, ["ioj", "col4"], ["Rf"])
-    ms(T.hc[:, 0:384:6], 0.0, ["hc"])
-    ms(T.d1[:, 0:8], 0.0, ["d1_0"])
+    ms(T.I0[:, 1:260:130], 0.0, ["I0_0", "I0_1"])
+    ms(T.I1[:, 1:260:130], 0.0, ["I1_0", "I1_1"])
     ms(T.c33[:], 33.0, ["c33"])
     ms(T.offm[:], 0, ["offm%d" % t for t in range(RO)])
-    ts(T.mask[:], T.tvec[:], col(1), A_.is_equal, ["tvec", "cols"], ["mask"])
-    ts(T.Sel[:], T.ioj[:, 0:8], col(2), A_.is_equal, ["ioj", "cols"], ["Sel"])
-    ts(T.l1[:], T.tvec[:], col(1), A_.is_lt, ["tvec", "cols"], ["l1"])
-    ts(T.Blk[:], T.iog[:], col(2), A_.is_equal, ["iog", "cols"], ["Blk"])
 
-    SC = [1.0, -1.0, 32.0, -64.0, 4096.0, 8192.0, 12288.0]
-    Id = {x: blk(T.Is, j) for j, x in enumerate(SC)}
-    act(Id[1.0], T.If[:], AF.Copy, ["If"], ["Is"])
+    act(Id[1.0], T.If[:], AF.Copy, ["If"], [In(1)])
+    act(Id[2.0], T.If[:], AF.Identity, ["If"], [In(2)], scale=2.0)
+    act(Id[SC[2]], T.If[:], AF.Identity, ["If"], [In(SC[2])], scale=SC[2])
     act(col(6), col(0), AF.Identity, ["cols"], ["col6"], scale=16.0)
-    act(col(7), col(1), AF.Identity, ["cols"], ["col7"], scale=48.0, bias=5.0)
-    act(col(8), col(1), AF.Identity, ["cols"], ["col8"], scale=-16.0, bias=240.0)
     act(col(9), col(1), AF.Identity, ["cols"], ["col9"], scale=-1.0, bias=15.0)
-    act(T.l2[:], T.If[:], AF.Identity, ["If", "cols"], ["l2"], scale=col(1))
-    for x in SC[1:]:
-        act(Id[x], T.If[:], AF.Identity, ["If"], ["I%d" % x], scale=x)
 
     cp(T.am_f[:], T.am_i[:], ["am_i"], ["am_f"])
     cp(col(5), T.w_i[:, 0:1], ["w_i"], ["col5"])
     mm(T.pT[:, 0:128], T.am_f[:], T.Rf[:], True, True, ["am_f", "Rf"], ["pT:a"])
     act(T.Wblk[:], T.Blk[:], AF.Identity, ["Blk", "col5"], ["Wblk"], scale=col(5))
-    ts(T.wa[:], T.wv[:], 0.0, A_.is_equal, ["wv0", "wv1"], ["wa"], 65536.0, A_.mult)
-    ts(T.wb[:], T.wv[:], 1.0, A_.is_equal, ["wv0", "wv1"], ["wb"], 256.0, A_.mult)
-    ts(T.wv[:], T.wv[:], 2.0, A_.is_equal, ["wv0", "wv1"], ["wv"])
-    cp(blk(T.A, 0), T.pT[:, 0:128], ["pT:a"], ["A0"])
-    send(0, blk(T.A, 0), blk(T.B, 0), "rn0", ["A0"])
+    ts(T.wa[:], T.wv[:], 0.0, A_.is_equal, ["wv"], ["wa"], 65536.0, A_.mult)
+    ts(T.wb[:], T.wv[:], 1.0, A_.is_equal, ["wv"], ["wb"], 256.0, A_.mult)
+    ts(T.wv[:], T.wv[:], 2.0, A_.is_equal, ["wv"], ["wv"])
+    cp(blk(T.A, 0), T.pT[:, 0:128], ["pT:a"], ["A0_0", "A0_1"])
+    send(0, blk(T.A, 0), blk(T.B, 0), "rn0", ["A0_0", "A0_1"])
 
     def init_keys():
-        for b in range(2):
-            mm(KB_[b][:, 0:400], Id[1.0], T.ones[:], True, False, ["Is", "ones"], [kname[b]], inc=False)
+        for b in range(3):
+            mm(LB[b][:, 1:512:2], Id[1.0], T.Kc[:, 256 * b:256 * b + 256], True, False, [In(1)] + ["Kc%d" % l for l in range(6)], [lname[b]], inc=False)
+
+    zw, qq = (T.Zb[:], T.Wblk[:], ["Zb", "Wblk"]), (Id[1.0], T.q2[:], [In(1), "q2"])
 
     def u1():
-        mm(T.pS[:, 0:128], T.Zb[:], T.Wblk[:], True, True, ["Zb", "Wblk"], ["pS:a"])
-        act(T.q1[:], T.pS[:, 0:128], AF.Identity, ["pS:a"], ["q1"], scale=2.0 ** -10, bias=2.0 ** -11 - 0.5)
-        act(T.q2[:], T.q1[:], AF.Identity, ["q1"], ["q2"], bias=RND)
-        act(T.q3[:], T.q2[:], AF.Identity, ["q2"], ["q3"], scale=-2048.0, bias=2048.0 * RND)
-
-        act(T.r1[:], T.pS[:, 0:128], AF.Identity, ["pS:a"], ["r1"], scale=2.0 ** -5, bias=2.0 ** -6 - 0.5)
-        act(T.r2[:], T.r1[:], AF.Identity, ["r1"], ["r2"], bias=RND)
-        act(T.r1[:], T.r2[:], AF.Identity, ["r2"], ["r1"], scale=-32.0, bias=32.0 * RND)
+        lin(T.pS[:, 256:384], "pS:c", [zw])
+        act(T.q1[:], T.pS[:, 256:384], AF.Identity, ["pS:c"], ["q1"], scale=2.0 ** -10, bias=128.5 + 2.0 ** -11)
+        act(T.q2[:], T.q1[:], AF.Identity, ["q1"], ["q2"], scale=-1024.0, bias=129.0 * 1024.0)
 
     def u2():
-        z2, q = (T.Zb[:], T.Wblk2[:], ["Zb", "Wblk2"]), (Id[1.0], T.q3[:], ["Is", "q3"])
-        lin(U, "pD1:U", [z2, (Id[1.0], T.c33[:], ["Is", "c33"]), q])
+        lin(U, "pU:U", [(T.Zb[:], T.Wblk2[:], ["Zb", "Wblk2"]), (Id[1.0], T.c33[:], [In(1), "c33"]), (Id[2.0], T.q2[:], [In(2), "q2"])])
+        lin(Uu, "pU:V", [zw, qq])
+        act(T.r1[:], Uu, AF.Identity, ["pU:V"], ["r1"], scale=2.0 ** -5, bias=128.5 + 2.0 ** -6)
+        act(T.r2[:], T.r1[:], AF.Identity, ["r1"], ["r2"], scale=-32.0, bias=129.0 * 32.0)
 
     def u3():
-        z2, q = (T.Zb[:], T.Wblk2[:], ["Zb", "Wblk2"]), (Id[1.0], T.q3[:], ["Is", "q3"])
-        lin(T.pD1[:, 0:128], "pD1:V", [z2, q])
-        lin(T.pD1[:, 128:256], "pD1:C", [(T.Zb[:], T.Wblk64[:], ["Zb", "Wblk64"]), (Id[32.0], T.q3[:], ["I32", "q3"]),
-                                         (Id[1.0], T.kc[:, 0:128], ["kc"]), (Id[1.0], T.kc[:, 128:256], ["kc2"])])
-        lin(T.pD1[:, 256:384], "pD1:u", [(T.Zb[:], T.Wblk[:], ["Zb", "Wblk"]), (T.If[:], T.r1[:], ["If", "r1"])])
+        lin(Um, "pU:m", [zw, qq, (Id[1.0], T.r2[:], [In(1), "r2"])])
+        lin(Cst, "pU:C", [zw, qq, (T.If[:], T.Cf[:], ["If", "Cf"])])
 
     act(T.Wblk2[:], T.Wblk[:], AF.Identity, ["Wblk"], ["Wblk2"], scale=2.0)
     u1()
-    init_keys()
-    u2()
-    act(T.Wblk64[:], T.Wblk[:], AF.Identity, ["Wblk"], ["Wblk64"], scale=64.0)
-    act(T.kc[:, 0:128], T.tvec[:], AF.Identity, ["tvec"], ["kc"], scale=-2048.0, bias=15 * 2048.0)
-    act(T.kc[:, 128:256], T.tvec[:], AF.Identity, ["tvec"], ["kc2"], scale=-320.0, bias=15 * 320.0)
     tt(T.wa[:], T.wa[:], T.wb[:], A_.add, ["wa", "wb"], ["wa"])
-    ts(T.wg[:], T.wg[:], col(2), A_.is_equal, ["wg0", "wg1", "cols"], ["wg"])
+    ts(T.wg[:], T.wg[:], col(2), A_.is_equal, ["wg", "cols"], ["wg"])
     tt(T.wa[:], T.wa[:], T.wv[:], A_.add, ["wa", "wv"], ["wa"])
-    tt(T.Wp[:, 0:96], T.wa[:], T.wg[:], A_.mult, ["wa", "wg"], ["Wp"])
-    ts(T.c0[:], T.tvec[:], 1.0, A_.min, ["tvec"], ["c0"])
-    ts(T.a1[:], T.ETi[:], float(MAGIC), A_.mult, ["ETi"], ["a1"])
-    ts(T.oend[:], T.ioj[:, 0:8], 16.0, A_.mult, ["ioj"], ["oend"], 15.0, A_.add)
-    ts(T.a2[:], T.a1[:], EMASK, A_.bitwise_and, ["a1"], ["a2"])
-    tt(T.l1[:], T.l1[:], T.Blk[:], A_.mult, ["l1", "Blk"], ["l1"])
-    ts(T.pH2[:, 256:384], T.a2[:], 4096.0, A_.add, ["a2"], ["pH2:ET"])
+    ts(T.a3[:], T.ETi[:], float(MAGIC), A_.mult, ["ETi"], ["a3"])
+    tt(T.Wp[:], T.wa[:], T.wg[:], A_.mult, ["wa", "wg"], ["Wp"])
+    ts(T.c1[:], T.tvec[:], -37.0, A_.mult, ["tvec"], ["c1"], 37.0 * 15 + 4096.0 - TOP, A_.add)
+    ts(T.a4[:], T.a3[:], EMASK, A_.bitwise_and, ["a3"], ["a4"])
+    ts(T.c0[:], T.tvec[:], 0.5, A_.is_lt, ["tvec"], ["c0"], -2.0 ** 88, A_.mult)
+    tt(T.Cf[:], T.a4[:], T.c1[:], A_.add, ["a4", "c1"], ["Cf"])
+    ts(T.mask[:], T.tvec[:], col(1), A_.is_equal, ["tvec", "cols"], ["mask"])
+    ts(T.Sel[:], T.ioj[:, 0:8], col(2), A_.is_equal, ["ioj", "cols"], ["Sel"])
+    u2()
 
-    def more_constants():
+    def consts_a():
+        for j, l in enumerate(ORDER):
+            ms(blk(T.Kc, j), -TOP * unit(l), ["Kc%d" % l])
+            act(T.Wk[:, 8 * j:8 * j + 8], T.Wp[:, 8 * l:8 * l + 8], AF.Identity, ["Wp"], ["Wk"], scale=unit(l))
         act(T.mask16[:], T.mask[:], AF.Identity, ["mask", "col6"], ["mask16"], scale=col(6))
         act(T.nSel[:], T.Sel[:], AF.Identity, ["Sel"], ["nSel"], scale=-1.0)
         act(T.Sel2[:], T.Sel[:], AF.Identity, ["Sel"], ["Sel2"], scale=2.0)
-        act(T.tvb[:], T.tvec[:], AF.Copy, ["tvec"], ["tvb"])
-        act(T.Wp[:, 96:144], T.Wp[:, 48:96], AF.Copy, ["Wp"], ["Wp1"])
-        act(T.c0b[:], T.c0[:], AF.Copy, ["c0"], ["c0b"])
-        act(T.Wp[:, 144:240], T.Wp[:, 48:144], AF.Copy, ["Wp", "Wp1"], ["Wp2"])
-        act(T.Wp[:, 240:432], T.Wp[:, 48:240], AF.Copy, ["Wp", "Wp1", "Wp2"], ["Wp3"])
 
-    def late_constants():
-        ts(T.ohor[:], T.ioj[:, 0:8], 6.0, A_.mult, ["ioj", "col7"], ["ohor"], col(7), A_.add)
-        ts(T.omA[:], T.ioj[:, 0:8], col(8), A_.add, ["ioj", "col8"], ["omA"])
-        ts(T.omB[:], T.ioj[:, 0:8], col(8), A_.add, ["ioj", "col8"], ["omB"], 8.0, A_.add)
-        ts(T.orev[:], T.ioj[:, 0:8], 16.0, A_.mult, ["ioj", "col9"], ["orev"], col(9), A_.add)
-        act(T.Wn[:], T.Wp[:, 48:432], AF.Identity, ["Wp", "Wp1", "Wp2", "Wp3"], ["Wn"], scale=-1.0)
+    def consts_b():
+        act(T.l2[:], T.If[:], AF.Identity, ["If", "cols"], ["l2"], scale=col(1))
+        act(T.Wy[:], T.Wp[:].indirect(T.orep8[:]), AF.Identity, ["Wp", "orep8"], ["Wy"], scale=-1.0)
+
+    def consts_c():
+        ts(T.oend[:], T.ioj[:, 0:8], 16.0, A_.mult, ["ioj"], ["oend"], 15.0, A_.add)
+        ts(col(7), col(1), 8.0, A_.is_ge, ["cols"], ["col7"])
+        ts(T.l1[:], T.tvec[:], col(1), A_.is_lt, ["tvec", "cols"], ["l1"])
+        ts(T.orep8[:], T.ioj[:, 0:24], 2.0, A_.mult, ["ioj", "col7"], ["orep8"], col(7), A_.add)
+        for x in SC[3:9]:
+            ts(Id[x], Id[1.0], x, A_.mult, [In(1)], [In(x)])
+
+    def consts_d():
+        tt(T.l1[:], T.l1[:], T.Blk[:], A_.mult, ["l1", "Blk"], ["l1"])
+        for x in SC[9:]:
+            ts(Id[x], Id[1.0], x, A_.mult, [In(1)], [In(x)])
         tt(T.Lin[:], T.l1[:], T.l2[:], A_.subtract, ["l1", "l2"], ["Lin"])
+        halves = [(255.0 * 32, 255.0 * 8192), (-17.0 * 32, -17.0 * 8192), (12288.0 / 64, -TOP / 64), (8192.0 / 64, -TOP / 64)]
+        for j, (lo, hi) in enumerate(halves):
+            ms(T.CT[0:64, 128 * j:128 * j + 128], lo, ["CT%da" % j])
+            ms(T.CT[64:128, 128 * j:128 * j + 128], hi, ["CT%db" % j])
+        for j in range(2):
+            ts(blk(T.LM, j), T.Lin[:], -17.0 * 2 ** (11 + 8 * j), A_.mult, ["Lin"], ["LM%d" % j])
+            ts(blk(T.BM, j), T.Blk[:], -17.0 * 2 ** (11 + 8 * j), A_.mult, ["Blk"], ["BM%d" % j])
+            ts(blk(T.LN, j), T.Lin[:], -17.0 * 2 ** (12 + 8 * j), A_.mult, ["Lin"], ["LN%d" % j])
+            ts(blk(T.BN, j), T.Blk[:], -17.0 * 2 ** (12 + 8 * j), A_.mult, ["Blk"], ["BN%d" % j])
+        ts(T.B25[:], T.Blk[:], 2.0 ** 25, A_.mult, ["Blk"], ["B25"])
+        ts(T.Ck[:], T.tvec[:], 24.5, A_.add, ["tvec"], ["Ck"], 2.0 ** 26, A_.mult)
+        ts(T.orev[:], T.ioj[:, 0:8], 16.0, A_.mult, ["ioj", "col9"], ["orev"], col(9), A_.add)
 
-    h = T.pH[:, 0:128]
-    Eb = [256, 384]
-    O = [T.O0, T.O1]
-    dd = [T.d0, T.d1]
-    WT = ["Wp", "Wp1", "Wp2", "Wp3"]
-    W_ = 128 // SPLIT
-    parts = [(j, W_ * j, W_ * j + W_) for j in range(SPLIT)]
-    oend = T.oend[:, 0:W_ // 16]
-    allp = lambda n: [n + "_%d" % j for j in range(SPLIT)]
+    const = lambda j: (ones, blk(T.CT, j), ["ones", "CT%da" % j, "CT%db" % j])
+    both = lambda x, name, m, mn: [(x, blk(m, j), [name, mn + "%d" % j]) for j in range(2)]
+    parts = [(j, 64 * j, 64 * j + 64) for j in range(2)]
+    allp = lambda n: [n + "_0", n + "_1"]
+    H = lambda a, b: T.pH[:, a:b]
+    WW = [T.W0, T.W1]
+    II = [T.I0, T.I1]
+    fil = H(0, 128)
+    Xw, Xt = T.X[:, 0:4112], T.X[:, 0:4096]
+    h = lambda a, b: T.pU[:, 128 + a:128 + b]
 
     for t in range(RO):
         last = t == RO - 1
         A, B = blk(T.A, t), blk(T.B, t)
-        kA, kB = "A%d" % t, "B%d" % t
-        live, liveB = blk(T.live, t), blk(T.liveB, t)
-        klive, kliveB = "live%d" % t, "liveB%d" % t
+        kA, kB = allp("A%d" % t), "B%d" % t
+        nl, nlB = blk(T.nl, t), blk(T.nlB, t)
+        knl, knlB = allp("nl%d" % t), "nlB%d" % t
         offm, offb = T.offm[:, 16 * t:16 * t + 8], T.offb[:, 16 * t:16 * t + 8]
         koffm, koffb = "offm%d" % t, "offb%d" % t
-        Xw = T.X[:, 0:4096]
 
-        tt(T.P1[:], A, U, A_.mult, [kA, "pD1:U"], ["P1"])
-        mm(T.pT[:, 0:128 - CUT], T.P1[:], T.If[:, CUT:128], True, True, ["P1", "If"], ["pT:a"])
-        mm(T.pS[:, 0:CUT], T.P1[:], T.If[:, 0:CUT], True, True, ["P1", "If"], ["pS:a"])
+        for j, a, b in parts:
+            tt(T.P1[:, a:b], T.A[:, 128 * t + a:128 * t + b], T.pU[:, a:b], A_.mult, [kA[j], "pU:U"], ["P1_%d" % j])
+        def turn(ps, key, a, b):
+            lin(ps, key, [(T.P1[:], T.If[:, a:b], allp("P1") + ["If"]), (ones, T.CQ[:, a:b], ["ones", "CQ0"])], final=False)
+
+        def wraps(pieces):
+            for js, a, b in pieces:
+                ts(T.qp[:, a:b], T.P1[:, a:b], T.K32[:, 1:2], A_.add, ["P1_%d" % j for j in js] + ["Kq"], ["qp_%d" % j for j in js],
+                   2.0 ** -17, A_.mult)
+
+        def unwrap(ps, key, a, b):
+            lin(ps, key, [(T.qp[:], T.Is[:, 256 + a:256 + b], allp("qp") + [In(SC[2])]), (ones, T.CQ[:, 128 + a:128 + b], ["ones", "CQ1"])], first=False)
+
+        def offsets(out, okey, ps, key):
+            ts(out, ps, T.K32[:, 0:1], A_.add, [key, "K32"], [okey], 2.0 ** -5, A_.mult)
+
+        tt(T.f2[:], A, Uu, A_.mult, kA + ["pU:V"], ["f2"])
+        turn(T.pT[:, 0:128 - CUT], "pT:a", CUT, 128)
+        turn(T.pS[:, 0:CUT], "pS:a", 0, CUT)
+        wraps([([j], a, b) for j, a, b in parts])
+        unwrap(T.pT[:, 0:128 - CUT], "pT:a", CUT, 128)
+        unwrap(T.pS[:, 0:CUT], "pS:a", 0, CUT)
+        u3()
         if t == 0:
-            u3()
-        else:
-            tt(T.f2[:], A, T.pD1[:, 0:128], A_.mult, [kA, "pD1:V"], ["f2"])
-        ts(T.P2[:, CUT:128], T.pT[:, 0:128 - CUT], T.K32[:, 0:1], A_.add, ["pT:a", "K32"], ["P2b"])
-        ts(T.P3[:, CUT:128], T.P2[:, CUT:128], 5, A_.arith_shift_right, ["P2b"], ["P3b"], 4095, A_.bitwise_and)
-        ts(T.P2[:, 0:CUT], T.pS[:, 0:CUT], T.K32[:, 0:1], A_.add, ["pS:a", "K32"], ["P2a"])
-        cp(T.offx[:, CUT:128], T.P3[:, CUT:128], ["P3b"], ["offx1"])
-        ts(T.P3[:, 0:CUT], T.P2[:, 0:CUT], 5, A_.arith_shift_right, ["P2a"], ["P3a"], 4095, A_.bitwise_and)
-        cp(T.offx[:, 0:CUT], T.P3[:, 0:CUT], ["P3a"], ["offx0"])
+            consts_a()
+        init_keys()
+        ts(T.f4[:], T.f2[:], 5, A_.arith_shift_right, ["f2"], ["f4"], 4095, A_.bitwise_and)
+        offsets(T.offx[:, CUT:128], "offx1", T.pT[:, 0:128 - CUT], "pT:a")
+        offsets(T.offx[:, 0:CUT], "offx0", T.pS[:, 0:CUT], "pS:a")
         if t == 0:
-            more_constants()
-        act(T.xb[:, 16 * CUT:2048], Xw.indirect(T.offx[:, CUT:128]), AF.Copy, ["X", "offx1"], ["xb1"])
-        cp(T.xb[:, 0:16 * CUT], Xw.indirect(T.offx[:, 0:CUT]), ["X", "offx0"], ["xb0"])
-        for j in range(16):
-            mm(T.pKA[:, 8 + j:8 + j + 369:16], T.xb[:, j:2048:16], T.Wp[:, 0:24], False, j == 15, ["xb0", "xb1", "Wp"], ["pKA:k"], inc=j == 15)
+            consts_c()
+        act(T.xb[:, 16 * CUT:2048], Xw.indirect(T.offx[:, CUT:128]), AF.Copy, ["X", "Xpad", "offx1"], ["xb1"])
+        cp(T.xb[:, 0:16 * CUT], Xw.indirect(T.offx[:, 0:CUT]), ["X", "Xpad", "offx0"], ["xb0"])
         if t == 0:
-            tt(T.f2[:], A, T.pD1[:, 0:128], A_.mult, [kA, "pD1:V"], ["f2"])
-        tt(T.Gu[:], T.pD1[:, 256:384], T.mask[:], A_.mult, ["pD1:u", "mask"], ["Gu"])
-        tt(T.f3[:], T.f2[:], T.pD1[:, 128:256], A_.add, ["f2", "pD1:C"], ["f3"])
-        if t == 0:
-            late_constants()
-        ts(T.f4[:], T.f3[:], 6, A_.arith_shift_right, ["f3"], ["f4"], 4095, A_.bitwise_and)
-        tt(T.fil[:], T.f4[:], T.pH2[:, 256:384], A_.add, ["f4", "pH2:ET"], ["fil"])
-        def keys_b():
+            consts_b()
+
+        def keys(b):
             for j in range(16):
-                mm(T.pKB[:, 8 + j:8 + j + 369:16], T.xb[:, j:2048:16], T.Wp[:, 24:48], False, j == 15,
-                   ["xb0", "xb1", "Wp"], ["pKB:k"], inc=j == 15)
+                mm(LB[b][:, 1 + 2 * j:2 + 2 * j + 480:32], T.xb[:, j:2048:16], T.Wk[:, 16 * b:16 * b + 16], False, j == 15,
+                   ["xb0", "xb1", "Wk"], [lname[b]], inc=j == 15)
 
+        def rekey(b):
+            for j in range(8):
+                mm(KB_[b][:, j:j + 377:8], T.xb[:, 8 * b + j:2048:16], T.Wp[:], j == 0, False, ["xb0", "xb1", "Wp"], [kname[b]], inc=False)
+
+        keys(0)
+        keys(1)
         if not TFIRST:
-            keys_b()
+            keys(2)
+        tt(T.Gu[:], Um, T.mask[:], A_.mult, ["pU:m", "mask"], ["Gu"])
+        tt(fil, T.f4[:], Cst, A_.add, ["f4", "pU:C"], ["pH:fil", "pH:m1_0", "pH:m1_1"])
 
         def b1():
-            tt(T.P1[:], B, U, A_.mult, [kB, "pD1:U"], ["P1"])
-            mm(T.pT[:, 0:128], T.P1[:], T.If[:], True, True, ["P1", "If"], ["pT:a"])
-            if TFIRST:
-                keys_b()
-            lin(T.pS[:, 256:264], "pS:c", [(T.mask16[:], T.Sel2[:], ["mask16", "Sel2"]), (T.Gu[:], T.Sel[:], ["Gu", "Sel"])])
-            for j in range(16):
-                mm(DX[j // 8][:, 48 * (j % 8):48 * (j % 8) + 48], T.xb[:, j:2048:16], T.Wp[:, 48:96], j % 8 == 0, False,
-                   ["xb0", "xb1", "Wp"], [xname[j // 8]], inc=False)
+            tt(T.P1[:], B, U, A_.mult, [kB, "pU:U"], allp("P1"))
+            turn(T.pT[:, 0:128], "pT:a", 0, 128)
 
         def b2():
-            ts(T.P2[:], T.pT[:, 0:128], T.K32[:, 0:1], A_.add, ["pT:a", "K32"], ["P2a", "P2b"])
-            mm(T.pT[:, 264:272], T.mask16[:], T.Sel[:], True, False, ["mask16", "Sel"], ["pT:m"], inc=False)
+            wraps([([0, 1], 0, 128)])
+            unwrap(T.pT[:, 0:128], "pT:a", 0, 128)
+            if TFIRST:
+                keys(2)
+            lin(T.pS[:, 128:136], "pS:b", [(T.mask16[:], T.Sel2[:], ["mask16", "Sel2"]), (T.Gu[:], T.Sel[:], ["Gu", "Sel"])])
 
         def b3():
-            ts(T.P3[:], T.P2[:], 5, A_.arith_shift_right, ["P2a", "P2b"], ["P3a", "P3b"], 4095, A_.bitwise_and)
+            offsets(T.offy[:], "offy", T.pT[:, 0:128], "pT:a")
+            mm(T.pT[:, 128:136], T.mask16[:], T.Sel[:], True, False, ["mask16", "Sel"], ["pT:m"], inc=False)
+            act(T.yb[:], Xw.indirect(T.offy[:]), AF.Copy, ["X", "Xpad", "offy"], ["yb"])
 
-        def b4():
-            cp(T.offy[:], T.P3[:], ["P3a", "P3b"], ["offy"])
-            act(T.yb[:, 0:16 * YCUT], Xw.indirect(T.offy[:, 0:YCUT]), AF.Copy, ["X", "offy"], ["yb"])
-
-        def b5():
-            cp(T.offc[:], T.pS[:, 256:264], ["pS:c"], ["offc"])
-
-        slots = {SLOT: b1, SLOT + GAP: b2, SLOT + GAP + 1: b3, SLOT + GAP + 2: b4, 12: b5}
+        slots = dict(zip(SLOTS, [b1, b2, b3]))
 
         def slot(n):
             if n in slots:
@@ -402,97 +418,89 @@ def rank_program(g, core, T, topo):
 
         slot(0)
 
-        for l in range(6):
-            kb, kn = KB_[l // 3], kname[l // 3]
-            c = 8 + 128 * (l % 3)
+        def region(l, a, b, first, step):
+            c = 256 * (ORDER.index(l) % 2) + 2 * a + first
+            return LB[l // 2][:, c:c + 2 * (b - a) - (step - 1):step]
+
+        def dcol(l, j, a, b, shift):
             if l == 0:
-                for j, a, b in parts:
-                    scan(T.h1[:, a:b], kb[:, c - 1 + a:c - 1 + b], T.c0[:, a:b], A_.max, A_.mult, [kn, "c0"], ["h1_%d" % j])
-                slot(1)
-                for j, a, b in parts:
-                    tt(T.eq[:, a:b], kb[:, c + a:c + b], T.h1[:, a:b], A_.is_ge, [kn, "h1_%d" % j], ["eq_%d" % j])
-                for j, a, b in parts:
-                    tt(T.cont[:, a:b], kb[:, c + a:c + b], T.h1[:, a:b], A_.is_le, [kn, "h1_%d" % j], ["cont_%d" % j])
-                slot(2)
-                continue
-            d, kd = dd[l % 2], "d%d" % (l % 2)
-            for j, a, b in parts:
-                tt(d[:, 8 + a:8 + b], kb[:, c + a:c + b], T.eq[:, a:b], A_.mult, [kn, "eq_%d" % j], [kd + "_%d" % j])
-            slot(3 * l)
-            for j, a, b in parts:
-                scan(T.pH[:, a:b], d[:, 7 + a:7 + b], T.cont[:, a:b], A_.max, A_.mult,
-                     [kd + "_%d" % j, kd + "_%d" % max(j - 1, 0), "cont_%d" % j], ["pH:h_%d" % j])
-            slot(3 * l + 1)
-            if l < 5:
-                for j, a, b in parts:
-                    tt(T.eq[:, a:b], d[:, 8 + a:8 + b], T.pH[:, a:b], A_.is_ge, [kd + "_%d" % j, "pH:h_%d" % j], ["eq_%d" % j])
-                for j, a, b in parts:
-                    tt(T.cont[:, a:b], d[:, 8 + a:8 + b], T.pH[:, a:b], A_.is_le, [kd + "_%d" % j, "pH:h_%d" % j], ["cont_%d" % j])
-                slot(3 * l + 2)
-            else:
-                dk = allp(kd) + allp("pH:h")
-                for j, a, b in parts:
-                    tt(T.nl[:, a:b], d[:, 8 + a:8 + b], T.pH[:, a:b], A_.is_lt, [kd + "_%d" % j, "pH:h_%d" % j], ["nl_%d" % j])
-                tt(live, d[:, 8:136], h, A_.is_ge, dk, [klive])
-                for j, a, b in parts:
-                    scan(T.ks[:, a:b], T.nl[:, a:b], T.nl[:, a:b], A_.mult, A_.add, ["nl_%d" % j], ["ks_%d" % j])
-        send(t, live, liveB, "rl%d" % t, [klive])
+                return region(0, a, b, 1 - 2 * shift, 2), lname[0]
+            c = 130 * j + 3 - 2 * shift
+            return II[l % 2][:, c:c + 127:2], "I%d_%d" % (l % 2, j)
 
+        for l in range(6):
+            if l > 0:
+                for j, a, b in parts:
+                    hk = lname[l // 2] + "h%d_%d" % (l, j)
+                    scan(II[l % 2][:, 130 * j + 2:130 * j + 130], T.D[:, 2 * a:2 * b], region(l, a, b, 0, 1), A_.subtract, A_.min,
+                         ["D_%d" % j, hk, lname[l // 2]], ["I%d_%d" % (l % 2, j)])
+                    if l > 1:
+                        d, kd = dcol(l - 1, j, a, b, 0)
+                    else:
+                        d, kd = T.D[:, 2 * a + 1:2 * b:2], "D_%d" % j
+                    tt(T.Qr[:, a:b], region(l, a, b, 0, 2), d, A_.subtract, [hk, kd], ["Q_%d" % j])
+                slot(2 * l)
+            if l in (2, 4):
+                rekey(l // 2 - 1)
+            for j, a, b in parts:
+                q, kq = (T.Qr[:, a:b], "Q_%d" % j) if l else (T.c0[:, a:b], "c0")
+                d, kd = dcol(l, j, a, b, 1)
+                if l < 5:
+                    out, ko = region(l + 1, a, b, 0, 2), lname[(l + 1) // 2] + "h%d_%d" % (l + 1, j)
+                    cp(T.D[:, 2 * a + 1:2 * b:2], dcol(l, j, a, b, 0)[0], [kd], ["D_%d" % j])
+                else:
+                    out, ko = h(a, b), "pU:h_%d" % j
+                scan(out, d, q, A_.max, A_.min, [kd, kq], [ko])
+            slot(2 * l + 1)
         for j, a, b in parts:
-            tt(T.G[:, a:b], T.ks[:, a:b].indirect(oend), T.mask[:, a:b], A_.mult, ["ks_%d" % j, "oend", "mask"], ["G_%d" % j])
-        lin(T.pS[:, 384:512], "pS:d", [(live, Id[1.0], [klive])])
-        mm(T.pT[:, 264:272], T.G[:], T.nSel[:], False, True, allp("G") + ["nSel"], ["pT:m"])
-        ts(offm, T.pT[:, 264:272], 15.0, A_.add, ["pT:m"], [koffm])
+            d, kd = dcol(5, j, a, b, 0)
+            tt(T.nl[:, 128 * t + a:128 * t + b], d, h(a, b), A_.is_lt, [kd, "pU:h_%d" % j], [knl[j]])
+        send(t, nl, nlB, "rl%d" % t, knl)
+
+        scan(T.ks[:], nl, nl, A_.mult, A_.add, knl, ["ks"])
+        cp(T.offc[:], T.pS[:, 128:136], ["pS:b"], ["offc"])
+        tt(T.G[:], T.ks[:].indirect(T.oend[:]), T.mask[:], A_.mult, ["ks", "oend", "mask"], ["G"])
+        mm(T.pT[:, 128:136], T.G[:], T.nSel[:], False, True, ["G", "nSel"], ["pT:m"])
+        for j in range(16):
+            mm(YB_[j // 8][:, j % 8:j % 8 + 377:8], T.yb[:, j:2048:16], T.Wp[:], j % 8 == 0, False,
+               ["yb", "Wp"], [yname[j // 8]], inc=False)
+        if not last:
+            lin(T.pS[:, 256:384], "pS:c", [(ones, nl, ["ones"] + knl)])
+        ts(offm, T.pT[:, 128:136], 15.0, A_.add, ["pT:m"], [koffm])
         send(t, T.offm[:, 16 * t:16 * t + 16], T.offb[:, 16 * t:16 * t + 16], "ro%d" % t, [koffm])
-        act(T.lT[:], T.pS[:, 384:512], AF.Copy, ["pS:d"], ["lT"])
-        if M_ACT:
-            act(T.M[:], T.xb[:, 0:2048].indirect(offm), AF.Copy, ["xb0", "xb1", koffm], ["M"])
-        else:
-            cp(T.M[:], T.xb[:, 0:2048].indirect(offm), ["xb0", "xb1", koffm], ["M"])
-        if YCUT < 128:
-            cp(T.yb[:, 16 * YCUT:2048], Xw.indirect(T.offy[:, YCUT:128]), ["X", "offy"], ["yb2"])
+        if not last:
+            act(T.junk[:], T.pS[:, 256:384], AF.Identity, ["pS:c"], ["junk", "K32"], scale=32.0, bias=-15.5 / 128, acc=T.K32[:, 0:1])
+            act(T.K32[:, 1:2], T.K32[:, 0:1], AF.Identity, ["K32"], ["Kq"], bias=KQ + 16.0)
+        cp(T.M[:], T.xb[:, 0:2048].indirect(offm), ["xb0", "xb1", koffm], ["M"])
         tt(T.ge[:], T.Zb[:], T.M[:], A_.is_ge, ["Zb", "M"], ["ge"])
-        tt(T.xs[:], Xw.indirect(T.offc[:]), T.M[:], A_.add, ["X", "offc", "M"], ["xs"])
+        tt(T.xs[:], Xt.indirect(T.offc[:]), T.M[:], A_.add, ["X", "offc", "M"], ["xs"])
+        if t == 0:
+            consts_d()
 
-        def ykeys(b, first):
-            for j in range(8):
-                mm(KB_[b][:, 48 * j:48 * j + 48], T.yb[:, 8 * b + j:2048:16], T.Wn[:, 0:48], first and j == 0, not first and j == 7,
-                   ["yb", "yb2", "Wn"], [kname[b]], inc=not first and j == 7)
-
-        def yref(b, first):
-            mm(KB_[b][:, 0:384], T.M[:], T.Wp[:, 48:432], first, not first, ["M"] + WT, [kname[b]], inc=not first)
-
-        gb = (T.ge[:], T.Blk[:], ["ge", "Blk"])
-        tv = (Id[1.0], T.tvb[:], ["tvb"])
-        if REF_FIRST:
-            yref(0, True)
-            yref(1, True)
-            ykeys(0, False)
-            lin(T.pS[:, 0:128], "pS:a", [gb])
-            ykeys(1, False)
+        cnt = (T.Blk[:], T.ge[:], ["ge", "Blk"])
+        mm(T.pYA[:, 0:384], T.M[:], T.Wy[:], False, True, ["M", "Wy"], [yname[0]])
+        mm(T.pYB[:, 0:384], T.M[:], T.Wy[:], False, True, ["M", "Wy"], [yname[1]])
+        lin(T.pS[:, 0:128], "pS:a", [cnt])
+        lin(T.pS[:, 128:256], "pS:b", [(nl, Id[-256.0], knl + [In(-256)]), cnt])
+        if HA_ACT:
+            act(T.sY[:, :, :, 0], T.pYA[:, 0:384], AF.Sign, [yname[0]], ["sY0"])
         else:
-            ykeys(0, True)
-            ykeys(1, True)
-            yref(0, False)
-            lin(T.pS[:, 0:128], "pS:a", [gb])
-            yref(1, False)
-        act(T.thrB[:], T.pS[:, 0:128], AF.Relu, ["pS:a"], ["thrB"], bias=-5.0 * BIG, scale=BIG)
-        act(T.sg[:], T.pS[:, 0:128], AF.Sign, ["pS:a"], ["sg"], bias=5.5, scale=-1.0)
-        lin(T.pS[:, 256:384], "pS:c", [gb, (Id[-64.0], live, [klive, "I-64"])])
-        lin(T.pT[:, 0:128], "pT:a", [tv, (T.lT[:], T.Lin[:], ["lT", "Lin"])])
-        act(T.pH[:, 128:256], T.sg[:], AF.Identity, ["sg"], ["pH:nf"], bias=0.5, scale=0.5)
-        act(T.sg2[:], T.pS[:, 256:384], AF.Sign, ["pS:c"], ["sg2"], bias=-58.5, scale=-1.0)
-        act(T.ab[:], T.pS[:, 256:384], AF.Abs, ["pS:c"], ["ab"], bias=53.0)
-        act(T.pH[:, 256:384], T.sg2[:], AF.Identity, ["sg2"], ["pH:E0a", "pH:E0b"], bias=4096.0, scale=4096.0)
-        act(T.ZA[:], T.pT[:, 0:128], AF.Copy, ["pT:a"], ["ZA"])
-        act(T.thrA[:], T.ab[:], AF.Relu, ["ab"], ["thrA"], bias=-5.5 * BIG, scale=BIG)
-        scan(T.Ha[:, 0:384], T.hc[:], KB_[0][:, 0:384], A_.mult, A_.add, ["hc", kname[0]], ["Ha0"])
-        scan(T.Ha[:, 384:768], T.hc[:], KB_[1][:, 0:384], A_.mult, A_.add, ["hc", kname[1]], ["Ha1"])
+            ts(T.sY[:, :, :, 0], T.pYA[:, 0:384], 1.0, A_.min, [yname[0]], ["sY0"], -1.0, A_.max)
+        ts(T.sY[:, :, :, 1], T.pYB[:, 0:384], 1.0, A_.min, [yname[1]], ["sY1"], -1.0, A_.max)
+        act(T.fT[:], T.pS[:, 0:128], AF.Sign, ["pS:a"], ["fT"], bias=-5.5)
+        act(T.lsT[:], T.pS[:, 128:256], AF.Sign, ["pS:b"], ["lsT"], bias=128.0)
+        act(T.nlf[:], T.pS[:, 128:256], AF.Sign, ["pS:b"], ["nlf"], bias=5.5, scale=-1.0)
+        levels = lambda s, n: [(s[:, l], Id[2.0 ** (5 - l)], [n + "0", n + "1", In(2 ** (5 - l))]) for l in range(6)]
+        valB = T.pYA[:, 0:128]
+        lin(valB, yname[0], levels(T.sY, "sY") + [(Id[64.0], T.fT[:], [In(64), "fT"]), (nlB, Id[-256.0], [knlB, In(-256)])])
         ts(T.xh[:], T.xs[:], 1, A_.arith_shift_right, ["xs"], ["xh"])
-        tt(T.gea[:], T.Ha[:].indirect(T.ohor[:]), T.thrB[:], A_.is_le, ["Ha0", "Ha1", "ohor", "thrB"], ["gea"])
-        cp(Xw.indirect(T.offc[:]), T.xh[:], ["xh", "offc"], ["X"])
+        hA = T.pYB[:, 256:384]
+        lin(hA, "pYB:h", [const(2), (T.lsT[:], Id[8192.0], ["lsT", In(8192)]), (T.nlf[:], Id[-4096.0], ["nlf", In(-4096)])])
+        cp(Xt.indirect(T.offc[:]), T.xh[:], ["xh", "offc"], ["X"])
+        if not last:
+            cp(T.X[:, 4096:4112], T.X[:, 0:16], ["X"], ["Xpad"])
 
-        def yx_sum(c, ps, key):
+        def yx_part(c, ps, key):
             for q in range(4):
                 mm(ps, Id[1.0], T.X[:, 1024 * q + 256 * c:1024 * q + 256 * c + 256], q == 0, q == 3, ["X"], [key], inc=q == 3)
 
@@ -500,94 +508,103 @@ def rank_program(g, core, T, topo):
             act(T.yxo[:, 256 * c:256 * c + 256], ps, AF.Copy, [key], ["yxo%d" % c])
             dma("s", T.yx[:, 256 * c:256 * c + 256], T.yxo[:, 256 * c:256 * c + 256], "stx%d" % c, ["yxo%d" % c], [])
 
-        tt(T.pH2[:, 0:128], T.gea[:], T.pH[:, 128:256], A_.mult, ["gea", "pH:nf"], ["pH2:gn"])
-        tt(T.keepB[:], T.gea[:], liveB, A_.mult, ["gea", kliveB], ["keepB"])
-        tt(T.nfk[:], T.pH2[:, 0:128], liveB, A_.mult, ["pH2:gn", kliveB], ["nfk"])
-        tt(h, A, T.pH[:, 256:384], A_.add, [kA, "pH:E0a", "pH:E0b"], allp("pH:h"))
-        scan(T.cN[:], T.c0b[:], T.nfk[:], A_.mult, A_.add, ["c0b", "nfk"], ["cN"])
+        def k_flags():
+            ts(T.kT[:], valB, -64.5, A_.is_ge, [yname[0]], ["kT"], 0.5, A_.subtract)
+            ts(T.nfT[:], valB, 0.0, A_.is_lt, [yname[0]], ["nfT"], 0.5, A_.subtract)
 
-        def k_turn():
-            lin(T.pKA[:, 0:128], "pKA:k", [(T.keepB[:], Id[1.0], ["keepB"])])
+        xA, nB, xB, valA = T.pYB[:, 0:128], T.pH[:, 128:256], T.pT[:, 384:512], T.pS[:, 384:512]
 
-        if KT_FIRST:
-            k_turn()
-        act(T.y0[:], T.yb[:, 0:2048].indirect(offb), AF.Copy, ["yb", "yb2", koffb], ["y0"])
-        mm(DX[0][:, 0:384], T.y0[:], T.Wn[:], False, True, ["y0", "Wn"], [xname[0]])
-        if not KT_FIRST:
-            k_turn()
-        act(T.kT[:], T.pKA[:, 0:128], AF.Copy, ["pKA:k"], ["kT"])
-        mm(DX[1][:, 0:384], T.y0[:], T.Wn[:], False, True, ["y0", "Wn"], [xname[1]])
-        lin(T.pKA[:, 256:384], "pKA:k", [tv, (T.kT[:], T.Lin[:], ["kT", "Lin"])])
-        lin(T.pKB[:, 0:128], "pKB:k", [(Id[8192.0], T.keepB[:], ["keepB", "I8192"]), (Id[4096.0], T.nfk[:], ["nfk", "I4096"])])
-        lin(T.pS[:, 256:384], "pS:c", [(Id[1.0], T.Zb[:], ["Zb"]), (Id[-1.0], T.y0[:], ["y0", "I-1"])])
-        tt(T.a1[:], T.cN[:].indirect(T.oend[:]), T.ZA[:], A_.add, ["cN", "oend", "ZA"], ["a1"])
-        scan(T.Hb[:, 0:384], T.hc[:], DX[0][:, 0:384], A_.mult, A_.add, ["hc", xname[0]], ["Hb0"])
-        ts(T.a2[:], T.a1[:], 15, A_.bitwise_and, ["a1"], ["a2"])
-        scan(T.Hb[:, 384:768], T.hc[:], DX[1][:, 0:384], A_.mult, A_.add, ["hc", xname[1]], ["Hb1"])
-        ts(T.a3[:], T.a2[:], float(MAGIC), A_.mult, ["a2"], ["a3"])
-        act(T.ZB[:], T.pKA[:, 256:384], AF.Copy, ["pKA:k"], ["ZB"])
+        def a_sum():
+            lin(xA, yname[1], both(T.kT[:], "kT", T.BN, "BN") + both(T.nfT[:], "nfT", T.BN, "BN"), first=False)
+
+        def cut(i, L, j, s, v):
+            ix = [slice(None), slice(8 * L + 4 * j, 8 * L + 4 * j + 4)] + [slice(None)] * 4
+            ix[5 - s] = v
+            return WW[i][tuple(ix)]
+
+        wkeys = lambda L, i, j: ["W%d%d%d_0" % (L, i, j), "W%d%d%d_1" % (L, i, j)]
+
+        def steps(L, n, ps, c, kx, names, cn, kn, e1, e3, e4):
+            def stage(s):
+                def fn(j, a, b):
+                    for v, alu in enumerate([A_.min, A_.max]):
+                        tt(cut(1 - s % 2, L, j, s, v), cut(s % 2, L, j, s, 0), cut(s % 2, L, j, s, 1), alu,
+                           wkeys(L, s % 2, j), [wkeys(L, 1 - s % 2, j)[v]])
+                return fn
+            return [lambda j, a, b: ts(e1[:, a:b], ps[:, c + a:c + b], 0.0, A_.is_lt, [kx], [n + "1_%d" % j], 16.0 * MAGIC, A_.mult),
+                    lambda j, a, b: tt(e3[:, a:b], ps[:, c + a:c + b], e1[:, a:b], A_.add, [kx, n + "1_%d" % j], [n + "3_%d" % j]),
+                    lambda j, a, b: ts(e4[:, a:b], e3[:, a:b], EMASK, A_.bitwise_and, [n + "3_%d" % j], [n + "4_%d" % j]),
+                    lambda j, a, b: tt(T.W0[:, 8 * L + 4 * j:8 * L + 4 * j + 4], e4[:, a:b], names[:, cn + a:cn + b], A_.add,
+                                       [n + "4_%d" % j, kn], wkeys(L, 0, j))] + [stage(s) for s in range(4)]
+
+        a_steps = steps(0, "a", T.pYB, 0, yname[1], T.pYB, 256, "pYB:h", T.a1, T.a3, T.a4) + [
+            lambda j, a, b: tt(T.a1[:, a:b], T.W0[:, 4 * j:4 * j + 4], T.pYA[:, 128 + a:128 + b], A_.min,
+                               wkeys(0, 0, j) + ["pYA:l"], ["a1_%d" % j]),
+            lambda j, a, b: tt(H(a, b), T.a1[:, a:b], H(a, b), A_.max, ["a1_%d" % j, "pH:fil"], ["pH:m1_%d" % j])]
+        b_steps = steps(1, "e", T.pT, 384, "pT:x", T.pH, 128, "pH:n", T.e1, T.e3, T.e4)
+
+        def run(todo):
+            for fn in todo:
+                for x in parts:
+                    fn(*x)
+
+        yx_early = [(0, T.pU[:, 0:256], "pU:U"), (1, T.pU[:, 256:512], "pU:C")][:YX0] if last else []
+        lin(xA, yname[1], [const(0)] + both(T.lsT[:], "lsT", T.LM, "LM"), final=False)
+        tt(hA, A, hA, A_.add, kA + ["pYB:h"], ["pYB:h"])
+        for x in yx_early:
+            yx_part(*x)
+        k_flags()
+        if K_EARLY:
+            a_sum()
+
+        act(T.y0[:], T.yb[:, 0:2048].indirect(offb), AF.Copy, ["yb", koffb], ["y0"])
+        mm(T.pKA[:, 0:384], T.y0[:], T.Wy[:], False, True, ["y0", "Wy"], [kname[0]])
+        mm(T.pKB[:, 0:384], T.y0[:], T.Wy[:], False, True, ["y0", "Wy"], [kname[1]])
+        if not K_EARLY:
+            a_sum()
+        run(a_steps[:EARLY])
+        lin(T.pYA[:, 256:384], "pYA:z", [(Id[1.0], T.Zb[:], ["Zb"]), (Id[-1.0], T.y0[:], ["y0", In(-1)])])
+        lin(xB, "pT:x", [const(1)] + both(T.kT[:], "kT", T.LN, "LN"), final=False)
+        lin(nB, "pH:n", [const(3), (T.kT[:], Id[24576.0], ["kT", In(24576)]), (T.nfT[:], Id[8192.0], ["nfT", In(8192)])])
+        act(T.sX[:, :, :, 0], T.pKA[:, 0:384], AF.Sign, [kname[0]], ["sX0"])
+        ts(T.sX[:, :, :, 1], T.pKB[:, 0:384], 1.0, A_.min, [kname[1]], ["sX1"], -1.0, A_.max)
+        lin(valA, "pS:d", [(Id[-256.0], T.nlf[:], [In(-256), "nlf"])] + levels(T.sX, "sX"))
         if last:
-            act(T.Zf[:], T.pS[:, 256:384], AF.Abs, ["pS:c"], ["Zf"])
+            act(T.Zf[:], T.pYA[:, 256:384], AF.Abs, ["pYA:z"], ["Zf"])
             dma("s", T.yz[:], T.Zf[:], "stz", ["Zf"], [])
-            yx_sum(0, T.pS[:, 0:256], "pS:a")
-            yx_out(0, T.pS[:, 0:256], "pS:a")
         else:
-            act(T.Zb[:], T.pS[:, 256:384], AF.Abs, ["pS:c"], ["Zb"])
-        for j, a, b in parts:
-            tt(T.geF[:, a:b], T.Hb[:].indirect(T.ohor[:, a // 16:b // 16]), T.thrA[:, a:b], A_.is_ge, ["Hb0", "Hb1", "ohor", "thrA"], ["geF_%d" % j])
-        lin(T.pT[:, 384:512], "pT:p", [(Id[12288.0], T.geF[:], allp("geF") + ["I12288"])])
-        if not last:
-            u1()
-        ts(T.a4[:], T.a3[:], EMASK, A_.bitwise_and, ["a3"], ["a4"])
-        for j, a, b in parts:
-            scan(T.cG[:, a:b], T.c0b[:, a:b], T.geF[:, a:b], A_.mult, A_.add, ["c0b", "geF_%d" % j], ["cG_%d" % j])
-        tt(T.vA[:], T.a4[:], h, A_.add, ["a4"] + allp("pH:h"), ["vA"])
-        for j, a, b in parts:
-            tt(T.e1[:, a:b], T.cG[:, a:b].indirect(oend), T.ZB[:, a:b], A_.add, ["cG_%d" % j, "oend", "ZB"], ["e1_%d" % j])
-        tt(T.pH2[:, 384:512], T.pKB[:, 0:128], B, A_.add, ["pKB:k", kB], ["pH2:nB"])
-        for j, a, b in parts:
-            ts(T.e2[:, a:b], T.e1[:, a:b], 15, A_.bitwise_and, ["e1_%d" % j], ["e2_%d" % j])
+            act(T.Zb[:], T.pYA[:, 256:384], AF.Abs, ["pYA:z"], ["Zb"])
+        tt(nB, B, nB, A_.add, [kB, "pH:n"], ["pH:n"])
+        run(a_steps[EARLY:LEAD])
+        act(T.gT[:], valA, AF.Sign, ["pS:d"], ["gT"], bias=-255.5)
+        lin(xB, "pT:x", both(T.gT[:], "gT", T.BM, "BM"), first=False)
+        lin(T.pYA[:, 128:256], "pYA:l", [(T.gT[:], T.B25[:], ["gT", "B25"]), (T.fT[:], Id[-2.0 ** 31], ["fT", In(-2 ** 31)]),
+                                         (Id[1.0], T.Ck[:], ["Ck"])])
         if last:
-            for x in [(1, T.pD0[:, 0:256], xname[0]), (2, T.pD1[:, 0:256], xname[1]), (3, T.pKA[:, 0:256], kname[0])]:
-                yx_sum(*x)
+            for x in yx_early:
+                yx_out(*x)
+            rest = [(1, T.pU[:, 256:512], "pU:C"), (2, T.pKA[:, 0:256], kname[0]), (3, T.pKB[:, 0:256], kname[1])]
+            if YX0 == 0:
+                rest = [(0, T.pU[:, 0:256], "pU:U")] + rest
+            for x in rest[max(YX0 - 1, 0):]:
+                yx_part(*x)
                 yx_out(*x)
         else:
-            mm(T.pD0[:, 0:128], T.ones[:, 0:128], T.nl[:], True, True, ["ones"] + allp("nl"), [xname[0]])
-            act(T.junk[:], T.pD0[:, 0:128], AF.Identity, [xname[0]], ["junk", "K32"], scale=32.0, acc=T.K32[:, 0:1])
-            init_keys()
+            u1()
             u2()
-            u3()
-        tt(T.pH[:, 256:320], T.vA[:, 0:128:2], T.pT[:, 384:512:2], A_.add, ["vA", "pT:p"], ["pH:E0a"])
-        for j, a, b in parts:
-            ts(T.e3[:, a:b], T.e2[:, a:b], float(MAGIC), A_.mult, ["e2_%d" % j], ["e3_%d" % j])
-        tt(T.O0[:, 0:64], T.vA[:, 1:128:2], T.pT[:, 385:512:2], A_.add, ["vA", "pT:p"], ["O0a"])
-        for j, a, b in parts:
-            ts(T.e4[:, a:b], T.e3[:, a:b], EMASK, A_.bitwise_and, ["e3_%d" % j], ["e4_%d" % j])
-        tt(T.pH[:, 320:384], T.e4[:, 0:128:2], T.pH2[:, 384:512:2], A_.add, allp("e4") + ["pH2:nB"], ["pH:E0b"])
-        tt(T.O0[:, 64:128], T.e4[:, 1:128:2], T.pH2[:, 385:512:2], A_.add, allp("e4") + ["pH2:nB"], ["O0b"])
 
-        for s in range(3):
-            i, o = s % 2, 1 - s % 2
-            rk = ["pH:E%da" % i, "pH:E%db" % i, "O%da" % i, "O%db" % i]
-            e0, e1 = T.pH[:, Eb[i]:Eb[i] + 128:2], T.pH[:, Eb[i] + 1:Eb[i] + 128:2]
-            o0, o1 = O[i][:, 0:128:2], O[i][:, 1:128:2]
-            tt(T.pH[:, Eb[o]:Eb[o] + 64], e0, o0, A_.min, rk, ["pH:E%da" % o])
-            tt(O[o][:, 0:64], e1, o1, A_.min, rk, ["O%da" % o])
-            tt(T.pH[:, Eb[o] + 64:Eb[o] + 128], e0, o0, A_.max, rk, ["pH:E%db" % o])
-            tt(O[o][:, 64:128], e1, o1, A_.max, rk, ["O%db" % o])
-        rk = ["pH:E1a", "pH:E1b", "O1a", "O1b"]
-        tt(T.Y[:, 0:128], T.pH[:, 384:512], T.O1[:], A_.min, rk, ["Ya"])
-        tt(T.Y[:, 128:256], T.pH[:, 384:512], T.O1[:], A_.max, rk, ["Yb"])
+        for n in range(len(b_steps)):
+            run(b_steps[n:n + 1])
+            run(a_steps[LEAD + n:LEAD + n + 1])
+        An, kAn = blk(T.A, t + 1), allp("A%d" % (t + 1))
         for j, a, b in parts:
-            tt(T.m1[:, a:b], T.Y[:].indirect(T.omA[:, a // 16:b // 16]), T.fil[:, a:b], A_.max, ["Ya", "Yb", "omA", "fil"], ["m1_%d" % j])
+            tt(T.m2[:, a:b], T.W0[:, 8 + 4 * j:12 + 4 * j], H(a, b), A_.max, wkeys(1, 0, j) + ["pH:m1_%d" % j], ["m2_%d" % j])
         for j, a, b in parts:
-            tt(T.m2[:, a:b], T.Y[:].indirect(T.omB[:, a // 16:b // 16]), T.m1[:, a:b], A_.max, ["Ya", "Yb", "omB", "m1_%d" % j], ["m2_%d" % j])
-        An, kAn = blk(T.A, t + 1), "A%d" % (t + 1)
-        ts(An, T.m2[:], 4095, A_.bitwise_and, allp("m2"), [kAn])
+            ts(T.A[:, 128 * t + 128 + a:128 * t + 128 + b], T.m2[:, a:b], 4095, A_.bitwise_and, ["m2_%d" % j], [kAn[j]])
         if not last:
-            send(t + 1, An, blk(T.B, t + 1), "rn%d" % (t + 1), [kAn])
+            send(t + 1, An, blk(T.B, t + 1), "rn%d" % (t + 1), kAn)
         else:
-            cp(T.yaf[:], An.indirect(T.orev[:]), [kAn, "orev"], ["yaf"])
+            cp(T.yaf[:], An.indirect(T.orev[:]), kAn + ["orev"], ["yaf"])
             mm(T.pT[:, 0:128], T.yaf[:], T.If[:], True, True, ["yaf", "If"], ["pT:a"])
             cp(T.yao[:], T.pT[:, 0:128], ["pT:a"], ["yao"])
             dma("a", T.ya[:], T.yao[:], "sta", ["yao"], [])

@@ -1,18 +1,22 @@
 from concourse.mybir import AluOpType, ActivationFunctionType
 
 RO = 4
-MAGIC = 0x1111 << 12
-EMASK = (1 << 15) | (1 << 18) | (1 << 21) | (1 << 24)
+SHIFTS = (9, 14, 19, 24)
+MAGIC = sum(1 << s for s in SHIFTS)
+EMASK = (1 << 12) | (1 << 16) | (1 << 20) | (1 << 24)
 TOP = float(1 << 24)
-CUT = 58
+BIG = 2.0 ** 26
+CUT = 64
 SLOTS = (2, 3, 5)
-KQ = 129.5 * 2 ** 17 - 8.0
 TFIRST = True
-HA_ACT = True
+NL_FIRST = True
+NL_POS = 0
 K_EARLY = True
+QY_ACT = False
+YCUT = 112
 EARLY = 1
-YX0 = 1
 LEAD = 6
+YX0 = 1
 ORDER = [1, 0, 2, 3, 4, 5]
 
 
@@ -20,30 +24,29 @@ def _sb(n, d):
     return ("sbuf", [128, n], d)
 
 
-F, BF, I32, U16 = "float32", "bfloat16", "int32", "uint16"
+F, BF, HF, I32, U16 = "float32", "bfloat16", "float16", "int32", "uint16"
 CUBE = [128, 16, 2, 2, 2, 2]
 SCRATCH = {
-    "X": _sb(4112, BF), "CQ": _sb(256, BF), "qp": _sb(128, BF), "LN": _sb(256, BF), "BN": _sb(256, BF), "xb": _sb(2048, BF), "yb": _sb(2048, BF),
+    "X": _sb(4112, BF), "xb": _sb(2048, BF), "yb": _sb(2048, BF),
     "am_i": _sb(128, I32), "am_f": _sb(128, F), "Zb": _sb(128, BF), "Zf": _sb(128, F), "w_i": _sb(4, I32),
     "cols": _sb(16, F), "coli": _sb(8, I32),
     "ioj": _sb(128, F), "iog": _sb(128, F), "tvec": _sb(128, F), "c0": _sb(128, F), "ETi": _sb(128, I32),
-    "If": _sb(128, F), "Rf": _sb(128, F), "Is": _sb(128 * 14, BF), "CT": _sb(128 * 4, BF),
-    "Blk": _sb(128, BF), "Wblk": _sb(128, BF), "Wblk2": _sb(128, BF), "mask": _sb(128, F), "mask16": _sb(128, BF),
-    "l1": _sb(128, F), "l2": _sb(128, F), "Lin": _sb(128, BF), "LM": _sb(256, BF), "BM": _sb(256, BF),
-    "Sel": _sb(8, BF), "nSel": _sb(8, BF), "Sel2": _sb(8, BF), "ones": _sb(128, BF), "c33": _sb(128, BF),
-    "wv": _sb(48, F), "wg": _sb(48, F), "wa": _sb(48, F), "wb": _sb(48, F), "Wp": _sb(48, BF),
+    "If": _sb(128, F), "Rf": _sb(128, F), "Is": _sb(128 * 10, BF), "CQ": _sb(256, BF), "Cs": _sb(128 * 4, BF),
+    "Blk": _sb(128, BF), "Wblk": _sb(128, BF), "Wblk2": _sb(128, BF), "mask": _sb(128, F), "maskS": _sb(128, F), "mask16": _sb(128, BF),
+    "l1": _sb(128, F), "l2": _sb(128, F), "Lin": _sb(128, BF), "LM": _sb(512, BF), "Bs": _sb(128 * 7, BF),
+    "Sel": _sb(8, BF), "nSel": _sb(8, F), "Sel2": _sb(8, BF), "SelH": _sb(8, HF), "ones": _sb(128, BF), "c33": _sb(128, BF),
+    "wv": _sb(48, F), "wg": _sb(48, F), "wa": _sb(48, F), "wb": _sb(48, F), "Wp": _sb(48, BF), "Wk": _sb(48, BF), "Kc": _sb(768, BF),
+    "Wn": _sb(768, BF), "Wy": _sb(384, BF), "orep": _sb(48, U16), "orep8": _sb(24, U16),
     "oend": _sb(8, U16), "orev": _sb(8, U16), "Cf": _sb(128, F), "c1": _sb(128, F),
     "K32": _sb(4, F), "junk": _sb(128, F),
-    "P1": _sb(128, F), "offx": _sb(128, U16), "offy": _sb(128, U16),
+    "P1": _sb(128, F), "qp": _sb(128, BF), "offx": _sb(128, U16), "offy": _sb(128, U16),
     "q1": _sb(128, BF), "q2": _sb(128, BF), "r1": _sb(128, BF), "r2": _sb(128, BF),
     "Gu": _sb(128, BF), "offc": _sb(8, U16), "f2": _sb(128, I32), "f4": _sb(128, I32),
-    "D": _sb(256, F), "I0": _sb(260, F), "I1": _sb(260, F), "Qr": _sb(128, F), "Wk": _sb(48, BF), "Kc": _sb(768, BF),
-    "B25": _sb(128, BF), "Ck": _sb(128, BF),
-    "ks": _sb(128, BF), "G": _sb(128, BF), "M": _sb(128, BF), "ge": _sb(128, BF), "y0": _sb(128, BF),
-    "sX": ("sbuf", [128, 6, 8, 2, 8], BF), "sY": ("sbuf", [128, 6, 8, 2, 8], BF), "Wy": _sb(384, BF), "orep8": _sb(24, U16),
+    "D": _sb(256, F), "I0": _sb(260, F), "I1": _sb(260, F), "Qr": _sb(128, F), "Hs": _sb(128, F),
+    "G1": _sb(128, F), "G2": _sb(128, HF), "M": _sb(128, BF), "ge": _sb(128, BF), "y0": _sb(128, BF),
+    "sX": _sb(768, BF), "sY": ("sbuf", [128, 6, 8, 2, 8], BF),
     "fT": _sb(128, BF), "lsT": _sb(128, BF), "nlf": _sb(128, BF), "kT": _sb(128, BF), "nfT": _sb(128, BF), "gT": _sb(128, BF),
-    "a1": _sb(128, F), "a3": _sb(128, I32), "a4": _sb(128, I32),
-    "e1": _sb(128, F), "e3": _sb(128, I32), "e4": _sb(128, I32),
+    "ab": _sb(128, BF), "a1": _sb(128, F), "a3": _sb(128, I32), "a4": _sb(128, I32), "e3": _sb(128, I32), "e4": _sb(128, I32),
     "W0": ("sbuf", CUBE, F), "W1": ("sbuf", CUBE, F), "m2": _sb(128, I32),
     "xs": _sb(128, I32), "xh": _sb(128, I32),
     "yaf": _sb(128, F), "yao": _sb(128, F), "yxo": _sb(1024, F),
@@ -184,11 +187,11 @@ def rank_program(g, core, T, topo):
     def blk(buf, t, n=128):
         return buf[:, n * t:n * t + n]
 
-    dma("s", T.am_i[:], T.am[:], "lda", [], ["am_i"])
+    dma("s", T.w_i[:, 0:1], T.wt[:], "ldw", [], ["w_i"])
     dma("a", T.Zb[:], T.zv[:], "ldz", [], ["Zb"])
-    dma("a", T.w_i[:, 0:1], T.wt[:], "ldw", [], ["w_i"])
-    dma("s", T.X[:, 0:4096], T.xt[:], "ldx", [], ["X"])
+    dma("s", T.am_i[:], T.am[:], "lda", [], ["am_i"])
     dma("a", T.X[:, 4096:4112], T.xt[:, 0:16], "ldp", [], ["Xpad"])
+    dma("s", T.X[:, 0:4096], T.xt[:], "ldx", [], ["X"])
     for t in range(RO):
         landed(t, "B%d" % t, "rn%d" % t)
         landed(t, "nlB%d" % t, "rl%d" % t)
@@ -198,20 +201,24 @@ def rank_program(g, core, T, topo):
     iota(T.coli[:, 0:1], [[0, 1]], 0, 1, ["coli0"], fl=False)
     iota(T.ioj[:], [[1, 128]], 0, 0, ["ioj"])
     iota(T.iog[:], [[1, 8], [0, 16]], 0, 0, ["iog"])
-    iota(T.tvec[:], [[0, 8], [1, 16]], 0, 0, ["tvec"])
     iota(T.wv[:], [[-3, 6], [-16, 8]], 0, 1, ["wv"])
     iota(T.wg[:], [[0, 6], [1, 8]], 0, 0, ["wg"])
+    iota(T.tvec[:], [[0, 8], [1, 16]], 0, 0, ["tvec"])
     iota(T.ETi[:], [[0, 8], [1, 16]], 0, 0, ["ETi"], fl=False)
 
     U, Uu, Cst, Um = (blk(T.pU, j) for j in range(4))
     KB_, kname = [T.pKA, T.pKB], ["pKA:k", "pKB:k"]
     YB_, yname = [T.pYA, T.pYB], ["pYA:k", "pYB:k"]
-    SC = [1.0, 2.0, -131072.0, 4.0, 8.0, 16.0, 32.0, 64.0, -256.0, 24576.0, 8192.0, -4096.0, -1.0, -2.0 ** 31]
+    LB, lname = [T.pKA, T.pKB, T.pYA], ["pKA:k", "pKB:k", "pYA:k"]
+    SC = [1.0, 2.0, -131072.0, 4.0, 8.0, 16.0, 32.0, 64.0, -256.0, -1.0]
     Id = {x: blk(T.Is, j) for j, x in enumerate(SC)}
     In = lambda x: "I%d" % x
-    ones = T.ones[:, 0:128]
-    LB, lname = [T.pKA, T.pKB, T.pYA], ["pKA:k", "pKB:k", "pYA:k"]
+    BS = [-33.0 * 2 ** 8, -33.0 * 2 ** 18, -33.0 * 2 ** 10, -33.0 * 2 ** 20, BIG / 2, BIG, -BIG]
+    Bk = lambda x, name, j: (x, blk(T.Bs, j), [name, "Bs%d" % j])
+    Cc = lambda j: (Id[1.0], blk(T.Cs, j), [In(1), "Cs%d" % j])
+    ones = T.ones[:]
     unit = lambda l: 2.0 ** (60 - 25 * l)
+    KQ = 129.5 - 2.0 ** -14
 
     ms(T.ones[:], 1.0, ["ones"])
     ts(T.coli[:, 1:2], T.coli[:, 0:1], 15, A_.bitwise_and, ["coli0"], ["coli1"])
@@ -231,107 +238,111 @@ def rank_program(g, core, T, topo):
     ms(T.I1[:, 1:260:130], 0.0, ["I1_0", "I1_1"])
     ms(T.c33[:], 33.0, ["c33"])
     ms(T.offm[:], 0, ["offm%d" % t for t in range(RO)])
+    ts(T.wa[:], T.wv[:], 0.0, A_.is_equal, ["wv"], ["wa"], 65536.0, A_.mult)
+    ts(T.wb[:], T.wv[:], 1.0, A_.is_equal, ["wv"], ["wb"], 256.0, A_.mult)
+    ts(T.wv[:], T.wv[:], 2.0, A_.is_equal, ["wv"], ["wv"])
+    ts(T.wg[:], T.wg[:], col(2), A_.is_equal, ["wg", "cols"], ["wg"])
+    tt(T.wa[:], T.wa[:], T.wb[:], A_.add, ["wa", "wb"], ["wa"])
+    for j, l in enumerate(ORDER):
+        ms(blk(T.Kc, j), -(TOP if l < 5 else 65536.0) * unit(l), ["Kc%d" % l])
 
     act(Id[1.0], T.If[:], AF.Copy, ["If"], [In(1)])
     act(Id[2.0], T.If[:], AF.Identity, ["If"], [In(2)], scale=2.0)
     act(Id[SC[2]], T.If[:], AF.Identity, ["If"], [In(SC[2])], scale=SC[2])
-    act(col(6), col(0), AF.Identity, ["cols"], ["col6"], scale=16.0)
-    act(col(9), col(1), AF.Identity, ["cols"], ["col9"], scale=-1.0, bias=15.0)
 
-    cp(T.am_f[:], T.am_i[:], ["am_i"], ["am_f"])
     cp(col(5), T.w_i[:, 0:1], ["w_i"], ["col5"])
+    cp(T.am_f[:], T.am_i[:], ["am_i"], ["am_f"])
+    ts(T.Wblk[:], T.Blk[:], col(5), A_.mult, ["Blk", "col5"], ["Wblk"])
+    ts(T.Wblk2[:], T.Blk[:], col(5), A_.mult, ["Blk", "col5"], ["Wblk2"], 2.0, A_.mult)
     mm(T.pT[:, 0:128], T.am_f[:], T.Rf[:], True, True, ["am_f", "Rf"], ["pT:a"])
-    act(T.Wblk[:], T.Blk[:], AF.Identity, ["Blk", "col5"], ["Wblk"], scale=col(5))
-    ts(T.wa[:], T.wv[:], 0.0, A_.is_equal, ["wv"], ["wa"], 65536.0, A_.mult)
-    ts(T.wb[:], T.wv[:], 1.0, A_.is_equal, ["wv"], ["wb"], 256.0, A_.mult)
-    ts(T.wv[:], T.wv[:], 2.0, A_.is_equal, ["wv"], ["wv"])
-    cp(blk(T.A, 0), T.pT[:, 0:128], ["pT:a"], ["A0_0", "A0_1"])
-    send(0, blk(T.A, 0), blk(T.B, 0), "rn0", ["A0_0", "A0_1"])
+    tt(T.wa[:], T.wa[:], T.wv[:], A_.add, ["wa", "wv"], ["wa"])
 
     def init_keys():
         for b in range(3):
             mm(LB[b][:, 1:512:2], Id[1.0], T.Kc[:, 256 * b:256 * b + 256], True, False, [In(1)] + ["Kc%d" % l for l in range(6)], [lname[b]], inc=False)
+        mm(T.pYA[:, 257:512:2], Id[1.0], blk(T.Cs, 3), False, False, ["Cs3"], [lname[2]], inc=False)
 
     zw, qq = (T.Zb[:], T.Wblk[:], ["Zb", "Wblk"]), (Id[1.0], T.q2[:], [In(1), "q2"])
 
+    def u0():
+        lin(T.pYA[:, 256:384], "pYA:z", [zw])
+
     def u1():
-        lin(T.pS[:, 256:384], "pS:c", [zw])
-        act(T.q1[:], T.pS[:, 256:384], AF.Identity, ["pS:c"], ["q1"], scale=2.0 ** -10, bias=128.5 + 2.0 ** -11)
+        act(T.q1[:], T.pYA[:, 256:384], AF.Identity, ["pYA:z"], ["q1"], scale=2.0 ** -10, bias=128.5 + 2.0 ** -11)
         act(T.q2[:], T.q1[:], AF.Identity, ["q1"], ["q2"], scale=-1024.0, bias=129.0 * 1024.0)
 
     def u2():
         lin(U, "pU:U", [(T.Zb[:], T.Wblk2[:], ["Zb", "Wblk2"]), (Id[1.0], T.c33[:], [In(1), "c33"]), (Id[2.0], T.q2[:], [In(2), "q2"])])
         lin(Uu, "pU:V", [zw, qq])
+
+    def u3():
         act(T.r1[:], Uu, AF.Identity, ["pU:V"], ["r1"], scale=2.0 ** -5, bias=128.5 + 2.0 ** -6)
         act(T.r2[:], T.r1[:], AF.Identity, ["r1"], ["r2"], scale=-32.0, bias=129.0 * 32.0)
 
-    def u3():
+    def u4():
         lin(Um, "pU:m", [zw, qq, (Id[1.0], T.r2[:], [In(1), "r2"])])
         lin(Cst, "pU:C", [zw, qq, (T.If[:], T.Cf[:], ["If", "Cf"])])
 
-    act(T.Wblk2[:], T.Wblk[:], AF.Identity, ["Wblk"], ["Wblk2"], scale=2.0)
+    u0()
     u1()
-    tt(T.wa[:], T.wa[:], T.wb[:], A_.add, ["wa", "wb"], ["wa"])
-    ts(T.wg[:], T.wg[:], col(2), A_.is_equal, ["wg", "cols"], ["wg"])
-    tt(T.wa[:], T.wa[:], T.wv[:], A_.add, ["wa", "wv"], ["wa"])
-    ts(T.a3[:], T.ETi[:], float(MAGIC), A_.mult, ["ETi"], ["a3"])
+    cp(blk(T.A, 0), T.pT[:, 0:128], ["pT:a"], ["A0_0", "A0_1"])
+    send(0, blk(T.A, 0), blk(T.B, 0), "rn0", ["A0_0", "A0_1"])
     tt(T.Wp[:], T.wa[:], T.wg[:], A_.mult, ["wa", "wg"], ["Wp"])
+    ts(T.a3[:], T.ETi[:], float(MAGIC), A_.mult, ["ETi"], ["a3_0", "a3_1"])
     ts(T.c1[:], T.tvec[:], -37.0, A_.mult, ["tvec"], ["c1"], 37.0 * 15 + 4096.0 - TOP, A_.add)
-    ts(T.a4[:], T.a3[:], EMASK, A_.bitwise_and, ["a3"], ["a4"])
-    ts(T.c0[:], T.tvec[:], 0.5, A_.is_lt, ["tvec"], ["c0"], -2.0 ** 88, A_.mult)
-    tt(T.Cf[:], T.a4[:], T.c1[:], A_.add, ["a4", "c1"], ["Cf"])
-    ts(T.mask[:], T.tvec[:], col(1), A_.is_equal, ["tvec", "cols"], ["mask"])
-    ts(T.Sel[:], T.ioj[:, 0:8], col(2), A_.is_equal, ["ioj", "cols"], ["Sel"])
+    ts(T.a4[:], T.a3[:], EMASK, A_.bitwise_and, ["a3_0", "a3_1"], ["a4_0", "a4_1"])
+    ts(blk(T.Cs, 3), T.tvec[:], 64.0, A_.add, ["tvec"], ["Cs3"], unit(5), A_.mult)
+    ts(T.orep[:], T.ioj[:, 0:48], 1.0, A_.mult, ["ioj"], ["orep"])
+    ms(blk(T.Cs, 2), -7.5 * BIG, ["Cs2"])
+    for j, x in enumerate(BS):
+        ts(blk(T.Bs, j), T.Blk[:], x, A_.mult, ["Blk"], ["Bs%d" % j])
     u2()
 
     def consts_a():
+        tt(T.Cf[:], T.a4[:], T.c1[:], A_.add, ["a4_0", "a4_1", "c1"], ["Cf"])
         for j, l in enumerate(ORDER):
-            ms(blk(T.Kc, j), -TOP * unit(l), ["Kc%d" % l])
-            act(T.Wk[:, 8 * j:8 * j + 8], T.Wp[:, 8 * l:8 * l + 8], AF.Identity, ["Wp"], ["Wk"], scale=unit(l))
-        act(T.mask16[:], T.mask[:], AF.Identity, ["mask", "col6"], ["mask16"], scale=col(6))
-        act(T.nSel[:], T.Sel[:], AF.Identity, ["Sel"], ["nSel"], scale=-1.0)
-        act(T.Sel2[:], T.Sel[:], AF.Identity, ["Sel"], ["Sel2"], scale=2.0)
-
-    def consts_b():
-        act(T.l2[:], T.If[:], AF.Identity, ["If", "cols"], ["l2"], scale=col(1))
-        act(T.Wy[:], T.Wp[:].indirect(T.orep8[:]), AF.Identity, ["Wp", "orep8"], ["Wy"], scale=-1.0)
+            act(T.Wk[:, 8 * j:8 * j + 8], T.Wp[:, 8 * l:8 * l + 8], AF.Identity, ["Wp"], ["Wk%d" % j], scale=unit(l) / (1 if l < 5 else 512))
+        act(T.Wn[:], T.Wp[:].indirect(T.orep[:]), AF.Identity, ["Wp", "orep"], ["Wn"], scale=-1.0)
 
     def consts_c():
-        ts(T.oend[:], T.ioj[:, 0:8], 16.0, A_.mult, ["ioj"], ["oend"], 15.0, A_.add)
+        ts(T.c0[:], T.tvec[:], 0.5, A_.is_lt, ["tvec"], ["c0"], -2.0 ** 88, A_.mult)
+        ts(T.mask[:], T.tvec[:], col(1), A_.is_equal, ["tvec", "cols"], ["mask"])
+        ts(T.Sel[:], T.ioj[:, 0:8], col(2), A_.is_equal, ["ioj", "cols"], ["Sel"])
+        ts(col(6), col(0), 16.0, A_.mult, ["cols"], ["col6"])
         ts(col(7), col(1), 8.0, A_.is_ge, ["cols"], ["col7"])
+        ts(T.oend[:], T.ioj[:, 0:8], 16.0, A_.mult, ["ioj"], ["oend"], 15.0, A_.add)
         ts(T.l1[:], T.tvec[:], col(1), A_.is_lt, ["tvec", "cols"], ["l1"])
+        ts(T.mask16[:], T.mask[:], col(6), A_.mult, ["mask", "col6"], ["mask16"])
+        ts(T.Sel2[:], T.Sel[:], 2.0, A_.mult, ["Sel"], ["Sel2"])
         ts(T.orep8[:], T.ioj[:, 0:24], 2.0, A_.mult, ["ioj", "col7"], ["orep8"], col(7), A_.add)
-        for x in SC[3:9]:
-            ts(Id[x], Id[1.0], x, A_.mult, [In(1)], [In(x)])
+
+    def consts_b():
+        act(T.maskS[:], T.mask[:], AF.Identity, ["mask"], ["maskS"], scale=-1.0 / unit(5))
+        act(T.nSel[:], T.Sel[:], AF.Identity, ["Sel"], ["nSel"], scale=-1.0)
+        act(T.l2[:], T.If[:], AF.Identity, ["If", "cols"], ["l2"], scale=col(1))
+        act(T.Wy[:], T.Wp[:].indirect(T.orep8[:]), AF.Identity, ["Wp", "orep8"], ["Wy"], scale=-1.0)
+        for x in SC[3:]:
+            act(Id[x], Id[1.0], AF.Identity, [In(1)], [In(x)], scale=x)
+
+    def consts_e():
+        cp(T.SelH[:], T.Sel[:], ["Sel"], ["SelH"])
+        tt(T.l1[:], T.l1[:], T.Blk[:], A_.mult, ["l1", "Blk"], ["l1"])
 
     def consts_d():
-        tt(T.l1[:], T.l1[:], T.Blk[:], A_.mult, ["l1", "Blk"], ["l1"])
-        for x in SC[9:]:
-            ts(Id[x], Id[1.0], x, A_.mult, [In(1)], [In(x)])
         tt(T.Lin[:], T.l1[:], T.l2[:], A_.subtract, ["l1", "l2"], ["Lin"])
-        halves = [(255.0 * 32, 255.0 * 8192), (-17.0 * 32, -17.0 * 8192), (12288.0 / 64, -TOP / 64), (8192.0 / 64, -TOP / 64)]
-        for j, (lo, hi) in enumerate(halves):
-            ms(T.CT[0:64, 128 * j:128 * j + 128], lo, ["CT%da" % j])
-            ms(T.CT[64:128, 128 * j:128 * j + 128], hi, ["CT%db" % j])
-        for j in range(2):
-            ts(blk(T.LM, j), T.Lin[:], -17.0 * 2 ** (11 + 8 * j), A_.mult, ["Lin"], ["LM%d" % j])
-            ts(blk(T.BM, j), T.Blk[:], -17.0 * 2 ** (11 + 8 * j), A_.mult, ["Blk"], ["BM%d" % j])
-            ts(blk(T.LN, j), T.Lin[:], -17.0 * 2 ** (12 + 8 * j), A_.mult, ["Lin"], ["LN%d" % j])
-            ts(blk(T.BN, j), T.Blk[:], -17.0 * 2 ** (12 + 8 * j), A_.mult, ["Blk"], ["BN%d" % j])
-        ts(T.B25[:], T.Blk[:], 2.0 ** 25, A_.mult, ["Blk"], ["B25"])
-        ts(T.Ck[:], T.tvec[:], 24.5, A_.add, ["tvec"], ["Ck"], 2.0 ** 26, A_.mult)
-        ts(T.orev[:], T.ioj[:, 0:8], 16.0, A_.mult, ["ioj", "col9"], ["orev"], col(9), A_.add)
+        ts(blk(T.Cs, 0), T.tvec[:], -7.5, A_.add, ["tvec"], ["Cs0"], BIG, A_.mult)
+        ts(blk(T.Cs, 1), T.tvec[:], -3.5, A_.add, ["tvec"], ["Cs1"], BIG, A_.mult)
+        ts(col(9), col(1), -1.0, A_.mult, ["cols"], ["col9"], 15.0, A_.add)
+        for j, s in enumerate(SHIFTS):
+            ts(blk(T.LM, j), T.Lin[:], -2.0 ** s, A_.mult, ["Lin"], ["LM%d" % j])
 
-    const = lambda j: (ones, blk(T.CT, j), ["ones", "CT%da" % j, "CT%db" % j])
-    both = lambda x, name, m, mn: [(x, blk(m, j), [name, mn + "%d" % j]) for j in range(2)]
+    ranks = lambda x, name: [(x, blk(T.LM, j), [name, "LM%d" % j]) for j in range(4)]
     parts = [(j, 64 * j, 64 * j + 64) for j in range(2)]
     allp = lambda n: [n + "_0", n + "_1"]
     H = lambda a, b: T.pH[:, a:b]
     WW = [T.W0, T.W1]
     II = [T.I0, T.I1]
-    fil = H(0, 128)
     Xw, Xt = T.X[:, 0:4112], T.X[:, 0:4096]
-    h = lambda a, b: T.pU[:, 128 + a:128 + b]
 
     for t in range(RO):
         last = t == RO - 1
@@ -342,15 +353,8 @@ def rank_program(g, core, T, topo):
         offm, offb = T.offm[:, 16 * t:16 * t + 8], T.offb[:, 16 * t:16 * t + 8]
         koffm, koffb = "offm%d" % t, "offb%d" % t
 
-        for j, a, b in parts:
-            tt(T.P1[:, a:b], T.A[:, 128 * t + a:128 * t + b], T.pU[:, a:b], A_.mult, [kA[j], "pU:U"], ["P1_%d" % j])
         def turn(ps, key, a, b):
             lin(ps, key, [(T.P1[:], T.If[:, a:b], allp("P1") + ["If"]), (ones, T.CQ[:, a:b], ["ones", "CQ0"])], final=False)
-
-        def wraps(pieces):
-            for js, a, b in pieces:
-                ts(T.qp[:, a:b], T.P1[:, a:b], T.K32[:, 1:2], A_.add, ["P1_%d" % j for j in js] + ["Kq"], ["qp_%d" % j for j in js],
-                   2.0 ** -17, A_.mult)
 
         def unwrap(ps, key, a, b):
             lin(ps, key, [(T.qp[:], T.Is[:, 256 + a:256 + b], allp("qp") + [In(SC[2])]), (ones, T.CQ[:, 128 + a:128 + b], ["ones", "CQ1"])], first=False)
@@ -358,17 +362,21 @@ def rank_program(g, core, T, topo):
         def offsets(out, okey, ps, key):
             ts(out, ps, T.K32[:, 0:1], A_.add, [key, "K32"], [okey], 2.0 ** -5, A_.mult)
 
+        for j, a, b in parts:
+            tt(T.P1[:, a:b], T.A[:, 128 * t + a:128 * t + b], T.pU[:, a:b], A_.mult, [kA[j], "pU:U"], ["P1_%d" % j])
         tt(T.f2[:], A, Uu, A_.mult, kA + ["pU:V"], ["f2"])
         turn(T.pT[:, 0:128 - CUT], "pT:a", CUT, 128)
         turn(T.pS[:, 0:CUT], "pS:a", 0, CUT)
-        wraps([([j], a, b) for j, a, b in parts])
+        for j, a, b in parts:
+            ts(T.qp[:, a:b], T.P1[:, a:b], 2.0 ** -17, A_.mult, ["P1_%d" % j, "Kq"], ["qp_%d" % j], T.K32[:, 1:2], A_.add)
         unwrap(T.pT[:, 0:128 - CUT], "pT:a", CUT, 128)
         unwrap(T.pS[:, 0:CUT], "pS:a", 0, CUT)
-        u3()
         if t == 0:
+            u3()
             consts_a()
-        init_keys()
         ts(T.f4[:], T.f2[:], 5, A_.arith_shift_right, ["f2"], ["f4"], 4095, A_.bitwise_and)
+        init_keys()
+        u4()
         offsets(T.offx[:, CUT:128], "offx1", T.pT[:, 0:128 - CUT], "pT:a")
         offsets(T.offx[:, 0:CUT], "offx0", T.pS[:, 0:CUT], "pS:a")
         if t == 0:
@@ -381,25 +389,31 @@ def rank_program(g, core, T, topo):
         def keys(b):
             for j in range(16):
                 mm(LB[b][:, 1 + 2 * j:2 + 2 * j + 480:32], T.xb[:, j:2048:16], T.Wk[:, 16 * b:16 * b + 16], False, j == 15,
-                   ["xb0", "xb1", "Wk"], [lname[b]], inc=j == 15)
+                   ["xb0", "xb1", "Wk%d" % (2 * b), "Wk%d" % (2 * b + 1)], [lname[b]], inc=j == 15)
 
         def rekey(b):
-            for j in range(8):
-                mm(KB_[b][:, j:j + 377:8], T.xb[:, 8 * b + j:2048:16], T.Wp[:], j == 0, False, ["xb0", "xb1", "Wp"], [kname[b]], inc=False)
+            for j in range(16):
+                mm(KB_[b][:, j:j + 369:16], T.xb[:, j:2048:16], T.Wp[:, 24 * b:24 * b + 24], j == 0, False, ["xb0", "xb1", "Wp"], [kname[b]], inc=False)
 
         keys(0)
         keys(1)
         if not TFIRST:
             keys(2)
         tt(T.Gu[:], Um, T.mask[:], A_.mult, ["pU:m", "mask"], ["Gu"])
-        tt(fil, T.f4[:], Cst, A_.add, ["f4", "pU:C"], ["pH:fil", "pH:m1_0", "pH:m1_1"])
+        tt(H(0, 128), T.f4[:], Cst, A_.add, ["f4", "pU:C"], allp("pH:m1"))
+        ts(H(128, 256), A, 12288.0 - TOP, A_.add, kA, ["pH:A"])
+        if t == 0:
+            consts_e()
 
         def b1():
             tt(T.P1[:], B, U, A_.mult, [kB, "pU:U"], allp("P1"))
             turn(T.pT[:, 0:128], "pT:a", 0, 128)
+            if QY_ACT:
+                act(T.qp[:], T.P1[:], AF.Identity, allp("P1") + ["Kq"], allp("qp"), scale=2.0 ** -17, bias=T.K32[:, 1:2])
 
         def b2():
-            wraps([([0, 1], 0, 128)])
+            if not QY_ACT:
+                ts(T.qp[:], T.P1[:], 2.0 ** -17, A_.mult, allp("P1") + ["Kq"], allp("qp"), T.K32[:, 1:2], A_.add)
             unwrap(T.pT[:, 0:128], "pT:a", 0, 128)
             if TFIRST:
                 keys(2)
@@ -408,7 +422,7 @@ def rank_program(g, core, T, topo):
         def b3():
             offsets(T.offy[:], "offy", T.pT[:, 0:128], "pT:a")
             mm(T.pT[:, 128:136], T.mask16[:], T.Sel[:], True, False, ["mask16", "Sel"], ["pT:m"], inc=False)
-            act(T.yb[:], Xw.indirect(T.offy[:]), AF.Copy, ["X", "Xpad", "offy"], ["yb"])
+            act(T.yb[:, 0:16 * YCUT], Xw.indirect(T.offy[:, 0:YCUT]), AF.Copy, ["X", "Xpad", "offy"], ["yb"])
 
         slots = dict(zip(SLOTS, [b1, b2, b3]))
 
@@ -444,61 +458,73 @@ def rank_program(g, core, T, topo):
                 rekey(l // 2 - 1)
             for j, a, b in parts:
                 q, kq = (T.Qr[:, a:b], "Q_%d" % j) if l else (T.c0[:, a:b], "c0")
+                if l == 5:
+                    d, kd = dcol(l, j, a, b, 0)
+                    scan(T.Hs[:, a:b], q, d, A_.min, A_.max, [kd, kq], ["Hs_%d" % j])
+                    continue
                 d, kd = dcol(l, j, a, b, 1)
-                if l < 5:
-                    out, ko = region(l + 1, a, b, 0, 2), lname[(l + 1) // 2] + "h%d_%d" % (l + 1, j)
-                    cp(T.D[:, 2 * a + 1:2 * b:2], dcol(l, j, a, b, 0)[0], [kd], ["D_%d" % j])
-                else:
-                    out, ko = h(a, b), "pU:h_%d" % j
-                scan(out, d, q, A_.max, A_.min, [kd, kq], [ko])
+                cp(T.D[:, 2 * a + 1:2 * b:2], dcol(l, j, a, b, 0)[0], [kd], ["D_%d" % j])
+                scan(region(l + 1, a, b, 0, 2), d, q, A_.max, A_.min, [kd, kq], [lname[(l + 1) // 2] + "h%d_%d" % (l + 1, j)])
             slot(2 * l + 1)
-        for j, a, b in parts:
-            d, kd = dcol(5, j, a, b, 0)
-            tt(T.nl[:, 128 * t + a:128 * t + b], d, h(a, b), A_.is_lt, [kd, "pU:h_%d" % j], [knl[j]])
-        send(t, nl, nlB, "rl%d" % t, knl)
 
-        scan(T.ks[:], nl, nl, A_.mult, A_.add, knl, ["ks"])
+        def dead(j, a, b):
+            d, kd = dcol(5, j, a, b, 0)
+            tt(T.nl[:, 128 * t + a:128 * t + b], d, T.Hs[:, a:b], A_.is_lt, [kd, "Hs_%d" % j], [knl[j]])
+
+        ends = T.Hs[:].indirect(T.oend[:])
         cp(T.offc[:], T.pS[:, 128:136], ["pS:b"], ["offc"])
-        tt(T.G[:], T.ks[:].indirect(T.oend[:]), T.mask[:], A_.mult, ["ks", "oend", "mask"], ["G"])
-        mm(T.pT[:, 128:136], T.G[:], T.nSel[:], False, True, ["G", "nSel"], ["pT:m"])
+        dead(*parts[0])
+        if NL_POS == 0:
+            dead(*parts[1])
+        tt(T.G1[:], ends, T.maskS[:], A_.mult, allp("Hs") + ["oend", "maskS"], ["G1"])
+        if NL_POS == 1:
+            dead(*parts[1])
+        tt(T.G2[:], ends, T.maskS[:], A_.mult, allp("Hs") + ["oend", "maskS"], ["G2"])
+        lin(T.pT[:, 128:136], "pT:m", [(T.G1[:], T.nSel[:], ["G1", "nSel"]), (T.G2[:], T.SelH[:], ["G2", "SelH"])], first=False)
+        if NL_POS == 2:
+            dead(*parts[1])
+        if YCUT < 128:
+            cp(T.yb[:, 16 * YCUT:2048], Xw.indirect(T.offy[:, YCUT:128]), ["X", "Xpad", "offy"], ["yb2"])
+        if NL_FIRST:
+            send(t, nl, nlB, "rl%d" % t, knl)
+        if not last:
+            lin(Uu, "pU:V", [(ones, nl, ["ones"] + knl)])
         for j in range(16):
             mm(YB_[j // 8][:, j % 8:j % 8 + 377:8], T.yb[:, j:2048:16], T.Wp[:], j % 8 == 0, False,
-               ["yb", "Wp"], [yname[j // 8]], inc=False)
-        if not last:
-            lin(T.pS[:, 256:384], "pS:c", [(ones, nl, ["ones"] + knl)])
-        ts(offm, T.pT[:, 128:136], 15.0, A_.add, ["pT:m"], [koffm])
+               ["yb", "yb2", "Wp"], [yname[j // 8]], inc=False)
+        cp(offm, T.pT[:, 128:136], ["pT:m"], [koffm])
         send(t, T.offm[:, 16 * t:16 * t + 16], T.offb[:, 16 * t:16 * t + 16], "ro%d" % t, [koffm])
+        if not NL_FIRST:
+            send(t, nl, nlB, "rl%d" % t, knl)
         if not last:
-            act(T.junk[:], T.pS[:, 256:384], AF.Identity, ["pS:c"], ["junk", "K32"], scale=32.0, bias=-15.5 / 128, acc=T.K32[:, 0:1])
-            act(T.K32[:, 1:2], T.K32[:, 0:1], AF.Identity, ["K32"], ["Kq"], bias=KQ + 16.0)
+            act(T.junk[:], Uu, AF.Identity, ["pU:V"], ["junk", "K32"], scale=32.0, bias=-15.5 / 128, acc=T.K32[:, 0:1])
+            act(T.K32[:, 1:2], T.K32[:, 0:1], AF.Identity, ["K32"], ["Kq"], scale=2.0 ** -17, bias=KQ + 2.0 ** -13)
         cp(T.M[:], T.xb[:, 0:2048].indirect(offm), ["xb0", "xb1", koffm], ["M"])
+        ts(H(256, 384), B, -TOP, A_.add, [kB], ["pH:B"])
         tt(T.ge[:], T.Zb[:], T.M[:], A_.is_ge, ["Zb", "M"], ["ge"])
         tt(T.xs[:], Xt.indirect(T.offc[:]), T.M[:], A_.add, ["X", "offc", "M"], ["xs"])
-        if t == 0:
-            consts_d()
 
         cnt = (T.Blk[:], T.ge[:], ["ge", "Blk"])
         mm(T.pYA[:, 0:384], T.M[:], T.Wy[:], False, True, ["M", "Wy"], [yname[0]])
         mm(T.pYB[:, 0:384], T.M[:], T.Wy[:], False, True, ["M", "Wy"], [yname[1]])
         lin(T.pS[:, 0:128], "pS:a", [cnt])
         lin(T.pS[:, 128:256], "pS:b", [(nl, Id[-256.0], knl + [In(-256)]), cnt])
-        if HA_ACT:
-            act(T.sY[:, :, :, 0], T.pYA[:, 0:384], AF.Sign, [yname[0]], ["sY0"])
-        else:
-            ts(T.sY[:, :, :, 0], T.pYA[:, 0:384], 1.0, A_.min, [yname[0]], ["sY0"], -1.0, A_.max)
+        act(T.sY[:, :, :, 0], T.pYA[:, 0:384], AF.Sign, [yname[0]], ["sY0"])
         ts(T.sY[:, :, :, 1], T.pYB[:, 0:384], 1.0, A_.min, [yname[1]], ["sY1"], -1.0, A_.max)
         act(T.fT[:], T.pS[:, 0:128], AF.Sign, ["pS:a"], ["fT"], bias=-5.5)
         act(T.lsT[:], T.pS[:, 128:256], AF.Sign, ["pS:b"], ["lsT"], bias=128.0)
         act(T.nlf[:], T.pS[:, 128:256], AF.Sign, ["pS:b"], ["nlf"], bias=5.5, scale=-1.0)
-        levels = lambda s, n: [(s[:, l], Id[2.0 ** (5 - l)], [n + "0", n + "1", In(2 ** (5 - l))]) for l in range(6)]
-        valB = T.pYA[:, 0:128]
-        lin(valB, yname[0], levels(T.sY, "sY") + [(Id[64.0], T.fT[:], [In(64), "fT"]), (nlB, Id[-256.0], [knlB, In(-256)])])
+        weight = lambda l: (Id[2.0 ** (5 - l)], In(2 ** (5 - l)))
+        valB, xA, LA, xB, valA = T.pYA[:, 0:128], T.pYB[:, 0:128], T.pYB[:, 128:256], T.pT[:, 384:512], T.pS[:, 384:512]
+        lin(valB, yname[0], [(T.sY[:, l], weight(l)[0], ["sY0", "sY1", weight(l)[1]]) for l in range(6)]
+            + [(Id[64.0], T.fT[:], [In(64), "fT"])], final=False)
         ts(T.xh[:], T.xs[:], 1, A_.arith_shift_right, ["xs"], ["xh"])
-        hA = T.pYB[:, 256:384]
-        lin(hA, "pYB:h", [const(2), (T.lsT[:], Id[8192.0], ["lsT", In(8192)]), (T.nlf[:], Id[-4096.0], ["nlf", In(-4096)])])
+        if t == 0:
+            consts_d()
         cp(Xt.indirect(T.offc[:]), T.xh[:], ["xh", "offc"], ["X"])
-        if not last:
-            cp(T.X[:, 4096:4112], T.X[:, 0:16], ["X"], ["Xpad"])
+        if last:
+            ts(T.orev[:], T.ioj[:, 0:8], 16.0, A_.mult, ["ioj", "col9"], ["orev"], col(9), A_.add)
+        lin(xA, yname[1], ranks(T.lsT[:], "lsT"), final=False)
 
         def yx_part(c, ps, key):
             for q in range(4):
@@ -508,14 +534,18 @@ def rank_program(g, core, T, topo):
             act(T.yxo[:, 256 * c:256 * c + 256], ps, AF.Copy, [key], ["yxo%d" % c])
             dma("s", T.yx[:, 256 * c:256 * c + 256], T.yxo[:, 256 * c:256 * c + 256], "stx%d" % c, ["yxo%d" % c], [])
 
+        def k_sum():
+            lin(valB, yname[0], [(nlB, Id[-256.0], [knlB, In(-256)])], first=False)
+
         def k_flags():
             ts(T.kT[:], valB, -64.5, A_.is_ge, [yname[0]], ["kT"], 0.5, A_.subtract)
             ts(T.nfT[:], valB, 0.0, A_.is_lt, [yname[0]], ["nfT"], 0.5, A_.subtract)
 
-        xA, nB, xB, valA = T.pYB[:, 0:128], T.pH[:, 128:256], T.pT[:, 384:512], T.pS[:, 384:512]
-
         def a_sum():
-            lin(xA, yname[1], both(T.kT[:], "kT", T.BN, "BN") + both(T.nfT[:], "nfT", T.BN, "BN"), first=False)
+            lin(xA, yname[1], [Bk(x, n, j) for x, n in ((T.kT[:], "kT"), (T.nfT[:], "nfT")) for j in (2, 3)], first=False)
+
+        def b_sum():
+            lin(xB, "pT:x", ranks(T.kT[:], "kT"), final=False)
 
         def cut(i, L, j, s, v):
             ix = [slice(None), slice(8 * L + 4 * j, 8 * L + 4 * j + 4)] + [slice(None)] * 4
@@ -524,24 +554,23 @@ def rank_program(g, core, T, topo):
 
         wkeys = lambda L, i, j: ["W%d%d%d_0" % (L, i, j), "W%d%d%d_1" % (L, i, j)]
 
-        def steps(L, n, ps, c, kx, names, cn, kn, e1, e3, e4):
+        def steps(L, n, ps, c, kx, scale, shift, cn, kn, e3, e4):
             def stage(s):
                 def fn(j, a, b):
                     for v, alu in enumerate([A_.min, A_.max]):
                         tt(cut(1 - s % 2, L, j, s, v), cut(s % 2, L, j, s, 0), cut(s % 2, L, j, s, 1), alu,
                            wkeys(L, s % 2, j), [wkeys(L, 1 - s % 2, j)[v]])
                 return fn
-            return [lambda j, a, b: ts(e1[:, a:b], ps[:, c + a:c + b], 0.0, A_.is_lt, [kx], [n + "1_%d" % j], 16.0 * MAGIC, A_.mult),
-                    lambda j, a, b: tt(e3[:, a:b], ps[:, c + a:c + b], e1[:, a:b], A_.add, [kx, n + "1_%d" % j], [n + "3_%d" % j]),
+            return [lambda j, a, b: ts(e3[:, a:b], ps[:, c + a:c + b], scale, A_.mult, [kx], [n + "3_%d" % j], shift * MAGIC, A_.add),
                     lambda j, a, b: ts(e4[:, a:b], e3[:, a:b], EMASK, A_.bitwise_and, [n + "3_%d" % j], [n + "4_%d" % j]),
-                    lambda j, a, b: tt(T.W0[:, 8 * L + 4 * j:8 * L + 4 * j + 4], e4[:, a:b], names[:, cn + a:cn + b], A_.add,
+                    lambda j, a, b: tt(T.W0[:, 8 * L + 4 * j:8 * L + 4 * j + 4], e4[:, a:b], H(cn + a, cn + b), A_.add,
                                        [n + "4_%d" % j, kn], wkeys(L, 0, j))] + [stage(s) for s in range(4)]
 
-        a_steps = steps(0, "a", T.pYB, 0, yname[1], T.pYB, 256, "pYB:h", T.a1, T.a3, T.a4) + [
-            lambda j, a, b: tt(T.a1[:, a:b], T.W0[:, 4 * j:4 * j + 4], T.pYA[:, 128 + a:128 + b], A_.min,
-                               wkeys(0, 0, j) + ["pYA:l"], ["a1_%d" % j]),
-            lambda j, a, b: tt(H(a, b), T.a1[:, a:b], H(a, b), A_.max, ["a1_%d" % j, "pH:fil"], ["pH:m1_%d" % j])]
-        b_steps = steps(1, "e", T.pT, 384, "pT:x", T.pH, 128, "pH:n", T.e1, T.e3, T.e4)
+        a_steps = steps(0, "a", T.pYB, 0, yname[1], 0.5, 23.5, 128, "pH:A", T.a3, T.a4) + [
+            lambda j, a, b: tt(T.a1[:, a:b], T.W0[:, 4 * j:4 * j + 4], T.pYB[:, 128 + a:128 + b], A_.min, wkeys(0, 0, j) + ["pYB:l"], ["a1_%d" % j]),
+            lambda j, a, b: tt(T.a1[:, a:b], T.a1[:, a:b], H(a, b), A_.max, ["a1_%d" % j, "pH:m1_%d" % j], ["a1_%d" % j]),
+            lambda j, a, b: tt(H(a, b), T.a1[:, a:b], T.pKA[:, a:b], A_.min, ["a1_%d" % j, kname[0]], ["pH:m1_%d" % j])]
+        b_steps = steps(1, "e", T.pT, 384, "pT:x", 1.0, 15.5, 256, "pH:B", T.e3, T.e4)
 
         def run(todo):
             for fn in todo:
@@ -549,53 +578,64 @@ def rank_program(g, core, T, topo):
                     fn(*x)
 
         yx_early = [(0, T.pU[:, 0:256], "pU:U"), (1, T.pU[:, 256:512], "pU:C")][:YX0] if last else []
-        lin(xA, yname[1], [const(0)] + both(T.lsT[:], "lsT", T.LM, "LM"), final=False)
-        tt(hA, A, hA, A_.add, kA + ["pYB:h"], ["pYB:h"])
         for x in yx_early:
             yx_part(*x)
-        k_flags()
         if K_EARLY:
+            k_sum()
+            k_flags()
             a_sum()
 
-        act(T.y0[:], T.yb[:, 0:2048].indirect(offb), AF.Copy, ["yb", koffb], ["y0"])
-        mm(T.pKA[:, 0:384], T.y0[:], T.Wy[:], False, True, ["y0", "Wy"], [kname[0]])
-        mm(T.pKB[:, 0:384], T.y0[:], T.Wy[:], False, True, ["y0", "Wy"], [kname[1]])
-        if not K_EARLY:
-            a_sum()
-        run(a_steps[:EARLY])
+        act(T.y0[:], T.yb[:, 0:2048].indirect(offb), AF.Copy, ["yb", "yb2", koffb], ["y0"])
+        mm(T.pKA[:, 0:384], T.y0[:], T.Wn[:, 0:384], False, True, ["y0", "Wn"], [kname[0]])
+        mm(T.pKB[:, 0:384], T.y0[:], T.Wn[:, 384:768], False, True, ["y0", "Wn"], [kname[1]])
+        if K_EARLY:
+            run(a_steps[:EARLY])
+            b_sum()
+        else:
+            k_sum()
         lin(T.pYA[:, 256:384], "pYA:z", [(Id[1.0], T.Zb[:], ["Zb"]), (Id[-1.0], T.y0[:], ["y0", In(-1)])])
-        lin(xB, "pT:x", [const(1)] + both(T.kT[:], "kT", T.LN, "LN"), final=False)
-        lin(nB, "pH:n", [const(3), (T.kT[:], Id[24576.0], ["kT", In(24576)]), (T.nfT[:], Id[8192.0], ["nfT", In(8192)])])
-        act(T.sX[:, :, :, 0], T.pKA[:, 0:384], AF.Sign, [kname[0]], ["sX0"])
-        ts(T.sX[:, :, :, 1], T.pKB[:, 0:384], 1.0, A_.min, [kname[1]], ["sX1"], -1.0, A_.max)
-        lin(valA, "pS:d", [(Id[-256.0], T.nlf[:], [In(-256), "nlf"])] + levels(T.sX, "sX"))
+        act(T.sX[:, 0:384], T.pKA[:, 0:384], AF.Sign, [kname[0]], ["sX0"])
+        ts(T.sX[:, 384:768], T.pKB[:, 0:384], 1.0, A_.min, [kname[1]], ["sX1"], -1.0, A_.max)
+        if not K_EARLY:
+            k_flags()
+        lin(valA, "pS:d", [(Id[-256.0], T.nlf[:], [In(-256), "nlf"])]
+            + [(blk(T.sX, l), weight(l)[0], ["sX%d" % (l // 3), weight(l)[1]]) for l in range(6)])
         if last:
             act(T.Zf[:], T.pYA[:, 256:384], AF.Abs, ["pYA:z"], ["Zf"])
             dma("s", T.yz[:], T.Zf[:], "stz", ["Zf"], [])
         else:
             act(T.Zb[:], T.pYA[:, 256:384], AF.Abs, ["pYA:z"], ["Zb"])
-        tt(nB, B, nB, A_.add, [kB, "pH:n"], ["pH:n"])
-        run(a_steps[EARLY:LEAD])
+        if not K_EARLY:
+            b_sum()
+            a_sum()
+        if not last:
+            u0()
+        run(a_steps[EARLY if K_EARLY else 0:LEAD])
         act(T.gT[:], valA, AF.Sign, ["pS:d"], ["gT"], bias=-255.5)
-        lin(xB, "pT:x", both(T.gT[:], "gT", T.BM, "BM"), first=False)
-        lin(T.pYA[:, 128:256], "pYA:l", [(T.gT[:], T.B25[:], ["gT", "B25"]), (T.fT[:], Id[-2.0 ** 31], ["fT", In(-2 ** 31)]),
-                                         (Id[1.0], T.Ck[:], ["Ck"])])
+        lin(xB, "pT:x", [Bk(T.gT[:], "gT", 0), Bk(T.gT[:], "gT", 1)], first=False)
+
+        lin(T.pS[:, 0:128], "pS:a", [Cc(1), Bk(T.kT[:], "kT", 4), Bk(T.gT[:], "gT", 4)])
+        lin(LA, "pYB:l", [Cc(0), Bk(T.kT[:], "kT", 5), Bk(T.nfT[:], "nfT", 5), Bk(T.lsT[:], "lsT", 4), Bk(T.nlf[:], "nlf", 4), Bk(T.gT[:], "gT", 4)])
+        act(T.ab[:], T.pS[:, 0:128], AF.Abs, ["pS:a"], ["ab"], scale=2.0)
+        if not last:
+            u1()
+        lin(T.pKA[:, 0:128], kname[0], [Cc(2), Bk(T.kT[:], "kT", 6), (Id[1.0], T.ab[:], ["ab"])])
         if last:
             for x in yx_early:
                 yx_out(*x)
-            rest = [(1, T.pU[:, 256:512], "pU:C"), (2, T.pKA[:, 0:256], kname[0]), (3, T.pKB[:, 0:256], kname[1])]
-            if YX0 == 0:
-                rest = [(0, T.pU[:, 0:256], "pU:U")] + rest
-            for x in rest[max(YX0 - 1, 0):]:
+            rest = [(0, T.pU[:, 0:256], "pU:U"), (1, T.pU[:, 256:512], "pU:C"), (2, T.pKB[:, 0:256], kname[1]), (3, T.pYA[:, 0:256], yname[0])]
+            for x in rest[YX0:]:
                 yx_part(*x)
                 yx_out(*x)
         else:
-            u1()
+            act(T.X[:, 4096:4112], T.X[:, 0:16], AF.Copy, ["X"], ["Xpad"])
             u2()
+            u3()
 
         for n in range(len(b_steps)):
             run(b_steps[n:n + 1])
             run(a_steps[LEAD + n:LEAD + n + 1])
+        run(a_steps[LEAD + len(b_steps):])
         An, kAn = blk(T.A, t + 1), allp("A%d" % (t + 1))
         for j, a, b in parts:
             tt(T.m2[:, a:b], T.W0[:, 8 + 4 * j:12 + 4 * j], H(a, b), A_.max, wkeys(1, 0, j) + ["pH:m1_%d" % j], ["m2_%d" % j])

@@ -8,15 +8,16 @@ TOP = float(1 << 24)
 BIG = 2.0 ** 26
 CUT = 64
 SLOTS = (2, 3, 5)
-TFIRST = True
+SLOTS0 = (6, 3, 4, 7, 9)
+TFIRST = False
 NL_FIRST = True
 NL_POS = 0
-K_EARLY = True
+K_EARLY = 2
 QY_ACT = False
 YCUT = 112
-EARLY = 1
-LEAD = 6
-YX0 = 1
+EARLY = 0
+LEAD = 5
+YX0 = 0
 ORDER = [1, 0, 2, 3, 4, 5]
 
 
@@ -30,10 +31,10 @@ SCRATCH = {
     "X": _sb(4112, BF), "xb": _sb(2048, BF), "yb": _sb(2048, BF),
     "am_i": _sb(128, I32), "am_f": _sb(128, F), "Zb": _sb(128, BF), "Zf": _sb(128, F), "w_i": _sb(4, I32),
     "cols": _sb(16, F), "coli": _sb(8, I32),
-    "ioj": _sb(128, F), "iog": _sb(128, F), "tvec": _sb(128, F), "c0": _sb(128, F), "ETi": _sb(128, I32),
-    "If": _sb(128, F), "Rf": _sb(128, F), "Is": _sb(128 * 10, BF), "CQ": _sb(256, BF), "Cs": _sb(128 * 4, BF),
+    "ioj": _sb(128, F), "iog": _sb(128, F), "tvec": _sb(128, F), "c0": _sb(128, F),
+    "If": _sb(128, F), "Rf": _sb(128, F), "Is": _sb(128 * 11, BF), "CQ": _sb(256, BF), "Cs": _sb(128 * 4, BF),
     "Blk": _sb(128, BF), "Wblk": _sb(128, BF), "Wblk2": _sb(128, BF), "mask": _sb(128, F), "maskS": _sb(128, F), "mask16": _sb(128, BF),
-    "l1": _sb(128, F), "l2": _sb(128, F), "Lin": _sb(128, BF), "LM": _sb(512, BF), "Bs": _sb(128 * 7, BF),
+    "l1": _sb(128, F), "l2": _sb(128, F), "nLin": _sb(128, BF), "Bs": _sb(128 * 5, BF),
     "Sel": _sb(8, BF), "nSel": _sb(8, F), "Sel2": _sb(8, BF), "SelH": _sb(8, HF), "ones": _sb(128, BF), "c33": _sb(128, BF),
     "wv": _sb(48, F), "wg": _sb(48, F), "wa": _sb(48, F), "wb": _sb(48, F), "Wp": _sb(48, BF), "Wk": _sb(48, BF), "Kc": _sb(768, BF),
     "Wn": _sb(768, BF), "Wy": _sb(384, BF), "orep": _sb(48, U16), "orep8": _sb(24, U16),
@@ -49,7 +50,7 @@ SCRATCH = {
     "ab": _sb(128, BF), "a1": _sb(128, F), "a3": _sb(128, I32), "a4": _sb(128, I32), "e3": _sb(128, I32), "e4": _sb(128, I32),
     "W0": ("sbuf", CUBE, F), "W1": ("sbuf", CUBE, F), "m2": _sb(128, I32),
     "xs": _sb(128, I32), "xh": _sb(128, I32),
-    "yaf": _sb(128, F), "yao": _sb(128, F), "yxo": _sb(1024, F),
+    "yaf": _sb(128, HF), "IdH": _sb(128, HF), "yao": _sb(128, F), "yxo": _sb(1024, F),
     "A": _sb(128 * (RO + 1), I32), "B": _sb(128 * RO, I32),
     "nl": _sb(128 * RO, BF), "nlB": _sb(128 * RO, BF), "offm": _sb(16 * RO, U16), "offb": _sb(16 * RO, U16),
     "pKA": ("psum", [128, 512], F), "pKB": ("psum", [128, 512], F), "pYA": ("psum", [128, 512], F), "pYB": ("psum", [128, 512], F),
@@ -204,16 +205,15 @@ def rank_program(g, core, T, topo):
     iota(T.wv[:], [[-3, 6], [-16, 8]], 0, 1, ["wv"])
     iota(T.wg[:], [[0, 6], [1, 8]], 0, 0, ["wg"])
     iota(T.tvec[:], [[0, 8], [1, 16]], 0, 0, ["tvec"])
-    iota(T.ETi[:], [[0, 8], [1, 16]], 0, 0, ["ETi"], fl=False)
 
     U, Uu, Cst, Um = (blk(T.pU, j) for j in range(4))
-    KB_, kname = [T.pKA, T.pKB], ["pKA:k", "pKB:k"]
+    KB_, kname = [T.pKA, T.pKB, T.pU], ["pKA:k", "pKB:k", "pU:U"]
     YB_, yname = [T.pYA, T.pYB], ["pYA:k", "pYB:k"]
     LB, lname = [T.pKA, T.pKB, T.pYA], ["pKA:k", "pKB:k", "pYA:k"]
-    SC = [1.0, 2.0, -131072.0, 4.0, 8.0, 16.0, 32.0, 64.0, -256.0, -1.0]
+    SC = [1.0, -2048.0, -131072.0, 2.0, 4.0, 8.0, 16.0, 32.0, 64.0, -256.0, -1.0]
     Id = {x: blk(T.Is, j) for j, x in enumerate(SC)}
     In = lambda x: "I%d" % x
-    BS = [-33.0 * 2 ** 8, -33.0 * 2 ** 18, -33.0 * 2 ** 10, -33.0 * 2 ** 20, BIG / 2, BIG, -BIG]
+    BS = [-0.5, -2.0, BIG / 2, BIG, -BIG]
     Bk = lambda x, name, j: (x, blk(T.Bs, j), [name, "Bs%d" % j])
     Cc = lambda j: (Id[1.0], blk(T.Cs, j), [In(1), "Cs%d" % j])
     ones = T.ones[:]
@@ -236,26 +236,25 @@ def rank_program(g, core, T, topo):
     ts(T.Rf[:], T.ioj[:], col(4), A_.is_equal, ["ioj", "col4"], ["Rf"])
     ms(T.I0[:, 1:260:130], 0.0, ["I0_0", "I0_1"])
     ms(T.I1[:, 1:260:130], 0.0, ["I1_0", "I1_1"])
-    ms(T.c33[:], 33.0, ["c33"])
+    ms(T.c33[0:64, :], 129.0 * 32, ["c33a"])
+    ms(T.c33[64:128, :], 33.0 / 64, ["c33b"])
     ms(T.offm[:], 0, ["offm%d" % t for t in range(RO)])
     ts(T.wa[:], T.wv[:], 0.0, A_.is_equal, ["wv"], ["wa"], 65536.0, A_.mult)
     ts(T.wb[:], T.wv[:], 1.0, A_.is_equal, ["wv"], ["wb"], 256.0, A_.mult)
     ts(T.wv[:], T.wv[:], 2.0, A_.is_equal, ["wv"], ["wv"])
     ts(T.wg[:], T.wg[:], col(2), A_.is_equal, ["wg", "cols"], ["wg"])
-    tt(T.wa[:], T.wa[:], T.wb[:], A_.add, ["wa", "wb"], ["wa"])
-    for j, l in enumerate(ORDER):
-        ms(blk(T.Kc, j), -(TOP if l < 5 else 65536.0) * unit(l), ["Kc%d" % l])
 
-    act(Id[1.0], T.If[:], AF.Copy, ["If"], [In(1)])
-    act(Id[2.0], T.If[:], AF.Identity, ["If"], [In(2)], scale=2.0)
-    act(Id[SC[2]], T.If[:], AF.Identity, ["If"], [In(SC[2])], scale=SC[2])
+    for x in SC:
+        act(Id[x], T.If[:], AF.Identity, ["If"], [In(x)], scale=x)
 
     cp(col(5), T.w_i[:, 0:1], ["w_i"], ["col5"])
     cp(T.am_f[:], T.am_i[:], ["am_i"], ["am_f"])
+    tt(T.wa[:], T.wa[:], T.wb[:], A_.add, ["wa", "wb"], ["wa"])
     ts(T.Wblk[:], T.Blk[:], col(5), A_.mult, ["Blk", "col5"], ["Wblk"])
     ts(T.Wblk2[:], T.Blk[:], col(5), A_.mult, ["Blk", "col5"], ["Wblk2"], 2.0, A_.mult)
-    mm(T.pT[:, 0:128], T.am_f[:], T.Rf[:], True, True, ["am_f", "Rf"], ["pT:a"])
     tt(T.wa[:], T.wa[:], T.wv[:], A_.add, ["wa", "wv"], ["wa"])
+    for j, l in enumerate(ORDER):
+        ms(blk(T.Kc, j), -(TOP if l < 5 else 65536.0) * unit(l), ["Kc%d" % l])
 
     def init_keys():
         for b in range(3):
@@ -272,7 +271,10 @@ def rank_program(g, core, T, topo):
         act(T.q2[:], T.q1[:], AF.Identity, ["q1"], ["q2"], scale=-1024.0, bias=129.0 * 1024.0)
 
     def u2():
-        lin(U, "pU:U", [(T.Zb[:], T.Wblk2[:], ["Zb", "Wblk2"]), (Id[1.0], T.c33[:], [In(1), "c33"]), (Id[2.0], T.q2[:], [In(2), "q2"])])
+        lin(U, "pU:U", [(T.Zb[:], T.Wblk2[:], ["Zb", "Wblk2"]), (ones, T.c33[:], ["ones", "c33a", "c33b"]),
+                        (Id[-2048.0], T.q1[:], [In(-2048), "q1"])])
+
+    def u2b():
         lin(Uu, "pU:V", [zw, qq])
 
     def u3():
@@ -284,59 +286,59 @@ def rank_program(g, core, T, topo):
         lin(Cst, "pU:C", [zw, qq, (T.If[:], T.Cf[:], ["If", "Cf"])])
 
     u0()
+    mm(T.pT[:, 0:128], T.am_f[:], T.Rf[:], True, True, ["am_f", "Rf"], ["pT:a"])
     u1()
     cp(blk(T.A, 0), T.pT[:, 0:128], ["pT:a"], ["A0_0", "A0_1"])
     send(0, blk(T.A, 0), blk(T.B, 0), "rn0", ["A0_0", "A0_1"])
     tt(T.Wp[:], T.wa[:], T.wg[:], A_.mult, ["wa", "wg"], ["Wp"])
-    ts(T.a3[:], T.ETi[:], float(MAGIC), A_.mult, ["ETi"], ["a3_0", "a3_1"])
-    ts(T.c1[:], T.tvec[:], -37.0, A_.mult, ["tvec"], ["c1"], 37.0 * 15 + 4096.0 - TOP, A_.add)
-    ts(T.a4[:], T.a3[:], EMASK, A_.bitwise_and, ["a3_0", "a3_1"], ["a4_0", "a4_1"])
     ts(blk(T.Cs, 3), T.tvec[:], 64.0, A_.add, ["tvec"], ["Cs3"], unit(5), A_.mult)
-    ts(T.orep[:], T.ioj[:, 0:48], 1.0, A_.mult, ["ioj"], ["orep"])
-    ms(blk(T.Cs, 2), -7.5 * BIG, ["Cs2"])
-    for j, x in enumerate(BS):
-        ts(blk(T.Bs, j), T.Blk[:], x, A_.mult, ["Blk"], ["Bs%d" % j])
+    ts(T.a3[:], T.tvec[:], float(MAGIC), A_.mult, ["tvec"], ["a3_0", "a3_1"])
     u2()
+    for j, l in enumerate(ORDER):
+        act(T.Wk[:, 8 * j:8 * j + 8], T.Wp[:, 8 * l:8 * l + 8], AF.Identity, ["Wp"], ["Wk%d" % j], scale=unit(l) / (1 if l < 5 else 512))
 
     def consts_a():
-        tt(T.Cf[:], T.a4[:], T.c1[:], A_.add, ["a4_0", "a4_1", "c1"], ["Cf"])
-        for j, l in enumerate(ORDER):
-            act(T.Wk[:, 8 * j:8 * j + 8], T.Wp[:, 8 * l:8 * l + 8], AF.Identity, ["Wp"], ["Wk%d" % j], scale=unit(l) / (1 if l < 5 else 512))
+        ts(T.c1[:], T.tvec[:], -37.0, A_.mult, ["tvec"], ["c1"], 37.0 * 15 + 4096.0 - TOP, A_.add)
+        ts(T.a4[:], T.a3[:], EMASK, A_.bitwise_and, ["a3_0", "a3_1"], ["a4_0", "a4_1"])
+        ts(T.mask[:], T.tvec[:], col(1), A_.is_equal, ["tvec", "cols"], ["mask"])
+        ts(col(7), col(1), 8.0, A_.is_ge, ["cols"], ["col7"])
+        ts(T.Sel[:], T.ioj[:, 0:8], col(2), A_.is_equal, ["ioj", "cols"], ["Sel"])
+
+    def consts_b():
+        u3()
+        act(col(6), col(0), AF.Identity, ["cols"], ["col6"], scale=16.0)
+        act(T.Sel2[:], T.Sel[:], AF.Identity, ["Sel"], ["Sel2"], scale=2.0)
+        act(T.mask16[:], T.mask[:], AF.Identity, ["mask", "col6"], ["mask16"], scale=col(6))
+        act(T.l2[:], T.If[:], AF.Identity, ["If", "cols"], ["l2"], scale=col(1))
+        act(T.maskS[:], T.mask[:], AF.Identity, ["mask"], ["maskS"], scale=-1.0 / unit(5))
+        act(T.nSel[:], T.Sel[:], AF.Identity, ["Sel"], ["nSel"], scale=-1.0)
+        act(T.Wy[:], T.Wp[:].indirect(T.orep8[:]), AF.Identity, ["Wp", "orep8"], ["Wy"], scale=-1.0)
         act(T.Wn[:], T.Wp[:].indirect(T.orep[:]), AF.Identity, ["Wp", "orep"], ["Wn"], scale=-1.0)
 
     def consts_c():
-        ts(T.c0[:], T.tvec[:], 0.5, A_.is_lt, ["tvec"], ["c0"], -2.0 ** 88, A_.mult)
-        ts(T.mask[:], T.tvec[:], col(1), A_.is_equal, ["tvec", "cols"], ["mask"])
-        ts(T.Sel[:], T.ioj[:, 0:8], col(2), A_.is_equal, ["ioj", "cols"], ["Sel"])
-        ts(col(6), col(0), 16.0, A_.mult, ["cols"], ["col6"])
-        ts(col(7), col(1), 8.0, A_.is_ge, ["cols"], ["col7"])
-        ts(T.oend[:], T.ioj[:, 0:8], 16.0, A_.mult, ["ioj"], ["oend"], 15.0, A_.add)
-        ts(T.l1[:], T.tvec[:], col(1), A_.is_lt, ["tvec", "cols"], ["l1"])
-        ts(T.mask16[:], T.mask[:], col(6), A_.mult, ["mask", "col6"], ["mask16"])
-        ts(T.Sel2[:], T.Sel[:], 2.0, A_.mult, ["Sel"], ["Sel2"])
         ts(T.orep8[:], T.ioj[:, 0:24], 2.0, A_.mult, ["ioj", "col7"], ["orep8"], col(7), A_.add)
-
-    def consts_b():
-        act(T.maskS[:], T.mask[:], AF.Identity, ["mask"], ["maskS"], scale=-1.0 / unit(5))
-        act(T.nSel[:], T.Sel[:], AF.Identity, ["Sel"], ["nSel"], scale=-1.0)
-        act(T.l2[:], T.If[:], AF.Identity, ["If", "cols"], ["l2"], scale=col(1))
-        act(T.Wy[:], T.Wp[:].indirect(T.orep8[:]), AF.Identity, ["Wp", "orep8"], ["Wy"], scale=-1.0)
-        for x in SC[3:]:
-            act(Id[x], Id[1.0], AF.Identity, [In(1)], [In(x)], scale=x)
+        ts(T.orep[:], T.ioj[:, 0:48], 1.0, A_.mult, ["ioj"], ["orep"])
+        ts(T.c0[:], T.tvec[:], 0.5, A_.is_lt, ["tvec"], ["c0"], -2.0 ** 88, A_.mult)
+        tt(T.Cf[:], T.a4[:], T.c1[:], A_.add, ["a4_0", "a4_1", "c1"], ["Cf"])
 
     def consts_e():
+        ts(T.oend[:], T.ioj[:, 0:8], 16.0, A_.mult, ["ioj"], ["oend"], 15.0, A_.add)
         cp(T.SelH[:], T.Sel[:], ["Sel"], ["SelH"])
+
+    def consts_f():
+        ts(T.l1[:], T.tvec[:], col(1), A_.is_lt, ["tvec", "cols"], ["l1"])
+        ts(blk(T.Cs, 0), T.tvec[:], -7.5, A_.add, ["tvec"], ["Cs0"], BIG, A_.mult)
+        ts(blk(T.Cs, 1), T.tvec[:], -3.5, A_.add, ["tvec"], ["Cs1"], BIG, A_.mult)
         tt(T.l1[:], T.l1[:], T.Blk[:], A_.mult, ["l1", "Blk"], ["l1"])
 
     def consts_d():
-        tt(T.Lin[:], T.l1[:], T.l2[:], A_.subtract, ["l1", "l2"], ["Lin"])
-        ts(blk(T.Cs, 0), T.tvec[:], -7.5, A_.add, ["tvec"], ["Cs0"], BIG, A_.mult)
-        ts(blk(T.Cs, 1), T.tvec[:], -3.5, A_.add, ["tvec"], ["Cs1"], BIG, A_.mult)
+        tt(T.nLin[:], T.l2[:], T.l1[:], A_.subtract, ["l1", "l2"], ["nLin"])
+        ms(blk(T.Cs, 2), -7.5 * BIG, ["Cs2"])
         ts(col(9), col(1), -1.0, A_.mult, ["cols"], ["col9"], 15.0, A_.add)
-        for j, s in enumerate(SHIFTS):
-            ts(blk(T.LM, j), T.Lin[:], -2.0 ** s, A_.mult, ["Lin"], ["LM%d" % j])
+        for j, x in enumerate(BS):
+            act(blk(T.Bs, j), T.Blk[:], AF.Identity, ["Blk"], ["Bs%d" % j], scale=x)
 
-    ranks = lambda x, name: [(x, blk(T.LM, j), [name, "LM%d" % j]) for j in range(4)]
+    ranks = lambda x, name: [(x, T.nLin[:], [name, "nLin"])]
     parts = [(j, 64 * j, 64 * j + 64) for j in range(2)]
     allp = lambda n: [n + "_0", n + "_1"]
     H = lambda a, b: T.pH[:, a:b]
@@ -364,7 +366,8 @@ def rank_program(g, core, T, topo):
 
         for j, a, b in parts:
             tt(T.P1[:, a:b], T.A[:, 128 * t + a:128 * t + b], T.pU[:, a:b], A_.mult, [kA[j], "pU:U"], ["P1_%d" % j])
-        tt(T.f2[:], A, Uu, A_.mult, kA + ["pU:V"], ["f2"])
+        if t > 0:
+            tt(T.f2[:], A, Uu, A_.mult, kA + ["pU:V"], ["f2"])
         turn(T.pT[:, 0:128 - CUT], "pT:a", CUT, 128)
         turn(T.pS[:, 0:CUT], "pS:a", 0, CUT)
         for j, a, b in parts:
@@ -372,18 +375,21 @@ def rank_program(g, core, T, topo):
         unwrap(T.pT[:, 0:128 - CUT], "pT:a", CUT, 128)
         unwrap(T.pS[:, 0:CUT], "pS:a", 0, CUT)
         if t == 0:
-            u3()
+            u2b()
             consts_a()
-        ts(T.f4[:], T.f2[:], 5, A_.arith_shift_right, ["f2"], ["f4"], 4095, A_.bitwise_and)
+        else:
+            ts(T.f4[:], T.f2[:], 5, A_.arith_shift_right, ["f2"], ["f4"], 4095, A_.bitwise_and)
         init_keys()
-        u4()
+        if t > 0:
+            u4()
         offsets(T.offx[:, CUT:128], "offx1", T.pT[:, 0:128 - CUT], "pT:a")
         offsets(T.offx[:, 0:CUT], "offx0", T.pS[:, 0:CUT], "pS:a")
-        if t == 0:
-            consts_c()
         act(T.xb[:, 16 * CUT:2048], Xw.indirect(T.offx[:, CUT:128]), AF.Copy, ["X", "Xpad", "offx1"], ["xb1"])
         cp(T.xb[:, 0:16 * CUT], Xw.indirect(T.offx[:, 0:CUT]), ["X", "Xpad", "offx0"], ["xb0"])
         if t == 0:
+            tt(T.f2[:], A, Uu, A_.mult, kA + ["pU:V"], ["f2"])
+            consts_c()
+            ts(T.f4[:], T.f2[:], 5, A_.arith_shift_right, ["f2"], ["f4"], 4095, A_.bitwise_and)
             consts_b()
 
         def keys(b):
@@ -393,14 +399,26 @@ def rank_program(g, core, T, topo):
 
         def rekey(b):
             for j in range(16):
-                mm(KB_[b][:, j:j + 369:16], T.xb[:, j:2048:16], T.Wp[:, 24 * b:24 * b + 24], j == 0, False, ["xb0", "xb1", "Wp"], [kname[b]], inc=False)
+                mm(KB_[b][:, j:j + 241:16], T.xb[:, j:2048:16], T.Wp[:, 16 * b:16 * b + 16], j == 0, False, ["xb0", "xb1", "Wp"], [kname[b]], inc=False)
 
         keys(0)
         keys(1)
         if not TFIRST:
             keys(2)
-        tt(T.Gu[:], Um, T.mask[:], A_.mult, ["pU:m", "mask"], ["Gu"])
-        tt(H(0, 128), T.f4[:], Cst, A_.add, ["f4", "pU:C"], allp("pH:m1"))
+
+        def from_u():
+            tt(T.Gu[:], Um, T.mask[:], A_.mult, ["pU:m", "mask"], ["Gu"])
+            tt(H(0, 128), T.f4[:], Cst, A_.add, ["f4", "pU:C"], allp("pH:m1"))
+
+        def column():
+            lin(T.pS[:, 128:136], "pS:b", [(T.mask16[:], T.Sel2[:], ["mask16", "Sel2"]), (T.Gu[:], T.Sel[:], ["Gu", "Sel"])])
+
+        def b4():
+            from_u()
+            column()
+
+        if t > 0:
+            from_u()
         ts(H(128, 256), A, 12288.0 - TOP, A_.add, kA, ["pH:A"])
         if t == 0:
             consts_e()
@@ -417,7 +435,8 @@ def rank_program(g, core, T, topo):
             unwrap(T.pT[:, 0:128], "pT:a", 0, 128)
             if TFIRST:
                 keys(2)
-            lin(T.pS[:, 128:136], "pS:b", [(T.mask16[:], T.Sel2[:], ["mask16", "Sel2"]), (T.Gu[:], T.Sel[:], ["Gu", "Sel"])])
+            if t > 0:
+                column()
 
         def b3():
             offsets(T.offy[:], "offy", T.pT[:, 0:128], "pT:a")
@@ -425,6 +444,8 @@ def rank_program(g, core, T, topo):
             act(T.yb[:, 0:16 * YCUT], Xw.indirect(T.offy[:, 0:YCUT]), AF.Copy, ["X", "Xpad", "offy"], ["yb"])
 
         slots = dict(zip(SLOTS, [b1, b2, b3]))
+        if t == 0:
+            slots = dict(zip(SLOTS0, [u4, b1, b2, b3, b4]))
 
         def slot(n):
             if n in slots:
@@ -439,6 +460,8 @@ def rank_program(g, core, T, topo):
         def dcol(l, j, a, b, shift):
             if l == 0:
                 return region(0, a, b, 1 - 2 * shift, 2), lname[0]
+            if l == 5:
+                return T.pU[:, 257 + 2 * a:256 + 2 * b:2], "pU:I_%d" % j
             c = 130 * j + 3 - 2 * shift
             return II[l % 2][:, c:c + 127:2], "I%d_%d" % (l % 2, j)
 
@@ -446,8 +469,9 @@ def rank_program(g, core, T, topo):
             if l > 0:
                 for j, a, b in parts:
                     hk = lname[l // 2] + "h%d_%d" % (l, j)
-                    scan(II[l % 2][:, 130 * j + 2:130 * j + 130], T.D[:, 2 * a:2 * b], region(l, a, b, 0, 1), A_.subtract, A_.min,
-                         ["D_%d" % j, hk, lname[l // 2]], ["I%d_%d" % (l % 2, j)])
+                    out = II[l % 2][:, 130 * j + 2:130 * j + 130] if l < 5 else T.pU[:, 256 + 2 * a:256 + 2 * b]
+                    scan(out, T.D[:, 2 * a:2 * b], region(l, a, b, 0, 1), A_.subtract, A_.min,
+                         ["D_%d" % j, hk, lname[l // 2]], [dcol(l, j, a, b, 0)[1]] + [["pU:C", "pU:m"][j]] * (l == 5))
                     if l > 1:
                         d, kd = dcol(l - 1, j, a, b, 0)
                     else:
@@ -488,7 +512,7 @@ def rank_program(g, core, T, topo):
         if NL_FIRST:
             send(t, nl, nlB, "rl%d" % t, knl)
         if not last:
-            lin(Uu, "pU:V", [(ones, nl, ["ones"] + knl)])
+            lin(Cst, "pU:C", [(ones, nl, ["ones"] + knl)])
         for j in range(16):
             mm(YB_[j // 8][:, j % 8:j % 8 + 377:8], T.yb[:, j:2048:16], T.Wp[:], j % 8 == 0, False,
                ["yb", "yb2", "Wp"], [yname[j // 8]], inc=False)
@@ -497,18 +521,21 @@ def rank_program(g, core, T, topo):
         if not NL_FIRST:
             send(t, nl, nlB, "rl%d" % t, knl)
         if not last:
-            act(T.junk[:], Uu, AF.Identity, ["pU:V"], ["junk", "K32"], scale=32.0, bias=-15.5 / 128, acc=T.K32[:, 0:1])
+            act(T.junk[:], Cst, AF.Identity, ["pU:C"], ["junk", "K32"], scale=32.0, bias=-15.5 / 128, acc=T.K32[:, 0:1])
             act(T.K32[:, 1:2], T.K32[:, 0:1], AF.Identity, ["K32"], ["Kq"], scale=2.0 ** -17, bias=KQ + 2.0 ** -13)
         cp(T.M[:], T.xb[:, 0:2048].indirect(offm), ["xb0", "xb1", koffm], ["M"])
         ts(H(256, 384), B, -TOP, A_.add, [kB], ["pH:B"])
         tt(T.ge[:], T.Zb[:], T.M[:], A_.is_ge, ["Zb", "M"], ["ge"])
         tt(T.xs[:], Xt.indirect(T.offc[:]), T.M[:], A_.add, ["X", "offc", "M"], ["xs"])
+        if t == 0:
+            consts_f()
 
         cnt = (T.Blk[:], T.ge[:], ["ge", "Blk"])
         mm(T.pYA[:, 0:384], T.M[:], T.Wy[:], False, True, ["M", "Wy"], [yname[0]])
         mm(T.pYB[:, 0:384], T.M[:], T.Wy[:], False, True, ["M", "Wy"], [yname[1]])
         lin(T.pS[:, 0:128], "pS:a", [cnt])
         lin(T.pS[:, 128:256], "pS:b", [(nl, Id[-256.0], knl + [In(-256)]), cnt])
+        rekey(2)
         act(T.sY[:, :, :, 0], T.pYA[:, 0:384], AF.Sign, [yname[0]], ["sY0"])
         ts(T.sY[:, :, :, 1], T.pYB[:, 0:384], 1.0, A_.min, [yname[1]], ["sY1"], -1.0, A_.max)
         act(T.fT[:], T.pS[:, 0:128], AF.Sign, ["pS:a"], ["fT"], bias=-5.5)
@@ -524,7 +551,7 @@ def rank_program(g, core, T, topo):
         cp(Xt.indirect(T.offc[:]), T.xh[:], ["xh", "offc"], ["X"])
         if last:
             ts(T.orev[:], T.ioj[:, 0:8], 16.0, A_.mult, ["ioj", "col9"], ["orev"], col(9), A_.add)
-        lin(xA, yname[1], ranks(T.lsT[:], "lsT"), final=False)
+            cp(T.IdH[:], Id[1.0], [In(1)], ["IdH"])
 
         def yx_part(c, ps, key):
             for q in range(4):
@@ -542,7 +569,7 @@ def rank_program(g, core, T, topo):
             ts(T.nfT[:], valB, 0.0, A_.is_lt, [yname[0]], ["nfT"], 0.5, A_.subtract)
 
         def a_sum():
-            lin(xA, yname[1], [Bk(x, n, j) for x, n in ((T.kT[:], "kT"), (T.nfT[:], "nfT")) for j in (2, 3)], first=False)
+            lin(xA, yname[1], ranks(T.lsT[:], "lsT") + [Bk(T.kT[:], "kT", 1), Bk(T.nfT[:], "nfT", 1)])
 
         def b_sum():
             lin(xB, "pT:x", ranks(T.kT[:], "kT"), final=False)
@@ -561,12 +588,12 @@ def rank_program(g, core, T, topo):
                         tt(cut(1 - s % 2, L, j, s, v), cut(s % 2, L, j, s, 0), cut(s % 2, L, j, s, 1), alu,
                            wkeys(L, s % 2, j), [wkeys(L, 1 - s % 2, j)[v]])
                 return fn
-            return [lambda j, a, b: ts(e3[:, a:b], ps[:, c + a:c + b], scale, A_.mult, [kx], [n + "3_%d" % j], shift * MAGIC, A_.add),
+            return [lambda j, a, b: ts(e3[:, a:b], ps[:, c + a:c + b], shift, A_.add, [kx], [n + "3_%d" % j], scale * MAGIC, A_.mult),
                     lambda j, a, b: ts(e4[:, a:b], e3[:, a:b], EMASK, A_.bitwise_and, [n + "3_%d" % j], [n + "4_%d" % j]),
                     lambda j, a, b: tt(T.W0[:, 8 * L + 4 * j:8 * L + 4 * j + 4], e4[:, a:b], H(cn + a, cn + b), A_.add,
                                        [n + "4_%d" % j, kn], wkeys(L, 0, j))] + [stage(s) for s in range(4)]
 
-        a_steps = steps(0, "a", T.pYB, 0, yname[1], 0.5, 23.5, 128, "pH:A", T.a3, T.a4) + [
+        a_steps = steps(0, "a", T.pYB, 0, yname[1], 0.5, 47.0, 128, "pH:A", T.a3, T.a4) + [
             lambda j, a, b: tt(T.a1[:, a:b], T.W0[:, 4 * j:4 * j + 4], T.pYB[:, 128 + a:128 + b], A_.min, wkeys(0, 0, j) + ["pYB:l"], ["a1_%d" % j]),
             lambda j, a, b: tt(T.a1[:, a:b], T.a1[:, a:b], H(a, b), A_.max, ["a1_%d" % j, "pH:m1_%d" % j], ["a1_%d" % j]),
             lambda j, a, b: tt(H(a, b), T.a1[:, a:b], T.pKA[:, a:b], A_.min, ["a1_%d" % j, kname[0]], ["pH:m1_%d" % j])]
@@ -577,29 +604,33 @@ def rank_program(g, core, T, topo):
                 for x in parts:
                     fn(*x)
 
-        yx_early = [(0, T.pU[:, 0:256], "pU:U"), (1, T.pU[:, 256:512], "pU:C")][:YX0] if last else []
+        yx_early = [(0, T.pYB[:, 256:512], "pYB:x")][:YX0] if last else []
         for x in yx_early:
             yx_part(*x)
         if K_EARLY:
             k_sum()
             k_flags()
+        if K_EARLY == 1:
             a_sum()
 
         act(T.y0[:], T.yb[:, 0:2048].indirect(offb), AF.Copy, ["yb", "yb2", koffb], ["y0"])
-        mm(T.pKA[:, 0:384], T.y0[:], T.Wn[:, 0:384], False, True, ["y0", "Wn"], [kname[0]])
-        mm(T.pKB[:, 0:384], T.y0[:], T.Wn[:, 384:768], False, True, ["y0", "Wn"], [kname[1]])
+        for b in range(3):
+            mm(KB_[b][:, 0:256], T.y0[:], blk(T.Wn, b, 256), False, True, ["y0", "Wn"], [kname[b]])
+        if K_EARLY == 2:
+            a_sum()
         if K_EARLY:
             run(a_steps[:EARLY])
             b_sum()
         else:
             k_sum()
         lin(T.pYA[:, 256:384], "pYA:z", [(Id[1.0], T.Zb[:], ["Zb"]), (Id[-1.0], T.y0[:], ["y0", In(-1)])])
-        act(T.sX[:, 0:384], T.pKA[:, 0:384], AF.Sign, [kname[0]], ["sX0"])
-        ts(T.sX[:, 384:768], T.pKB[:, 0:384], 1.0, A_.min, [kname[1]], ["sX1"], -1.0, A_.max)
+        act(blk(T.sX, 1, 256), T.pKB[:, 0:256], AF.Sign, [kname[1]], ["sX1"])
+        for b in (0, 2):
+            ts(blk(T.sX, b, 256), KB_[b][:, 0:256], 1.0, A_.min, [kname[b]], ["sX%d" % b], -1.0, A_.max)
         if not K_EARLY:
             k_flags()
         lin(valA, "pS:d", [(Id[-256.0], T.nlf[:], [In(-256), "nlf"])]
-            + [(blk(T.sX, l), weight(l)[0], ["sX%d" % (l // 3), weight(l)[1]]) for l in range(6)])
+            + [(blk(T.sX, l), weight(l)[0], ["sX%d" % (l // 2), weight(l)[1]]) for l in range(6)])
         if last:
             act(T.Zf[:], T.pYA[:, 256:384], AF.Abs, ["pYA:z"], ["Zf"])
             dma("s", T.yz[:], T.Zf[:], "stz", ["Zf"], [])
@@ -610,26 +641,29 @@ def rank_program(g, core, T, topo):
             a_sum()
         if not last:
             u0()
-        run(a_steps[EARLY if K_EARLY else 0:LEAD])
+        run(a_steps[EARLY if K_EARLY else 0:max(EARLY, 1)])
+        lin(LA, "pYB:l", [Cc(0), Bk(T.kT[:], "kT", 3), Bk(T.nfT[:], "nfT", 3), Bk(T.lsT[:], "lsT", 2), Bk(T.nlf[:], "nlf", 2)], final=False)
+        run(a_steps[max(EARLY, 1):LEAD])
         act(T.gT[:], valA, AF.Sign, ["pS:d"], ["gT"], bias=-255.5)
-        lin(xB, "pT:x", [Bk(T.gT[:], "gT", 0), Bk(T.gT[:], "gT", 1)], first=False)
+        lin(xB, "pT:x", [Bk(T.gT[:], "gT", 0)], first=False)
 
-        lin(T.pS[:, 0:128], "pS:a", [Cc(1), Bk(T.kT[:], "kT", 4), Bk(T.gT[:], "gT", 4)])
-        lin(LA, "pYB:l", [Cc(0), Bk(T.kT[:], "kT", 5), Bk(T.nfT[:], "nfT", 5), Bk(T.lsT[:], "lsT", 4), Bk(T.nlf[:], "nlf", 4), Bk(T.gT[:], "gT", 4)])
+        lin(LA, "pYB:l", [Bk(T.gT[:], "gT", 2)], first=False)
+        lin(T.pS[:, 0:128], "pS:a", [Cc(1), Bk(T.kT[:], "kT", 2), Bk(T.gT[:], "gT", 2)])
         act(T.ab[:], T.pS[:, 0:128], AF.Abs, ["pS:a"], ["ab"], scale=2.0)
         if not last:
             u1()
-        lin(T.pKA[:, 0:128], kname[0], [Cc(2), Bk(T.kT[:], "kT", 6), (Id[1.0], T.ab[:], ["ab"])])
+        lin(T.pKA[:, 0:128], kname[0], [Cc(2), Bk(T.kT[:], "kT", 4), (Id[1.0], T.ab[:], ["ab"])])
         if last:
             for x in yx_early:
                 yx_out(*x)
-            rest = [(0, T.pU[:, 0:256], "pU:U"), (1, T.pU[:, 256:512], "pU:C"), (2, T.pKB[:, 0:256], kname[1]), (3, T.pYA[:, 0:256], yname[0])]
+            rest = [(0, T.pU[:, 0:256], "pU:U"), (1, T.pKB[:, 0:256], kname[1]), (2, T.pYA[:, 0:256], yname[0]), (3, T.pS[:, 128:384], "pS:b")]
             for x in rest[YX0:]:
                 yx_part(*x)
                 yx_out(*x)
         else:
             act(T.X[:, 4096:4112], T.X[:, 0:16], AF.Copy, ["X"], ["Xpad"])
             u2()
+            u2b()
             u3()
 
         for n in range(len(b_steps)):
@@ -644,9 +678,9 @@ def rank_program(g, core, T, topo):
         if not last:
             send(t + 1, An, blk(T.B, t + 1), "rn%d" % (t + 1), kAn)
         else:
-            cp(T.yaf[:], An.indirect(T.orev[:]), kAn + ["orev"], ["yaf"])
-            mm(T.pT[:, 0:128], T.yaf[:], T.If[:], True, True, ["yaf", "If"], ["pT:a"])
-            cp(T.yao[:], T.pT[:, 0:128], ["pT:a"], ["yao"])
+            ts(T.yaf[:], An.indirect(T.orev[:]), -2048.0, A_.add, kAn + ["orev"], ["yaf"])
+            mm(T.pT[:, 0:128], T.yaf[:], T.IdH[:], True, True, ["yaf", "IdH"], ["pT:a"])
+            ts(T.yao[:], T.pT[:, 0:128], 2048.0, A_.add, ["pT:a"], ["yao"])
             dma("a", T.ya[:], T.yao[:], "sta", ["yao"], [])
 
     for s in sorted(total):

@@ -7,17 +7,15 @@ EMASK = (1 << 12) | (1 << 16) | (1 << 20) | (1 << 24)
 TOP = float(1 << 24)
 BIG = 2.0 ** 26
 CUT = 64
-SLOTS = (2, 3, 5)
-SLOTS0 = (6, 3, 4, 7, 9)
-TFIRST = False
-NL_FIRST = True
-NL_POS = 0
-K_EARLY = 2
-QY_ACT = False
 YCUT = 112
-EARLY = 0
+SLOTS = (-1, -1, 2, 3, 5, 6)
+SLOTS0 = (1, 1, 2, 3, 5, 6, 7)
+REKEY = (3, 4)
+GT = 3
+GORD = "abcCAB"
+COPY_ACT = (1, 2)
 LEAD = 5
-YX0 = 0
+FILL = ((10,), (11,), (12,), (13,), (14, 15), (16, 17), ())
 ORDER = [1, 0, 2, 3, 4, 5]
 
 
@@ -32,11 +30,11 @@ SCRATCH = {
     "am_i": _sb(128, I32), "am_f": _sb(128, F), "Zb": _sb(128, BF), "Zf": _sb(128, F), "w_i": _sb(4, I32),
     "cols": _sb(16, F), "coli": _sb(8, I32),
     "ioj": _sb(128, F), "iog": _sb(128, F), "tvec": _sb(128, F), "c0": _sb(128, F),
-    "If": _sb(128, F), "Rf": _sb(128, F), "Is": _sb(128 * 11, BF), "CQ": _sb(256, BF), "Cs": _sb(128 * 4, BF),
+    "If": _sb(128, F), "Rf": _sb(128, F), "Is": _sb(128 * 12, BF), "sT": _sb(128, BF), "fil": _sb(128, F), "CQ": _sb(128, BF), "Cs": _sb(128 * 4, BF),
     "Blk": _sb(128, BF), "Wblk": _sb(128, BF), "Wblk2": _sb(128, BF), "mask": _sb(128, F), "maskS": _sb(128, F), "mask16": _sb(128, BF),
-    "l1": _sb(128, F), "l2": _sb(128, F), "nLin": _sb(128, BF), "Bs": _sb(128 * 5, BF),
+    "l1": _sb(128, BF), "l2": _sb(128, BF), "nLin": _sb(128, BF), "Bs": _sb(128 * 5, BF),
     "Sel": _sb(8, BF), "nSel": _sb(8, F), "Sel2": _sb(8, BF), "SelH": _sb(8, HF), "ones": _sb(128, BF), "c33": _sb(128, BF),
-    "wv": _sb(48, F), "wg": _sb(48, F), "wa": _sb(48, F), "wb": _sb(48, F), "Wp": _sb(48, BF), "Wk": _sb(48, BF), "Kc": _sb(768, BF),
+    "wv": _sb(48, F), "wg": _sb(48, F), "wa": _sb(48, F), "wb": _sb(48, F), "wc": _sb(48, F), "Wp": _sb(48, BF), "Wk": _sb(48, BF), "Kc": _sb(768, BF),
     "Wn": _sb(768, BF), "Wy": _sb(384, BF), "orep": _sb(48, U16), "orep8": _sb(24, U16),
     "oend": _sb(8, U16), "orev": _sb(8, U16), "Cf": _sb(128, F), "c1": _sb(128, F),
     "K32": _sb(4, F), "junk": _sb(128, F),
@@ -50,13 +48,13 @@ SCRATCH = {
     "ab": _sb(128, BF), "a1": _sb(128, F), "a3": _sb(128, I32), "a4": _sb(128, I32), "e3": _sb(128, I32), "e4": _sb(128, I32),
     "W0": ("sbuf", CUBE, F), "W1": ("sbuf", CUBE, F), "m2": _sb(128, I32),
     "xs": _sb(128, I32), "xh": _sb(128, I32),
-    "yaf": _sb(128, HF), "IdH": _sb(128, HF), "yao": _sb(128, F), "yxo": _sb(1024, F),
+    "yaf": _sb(128, HF), "IdH": _sb(128, HF), "yao": _sb(256, F), "yxo": _sb(1024, F),
     "A": _sb(128 * (RO + 1), I32), "B": _sb(128 * RO, I32),
     "nl": _sb(128 * RO, BF), "nlB": _sb(128 * RO, BF), "offm": _sb(16 * RO, U16), "offb": _sb(16 * RO, U16),
     "pKA": ("psum", [128, 512], F), "pKB": ("psum", [128, 512], F), "pYA": ("psum", [128, 512], F), "pYB": ("psum", [128, 512], F),
     "pH": ("psum", [128, 512], F), "pU": ("psum", [128, 512], F), "pT": ("psum", [128, 512], F), "pS": ("psum", [128, 512], F),
 }
-SEMAPHORES = (["cv", "ca", "cp", "cg", "ls", "ldx", "lda", "ldz", "ldw", "ldp", "sta", "stz", "stx0", "stx1", "stx2", "stx3"]
+SEMAPHORES = (["cv", "ca", "cp", "cg", "ls", "ldx", "lda", "ldz", "ldw", "ldp", "sta0", "sta1", "stz", "stx0", "stx1", "stx2", "stx3"]
               + ["rn%d" % t for t in range(RO)] + ["rl%d" % t for t in range(RO)] + ["ro%d" % t for t in range(RO)])
 
 
@@ -205,56 +203,65 @@ def rank_program(g, core, T, topo):
     iota(T.wv[:], [[-3, 6], [-16, 8]], 0, 1, ["wv"])
     iota(T.wg[:], [[0, 6], [1, 8]], 0, 0, ["wg"])
     iota(T.tvec[:], [[0, 8], [1, 16]], 0, 0, ["tvec"])
+    iota(T.c1[:], [[0, 8], [-37, 16]], 37 * 15 + 12288 - (1 << 24), 0, ["c1"])
+    iota(T.D[:, 0:256:2], [[0, 128]], 0, 0, ["D_0", "D_1"])
+    iota(T.CQ[:], [[0, 128]], 62 * 1024, 0, ["CQ0"])
 
     U, Uu, Cst, Um = (blk(T.pU, j) for j in range(4))
     KB_, kname = [T.pKA, T.pKB, T.pU], ["pKA:k", "pKB:k", "pU:U"]
     YB_, yname = [T.pYA, T.pYB], ["pYA:k", "pYB:k"]
     LB, lname = [T.pKA, T.pKB, T.pYA], ["pKA:k", "pKB:k", "pYA:k"]
-    SC = [1.0, -2048.0, -131072.0, 2.0, 4.0, 8.0, 16.0, 32.0, 64.0, -256.0, -1.0]
+    SC = [1.0, -2048.0, -131072.0, 2.0, 4.0, 8.0, 16.0, 32.0, 64.0, -256.0, -1.0, 8192.0]
     Id = {x: blk(T.Is, j) for j, x in enumerate(SC)}
     In = lambda x: "I%d" % x
-    BS = [-0.5, -2.0, BIG / 2, BIG, -BIG]
+    BS = [-1.0, -2.0, BIG / 2, BIG, -BIG]
     Bk = lambda x, name, j: (x, blk(T.Bs, j), [name, "Bs%d" % j])
     Cc = lambda j: (Id[1.0], blk(T.Cs, j), [In(1), "Cs%d" % j])
     ones = T.ones[:]
     unit = lambda l: 2.0 ** (60 - 25 * l)
-    KQ = 129.5 - 2.0 ** -14
+    KQ, KO = 129.5 - 2.0 ** -14, 68.0 * 2 ** 17 - 16
 
     ms(T.ones[:], 1.0, ["ones"])
+    ms(T.I0[:, 1:260:130], 0.0, ["I0_0", "I0_1"])
+    ms(T.I1[:, 1:260:130], 0.0, ["I1_0", "I1_1"])
+    ms(T.offc[:], 0, ["offc"])
+    for j, l in enumerate(ORDER):
+        act(blk(T.Kc, j), ones, AF.Identity, ["ones"], ["Kc%d" % l], scale=-(TOP if l < 5 else 65536.0) * unit(l))
     ts(T.coli[:, 1:2], T.coli[:, 0:1], 15, A_.bitwise_and, ["coli0"], ["coli1"])
     ts(T.coli[:, 2:3], T.coli[:, 0:1], 4, A_.arith_shift_right, ["coli0"], ["coli2"])
-    ms(T.K32[:, 0:1], -15.5, ["K32"])
+    ms(T.K32[:, 0:1], KO, ["K32"])
     ms(T.K32[:, 1:2], KQ, ["Kq"])
-    ms(T.CQ[:, 0:128], 62.0 * 1024, ["CQ0"])
-    ms(T.CQ[:, 128:256], 68.0 * 1024, ["CQ1"])
     cp(T.cols[:, 0:3], T.coli[:, 0:3], ["coli0", "coli1", "coli2"], ["cols"])
-    ms(T.D[:], 0.0, ["D_0", "D_1"])
+    ms(T.c33[0:64, :], 129.0 * 32, ["c33a"])
+    ms(T.c33[64:128, :], 33.0 / 64, ["c33b"])
+    ms(T.offm[:], 0, ["offm%d" % t for t in range(RO)])
     ts(col(3), col(1), -2.0, A_.mult, ["cols"], ["col3a"], 15.0, A_.add)
     ts(T.If[:], T.ioj[:], col(0), A_.is_equal, ["ioj", "cols"], ["If"])
     tt(col(4), col(3), col(0), A_.add, ["col3a", "cols"], ["col4"])
     ts(T.Blk[:], T.iog[:], col(2), A_.is_equal, ["iog", "cols"], ["Blk"])
     ts(T.Rf[:], T.ioj[:], col(4), A_.is_equal, ["ioj", "col4"], ["Rf"])
-    ms(T.I0[:, 1:260:130], 0.0, ["I0_0", "I0_1"])
-    ms(T.I1[:, 1:260:130], 0.0, ["I1_0", "I1_1"])
-    ms(T.c33[0:64, :], 129.0 * 32, ["c33a"])
-    ms(T.c33[64:128, :], 33.0 / 64, ["c33b"])
-    ms(T.offm[:], 0, ["offm%d" % t for t in range(RO)])
     ts(T.wa[:], T.wv[:], 0.0, A_.is_equal, ["wv"], ["wa"], 65536.0, A_.mult)
     ts(T.wb[:], T.wv[:], 1.0, A_.is_equal, ["wv"], ["wb"], 256.0, A_.mult)
-    ts(T.wv[:], T.wv[:], 2.0, A_.is_equal, ["wv"], ["wv"])
-    ts(T.wg[:], T.wg[:], col(2), A_.is_equal, ["wg", "cols"], ["wg"])
+    ts(T.wc[:], T.wv[:], 2.0, A_.is_equal, ["wv"], ["wc"])
 
-    for x in SC:
+    for x in SC[:5]:
         act(Id[x], T.If[:], AF.Identity, ["If"], [In(x)], scale=x)
 
-    cp(col(5), T.w_i[:, 0:1], ["w_i"], ["col5"])
+    tt(T.Wblk[:], T.w_i[:, 0:1].indirect(T.offc[:]), T.Blk[:], A_.mult, ["w_i", "offc", "Blk"], ["Wblk"])
     cp(T.am_f[:], T.am_i[:], ["am_i"], ["am_f"])
     tt(T.wa[:], T.wa[:], T.wb[:], A_.add, ["wa", "wb"], ["wa"])
-    ts(T.Wblk[:], T.Blk[:], col(5), A_.mult, ["Blk", "col5"], ["Wblk"])
-    ts(T.Wblk2[:], T.Blk[:], col(5), A_.mult, ["Blk", "col5"], ["Wblk2"], 2.0, A_.mult)
-    tt(T.wa[:], T.wa[:], T.wv[:], A_.add, ["wa", "wv"], ["wa"])
-    for j, l in enumerate(ORDER):
-        ms(blk(T.Kc, j), -(TOP if l < 5 else 65536.0) * unit(l), ["Kc%d" % l])
+    ts(T.Wblk2[:], T.Wblk[:], 2.0, A_.mult, ["Wblk"], ["Wblk2"])
+    ts(T.wg[:], T.wg[:], col(2), A_.is_equal, ["wg", "cols"], ["wg"])
+    ts(col(7), col(1), 8.0, A_.is_ge, ["cols"], ["col7"])
+    tt(T.wa[:], T.wa[:], T.wc[:], A_.add, ["wa", "wc"], ["wa"])
+    ts(T.orep8[:], T.ioj[:, 0:24], 2.0, A_.mult, ["ioj", "col7"], ["orep8"], col(7), A_.add)
+    ts(T.orep[:], T.ioj[:, 0:48], 1.0, A_.mult, ["ioj"], ["orep"])
+    tt(T.Wp[:], T.wa[:], T.wg[:], A_.mult, ["wa", "wg"], ["Wp"])
+
+    def level_weights(a, b):
+        for j in range(a, b):
+            l = ORDER[j]
+            act(T.Wk[:, 8 * j:8 * j + 8], T.Wp[:, 8 * l:8 * l + 8], AF.Identity, ["Wp"], ["Wk%d" % j], scale=unit(l) / (1 if l < 5 else 512))
 
     def init_keys():
         for b in range(3):
@@ -285,39 +292,61 @@ def rank_program(g, core, T, topo):
         lin(Um, "pU:m", [zw, qq, (Id[1.0], T.r2[:], [In(1), "r2"])])
         lin(Cst, "pU:C", [zw, qq, (T.If[:], T.Cf[:], ["If", "Cf"])])
 
-    u0()
+    lin(T.pYB[:, 0:128], "pYB:k", [(T.Wblk[:], T.Zb[:], ["Zb", "Wblk"])])
     mm(T.pT[:, 0:128], T.am_f[:], T.Rf[:], True, True, ["am_f", "Rf"], ["pT:a"])
+    act(T.r1[:], T.pYB[:, 0:128], AF.Identity, ["pYB:k"], ["r1"], scale=2.0 ** -10, bias=128.5 + 2.0 ** -11)
+    mm(T.pS[:, 0:128], T.Rf[:], T.am_f[:], True, True, ["am_f", "Rf"], ["pS:a"])
+    level_weights(0, 3)
+    u0()
+    lin(T.pYB[:, 128:256], "pYB:l", [(T.Wblk2[:], T.Zb[:], ["Zb", "Wblk2"]), (ones, T.c33[:], ["ones", "c33a", "c33b"]),
+                                     (Id[-2048.0], T.r1[:], [In(-2048), "r1"])])
     u1()
+    for j in (1, 2, 3, 4):
+        ts(blk(T.Bs, j), T.Blk[:], BS[j], A_.mult, ["Blk"], ["Bs%d" % j])
     cp(blk(T.A, 0), T.pT[:, 0:128], ["pT:a"], ["A0_0", "A0_1"])
     send(0, blk(T.A, 0), blk(T.B, 0), "rn0", ["A0_0", "A0_1"])
-    tt(T.Wp[:], T.wa[:], T.wg[:], A_.mult, ["wa", "wg"], ["Wp"])
+    cp(T.P1[:], T.pS[:, 0:128], ["pS:a"], ["P1_0", "P1_1"])
+    for x in SC[7:]:
+        iota(Id[x], [[0, 128]], int(x), 0, [In(x)])
+        op("g", lambda x=x: g.affine_select(Id[x], Id[x], [[-1, 128]], A_.is_equal, 0.0, 0, 1), [In(x)], [In(x)])
+    op("g", lambda: g.affine_select(T.l1[:], T.Blk[:], [[-1, 128]], A_.is_gt, 0.0, 0, 1), ["Blk"], ["l1"])
+    lanes = [(1, CUT, 128), (0, 0, CUT)]
+    for j, a, b in lanes:
+        tt(T.e3[:, a:b], T.P1[:, a:b], T.pYB[:, 128 + a:128 + b], A_.mult, ["P1_0", "P1_1", "pYB:l"], ["e3_%d" % j])
     ts(blk(T.Cs, 3), T.tvec[:], 64.0, A_.add, ["tvec"], ["Cs3"], unit(5), A_.mult)
+    for j, a, b in lanes:
+        ts(T.e4[:, a:b], T.e3[:, a:b], 5, A_.arith_shift_right, ["e3_%d" % j], ["e4_%d" % j], 4095, A_.bitwise_and)
+    ts(Id[8.0], Id[1.0], 8.0, A_.mult, [In(1)], [In(8)])
+    for j, a, b in lanes:
+        cp(T.offx[:, a:b], T.e4[:, a:b], ["e4_%d" % j], ["offx%d" % j])
     ts(T.a3[:], T.tvec[:], float(MAGIC), A_.mult, ["tvec"], ["a3_0", "a3_1"])
+    ts(Id[16.0], Id[1.0], 16.0, A_.mult, [In(1)], [In(16)])
     u2()
-    for j, l in enumerate(ORDER):
-        act(T.Wk[:, 8 * j:8 * j + 8], T.Wp[:, 8 * l:8 * l + 8], AF.Identity, ["Wp"], ["Wk%d" % j], scale=unit(l) / (1 if l < 5 else 512))
+    u2b()
+    level_weights(3, 6)
 
     def consts_a():
-        ts(T.c1[:], T.tvec[:], -37.0, A_.mult, ["tvec"], ["c1"], 37.0 * 15 + 4096.0 - TOP, A_.add)
-        ts(T.a4[:], T.a3[:], EMASK, A_.bitwise_and, ["a3_0", "a3_1"], ["a4_0", "a4_1"])
         ts(T.mask[:], T.tvec[:], col(1), A_.is_equal, ["tvec", "cols"], ["mask"])
-        ts(col(7), col(1), 8.0, A_.is_ge, ["cols"], ["col7"])
         ts(T.Sel[:], T.ioj[:, 0:8], col(2), A_.is_equal, ["ioj", "cols"], ["Sel"])
+        ts(T.a4[:], T.a3[:], EMASK, A_.bitwise_and, ["a3_0", "a3_1"], ["a4_0", "a4_1"])
+        tt(T.f2[:], blk(T.A, 0), Uu, A_.mult, ["A0_0", "A0_1", "pU:V"], ["f2"])
 
     def consts_b():
-        u3()
         act(col(6), col(0), AF.Identity, ["cols"], ["col6"], scale=16.0)
+        act(T.l2[:], T.If[:], AF.Identity, ["If", "cols"], ["l2"], scale=col(1))
+        act(blk(T.Bs, 0), T.Blk[:], AF.Identity, ["Blk"], ["Bs0"], scale=BS[0])
+        u3()
         act(T.Sel2[:], T.Sel[:], AF.Identity, ["Sel"], ["Sel2"], scale=2.0)
         act(T.mask16[:], T.mask[:], AF.Identity, ["mask", "col6"], ["mask16"], scale=col(6))
-        act(T.l2[:], T.If[:], AF.Identity, ["If", "cols"], ["l2"], scale=col(1))
         act(T.maskS[:], T.mask[:], AF.Identity, ["mask"], ["maskS"], scale=-1.0 / unit(5))
         act(T.nSel[:], T.Sel[:], AF.Identity, ["Sel"], ["nSel"], scale=-1.0)
         act(T.Wy[:], T.Wp[:].indirect(T.orep8[:]), AF.Identity, ["Wp", "orep8"], ["Wy"], scale=-1.0)
-        act(T.Wn[:], T.Wp[:].indirect(T.orep[:]), AF.Identity, ["Wp", "orep"], ["Wn"], scale=-1.0)
+        minus(0)
+
+    def minus(b):
+        act(blk(T.Wn, b, 256), T.Wp[:].indirect(blk(T.orep, b, 16)), AF.Identity, ["Wp", "orep"], ["Wn%d" % b], scale=-1.0)
 
     def consts_c():
-        ts(T.orep8[:], T.ioj[:, 0:24], 2.0, A_.mult, ["ioj", "col7"], ["orep8"], col(7), A_.add)
-        ts(T.orep[:], T.ioj[:, 0:48], 1.0, A_.mult, ["ioj"], ["orep"])
         ts(T.c0[:], T.tvec[:], 0.5, A_.is_lt, ["tvec"], ["c0"], -2.0 ** 88, A_.mult)
         tt(T.Cf[:], T.a4[:], T.c1[:], A_.add, ["a4_0", "a4_1", "c1"], ["Cf"])
 
@@ -326,19 +355,13 @@ def rank_program(g, core, T, topo):
         cp(T.SelH[:], T.Sel[:], ["Sel"], ["SelH"])
 
     def consts_f():
-        ts(T.l1[:], T.tvec[:], col(1), A_.is_lt, ["tvec", "cols"], ["l1"])
-        ts(blk(T.Cs, 0), T.tvec[:], -7.5, A_.add, ["tvec"], ["Cs0"], BIG, A_.mult)
-        ts(blk(T.Cs, 1), T.tvec[:], -3.5, A_.add, ["tvec"], ["Cs1"], BIG, A_.mult)
-        tt(T.l1[:], T.l1[:], T.Blk[:], A_.mult, ["l1", "Blk"], ["l1"])
-
-    def consts_d():
         tt(T.nLin[:], T.l2[:], T.l1[:], A_.subtract, ["l1", "l2"], ["nLin"])
         ms(blk(T.Cs, 2), -7.5 * BIG, ["Cs2"])
-        ts(col(9), col(1), -1.0, A_.mult, ["cols"], ["col9"], 15.0, A_.add)
-        for j, x in enumerate(BS):
-            act(blk(T.Bs, j), T.Blk[:], AF.Identity, ["Blk"], ["Bs%d" % j], scale=x)
+        ts(T.f4[:], T.f2[:], 5, A_.arith_shift_right, ["f2"], ["f4"], 4095, A_.bitwise_and)
 
-    ranks = lambda x, name: [(x, T.nLin[:], [name, "nLin"])]
+    def consts_g(n):
+        ts(blk(T.Cs, n), T.tvec[:], [0.5, -3.5][n], A_.add, ["tvec"], ["Cs%d" % n], BIG, A_.mult)
+
     parts = [(j, 64 * j, 64 * j + 64) for j in range(2)]
     allp = lambda n: [n + "_0", n + "_1"]
     H = lambda a, b: T.pH[:, a:b]
@@ -359,37 +382,32 @@ def rank_program(g, core, T, topo):
             lin(ps, key, [(T.P1[:], T.If[:, a:b], allp("P1") + ["If"]), (ones, T.CQ[:, a:b], ["ones", "CQ0"])], final=False)
 
         def unwrap(ps, key, a, b):
-            lin(ps, key, [(T.qp[:], T.Is[:, 256 + a:256 + b], allp("qp") + [In(SC[2])]), (ones, T.CQ[:, 128 + a:128 + b], ["ones", "CQ1"])], first=False)
+            lin(ps, key, [(T.qp[:], T.Is[:, 256 + a:256 + b], allp("qp") + [In(SC[2])])], first=False)
 
         def offsets(out, okey, ps, key):
-            ts(out, ps, T.K32[:, 0:1], A_.add, [key, "K32"], [okey], 2.0 ** -5, A_.mult)
+            ts(out, ps, T.K32[:, 0:1], A_.add, [key, "K32"], [okey], 2.0 ** -5 + 2.0 ** -25, A_.mult)
 
-        for j, a, b in parts:
-            tt(T.P1[:, a:b], T.A[:, 128 * t + a:128 * t + b], T.pU[:, a:b], A_.mult, [kA[j], "pU:U"], ["P1_%d" % j])
         if t > 0:
+            for j, a, b in parts:
+                tt(T.P1[:, a:b], T.A[:, 128 * t + a:128 * t + b], T.pU[:, a:b], A_.mult, [kA[j], "pU:U"], ["P1_%d" % j])
+            turn(T.pT[:, 0:128 - CUT], "pT:a", CUT, 128)
+            turn(T.pS[:, 0:CUT], "pS:a", 0, CUT)
+            for j, a, b in parts:
+                ts(T.qp[:, a:b], T.P1[:, a:b], 2.0 ** -17, A_.mult, ["P1_%d" % j, "Kq"], ["qp_%d" % j], T.K32[:, 1:2], A_.add)
+            unwrap(T.pT[:, 0:128 - CUT], "pT:a", CUT, 128)
             tt(T.f2[:], A, Uu, A_.mult, kA + ["pU:V"], ["f2"])
-        turn(T.pT[:, 0:128 - CUT], "pT:a", CUT, 128)
-        turn(T.pS[:, 0:CUT], "pS:a", 0, CUT)
-        for j, a, b in parts:
-            ts(T.qp[:, a:b], T.P1[:, a:b], 2.0 ** -17, A_.mult, ["P1_%d" % j, "Kq"], ["qp_%d" % j], T.K32[:, 1:2], A_.add)
-        unwrap(T.pT[:, 0:128 - CUT], "pT:a", CUT, 128)
-        unwrap(T.pS[:, 0:CUT], "pS:a", 0, CUT)
-        if t == 0:
-            u2b()
-            consts_a()
-        else:
+            unwrap(T.pS[:, 0:CUT], "pS:a", 0, CUT)
             ts(T.f4[:], T.f2[:], 5, A_.arith_shift_right, ["f2"], ["f4"], 4095, A_.bitwise_and)
         init_keys()
         if t > 0:
             u4()
-        offsets(T.offx[:, CUT:128], "offx1", T.pT[:, 0:128 - CUT], "pT:a")
-        offsets(T.offx[:, 0:CUT], "offx0", T.pS[:, 0:CUT], "pS:a")
+            offsets(T.offx[:, CUT:128], "offx1", T.pT[:, 0:128 - CUT], "pT:a")
+            offsets(T.offx[:, 0:CUT], "offx0", T.pS[:, 0:CUT], "pS:a")
         act(T.xb[:, 16 * CUT:2048], Xw.indirect(T.offx[:, CUT:128]), AF.Copy, ["X", "Xpad", "offx1"], ["xb1"])
         cp(T.xb[:, 0:16 * CUT], Xw.indirect(T.offx[:, 0:CUT]), ["X", "Xpad", "offx0"], ["xb0"])
         if t == 0:
-            tt(T.f2[:], A, Uu, A_.mult, kA + ["pU:V"], ["f2"])
+            consts_a()
             consts_c()
-            ts(T.f4[:], T.f2[:], 5, A_.arith_shift_right, ["f2"], ["f4"], 4095, A_.bitwise_and)
             consts_b()
 
         def keys(b):
@@ -401,57 +419,54 @@ def rank_program(g, core, T, topo):
             for j in range(16):
                 mm(KB_[b][:, j:j + 241:16], T.xb[:, j:2048:16], T.Wp[:, 16 * b:16 * b + 16], j == 0, False, ["xb0", "xb1", "Wp"], [kname[b]], inc=False)
 
-        keys(0)
-        keys(1)
-        if not TFIRST:
-            keys(2)
+        for b in range(3):
+            keys(b)
 
         def from_u():
             tt(T.Gu[:], Um, T.mask[:], A_.mult, ["pU:m", "mask"], ["Gu"])
-            tt(H(0, 128), T.f4[:], Cst, A_.add, ["f4", "pU:C"], allp("pH:m1"))
+            tt(T.fil[:], T.f4[:], Cst, A_.add, ["f4", "pU:C"], ["fil"])
 
         def column():
             lin(T.pS[:, 128:136], "pS:b", [(T.mask16[:], T.Sel2[:], ["mask16", "Sel2"]), (T.Gu[:], T.Sel[:], ["Gu", "Sel"])])
 
-        def b4():
-            from_u()
-            column()
+        def b1(j, a, b):
+            tt(T.P1[:, a:b], T.B[:, 128 * t + a:128 * t + b], T.pU[:, a:b], A_.mult, [kB, "pU:U"], ["P1_%d" % j])
+            if j:
+                turn(T.pT[:, 0:128], "pT:a", 0, 128)
+
+        def b2(j, a, b):
+            ts(T.qp[:, a:b], T.P1[:, a:b], 2.0 ** -17, A_.mult, ["P1_%d" % j, "Kq"], ["qp_%d" % j], T.K32[:, 1:2], A_.add)
+            if j:
+                unwrap(T.pT[:, 0:128], "pT:a", 0, 128)
+                if t > 0:
+                    column()
+
+        def b3(j, a, b):
+            offsets(T.offy[:, a:b], "offy%d" % j, T.pT[:, a:b], "pT:a")
+            b = min(b, YCUT if t else 128)
+            act(T.yb[:, 16 * a:16 * b], Xw.indirect(T.offy[:, a:b]), AF.Copy, ["X", "Xpad", "offy%d" % j], ["yb%d" % j])
+            if j:
+                mm(T.pT[:, 128:136], T.mask16[:], T.Sel[:], True, False, ["mask16", "Sel"], ["pT:m"], inc=False)
 
         if t > 0:
             from_u()
-        ts(H(128, 256), A, 12288.0 - TOP, A_.add, kA, ["pH:A"])
+            ts(H(128, 256), A, 12288.0 - TOP, A_.add, kA, ["pH:A"])
         if t == 0:
             consts_e()
-
-        def b1():
-            tt(T.P1[:], B, U, A_.mult, [kB, "pU:U"], allp("P1"))
-            turn(T.pT[:, 0:128], "pT:a", 0, 128)
-            if QY_ACT:
-                act(T.qp[:], T.P1[:], AF.Identity, allp("P1") + ["Kq"], allp("qp"), scale=2.0 ** -17, bias=T.K32[:, 1:2])
-
-        def b2():
-            if not QY_ACT:
-                ts(T.qp[:], T.P1[:], 2.0 ** -17, A_.mult, allp("P1") + ["Kq"], allp("qp"), T.K32[:, 1:2], A_.add)
-            unwrap(T.pT[:, 0:128], "pT:a", 0, 128)
-            if TFIRST:
-                keys(2)
-            if t > 0:
-                column()
-
-        def b3():
-            offsets(T.offy[:], "offy", T.pT[:, 0:128], "pT:a")
-            mm(T.pT[:, 128:136], T.mask16[:], T.Sel[:], True, False, ["mask16", "Sel"], ["pT:m"], inc=False)
-            act(T.yb[:, 0:16 * YCUT], Xw.indirect(T.offy[:, 0:YCUT]), AF.Copy, ["X", "Xpad", "offy"], ["yb"])
-
-        slots = dict(zip(SLOTS, [b1, b2, b3]))
-        if t == 0:
-            slots = dict(zip(SLOTS0, [u4, b1, b2, b3, b4]))
+        if t == 1:
+            ts(col(9), col(1), -1.0, A_.mult, ["cols"], ["col9"], 15.0, A_.add)
+            cp(T.IdH[:], Id[1.0], [In(1)], ["IdH"])
+        if t == 2:
+            ts(T.orev[:], T.ioj[:, 0:8], 16.0, A_.mult, ["ioj", "col9"], ["orev"], col(9), A_.add)
+        pieces = [(fn, x) for fn in (b1, b2, b3) for x in parts]
+        slots = list(zip(SLOTS if t else SLOTS0, pieces + [(u4, ())]))
 
         def slot(n):
-            if n in slots:
-                slots[n]()
+            for m, (fn, x) in slots:
+                if m == n:
+                    fn(*x)
 
-        slot(0)
+        slot(-1)
 
         def region(l, a, b, first, step):
             c = 256 * (ORDER.index(l) % 2) + 2 * a + first
@@ -461,7 +476,7 @@ def rank_program(g, core, T, topo):
             if l == 0:
                 return region(0, a, b, 1 - 2 * shift, 2), lname[0]
             if l == 5:
-                return T.pU[:, 257 + 2 * a:256 + 2 * b:2], "pU:I_%d" % j
+                return T.pH[:, 257 + 2 * a:256 + 2 * b:2], "pH:I_%d" % j
             c = 130 * j + 3 - 2 * shift
             return II[l % 2][:, c:c + 127:2], "I%d_%d" % (l % 2, j)
 
@@ -469,17 +484,16 @@ def rank_program(g, core, T, topo):
             if l > 0:
                 for j, a, b in parts:
                     hk = lname[l // 2] + "h%d_%d" % (l, j)
-                    out = II[l % 2][:, 130 * j + 2:130 * j + 130] if l < 5 else T.pU[:, 256 + 2 * a:256 + 2 * b]
+                    out = II[l % 2][:, 130 * j + 2:130 * j + 130] if l < 5 else H(256 + 2 * a, 256 + 2 * b)
                     scan(out, T.D[:, 2 * a:2 * b], region(l, a, b, 0, 1), A_.subtract, A_.min,
-                         ["D_%d" % j, hk, lname[l // 2]], [dcol(l, j, a, b, 0)[1]] + [["pU:C", "pU:m"][j]] * (l == 5))
+                         ["D_%d" % j, hk, lname[l // 2]], [dcol(l, j, a, b, 0)[1]] + ["pH:B"] * (l == 5 and j == 0))
                     if l > 1:
                         d, kd = dcol(l - 1, j, a, b, 0)
                     else:
                         d, kd = T.D[:, 2 * a + 1:2 * b:2], "D_%d" % j
                     tt(T.Qr[:, a:b], region(l, a, b, 0, 2), d, A_.subtract, [hk, kd], ["Q_%d" % j])
-                slot(2 * l)
-            if l in (2, 4):
-                rekey(l // 2 - 1)
+            if l in REKEY:
+                rekey(REKEY.index(l))
             for j, a, b in parts:
                 q, kq = (T.Qr[:, a:b], "Q_%d" % j) if l else (T.c0[:, a:b], "c0")
                 if l == 5:
@@ -487,71 +501,86 @@ def rank_program(g, core, T, topo):
                     scan(T.Hs[:, a:b], q, d, A_.min, A_.max, [kd, kq], ["Hs_%d" % j])
                     continue
                 d, kd = dcol(l, j, a, b, 1)
-                cp(T.D[:, 2 * a + 1:2 * b:2], dcol(l, j, a, b, 0)[0], [kd], ["D_%d" % j])
+                if l in COPY_ACT and t > 0:
+                    act(T.D[:, 2 * a + 1:2 * b:2], dcol(l, j, a, b, 0)[0], AF.Copy, [kd], ["D_%d" % j])
+                else:
+                    cp(T.D[:, 2 * a + 1:2 * b:2], dcol(l, j, a, b, 0)[0], [kd], ["D_%d" % j])
                 scan(region(l + 1, a, b, 0, 2), d, q, A_.max, A_.min, [kd, kq], [lname[(l + 1) // 2] + "h%d_%d" % (l + 1, j)])
-            slot(2 * l + 1)
+                slot(2 * l + j)
 
         def dead(j, a, b):
             d, kd = dcol(5, j, a, b, 0)
             tt(T.nl[:, 128 * t + a:128 * t + b], d, T.Hs[:, a:b], A_.is_lt, [kd, "Hs_%d" % j], [knl[j]])
 
-        ends = T.Hs[:].indirect(T.oend[:])
-        cp(T.offc[:], T.pS[:, 128:136], ["pS:b"], ["offc"])
-        dead(*parts[0])
-        if NL_POS == 0:
-            dead(*parts[1])
-        tt(T.G1[:], ends, T.maskS[:], A_.mult, allp("Hs") + ["oend", "maskS"], ["G1"])
-        if NL_POS == 1:
-            dead(*parts[1])
-        tt(T.G2[:], ends, T.maskS[:], A_.mult, allp("Hs") + ["oend", "maskS"], ["G2"])
-        lin(T.pT[:, 128:136], "pT:m", [(T.G1[:], T.nSel[:], ["G1", "nSel"]), (T.G2[:], T.SelH[:], ["G2", "SelH"])], first=False)
-        if NL_POS == 2:
-            dead(*parts[1])
-        if YCUT < 128:
-            cp(T.yb[:, 16 * YCUT:2048], Xw.indirect(T.offy[:, YCUT:128]), ["X", "Xpad", "offy"], ["yb2"])
-        if NL_FIRST:
-            send(t, nl, nlB, "rl%d" % t, knl)
-        if not last:
+        def ends(G, n, j, a, b):
+            tt(G[:, a:b], T.Hs[:, a:b].indirect(T.oend[:, 0:4]), T.maskS[:, a:b], A_.mult, ["Hs_%d" % j, "oend", "maskS"], [n + "_%d" % j])
+
+        if t > 0:
+            cp(T.offc[:], T.pS[:, 128:136], ["pS:b"], ["offc"])
+        for c in GORD:
+            x = parts[c in "ABC"]
+            if c in "aA":
+                ends(T.G1, "G1", *x)
+            elif c in "bB":
+                ends(T.G2, "G2", *x)
+            else:
+                dead(*x)
+        send(t, nl, nlB, "rl%d" % t, knl)
+        lin(T.pT[:, 128:136], "pT:m", [(T.G1[:], T.nSel[:], allp("G1") + ["nSel"]), (T.G2[:], T.SelH[:], allp("G2") + ["SelH"])], first=False)
+        if t == 0:
+            tt(T.Gu[:], Um, T.mask[:], A_.mult, ["pU:m", "mask"], ["Gu"])
+            column()
+            consts_f()
+        else:
+            cp(T.yb[:, 16 * YCUT:2048], Xw.indirect(T.offy[:, YCUT:128]), ["X", "Xpad", "offy1"], ["yb2"])
+        if 0 < t < RO - 1:
             lin(Cst, "pU:C", [(ones, nl, ["ones"] + knl)])
         for j in range(16):
             mm(YB_[j // 8][:, j % 8:j % 8 + 377:8], T.yb[:, j:2048:16], T.Wp[:], j % 8 == 0, False,
-               ["yb", "yb2", "Wp"], [yname[j // 8]], inc=False)
+               ["yb0", "yb1", "yb2", "Wp"], [yname[j // 8]], inc=False)
         cp(offm, T.pT[:, 128:136], ["pT:m"], [koffm])
         send(t, T.offm[:, 16 * t:16 * t + 16], T.offb[:, 16 * t:16 * t + 16], "ro%d" % t, [koffm])
-        if not NL_FIRST:
-            send(t, nl, nlB, "rl%d" % t, knl)
-        if not last:
-            act(T.junk[:], Cst, AF.Identity, ["pU:C"], ["junk", "K32"], scale=32.0, bias=-15.5 / 128, acc=T.K32[:, 0:1])
-            act(T.K32[:, 1:2], T.K32[:, 0:1], AF.Identity, ["K32"], ["Kq"], scale=2.0 ** -17, bias=KQ + 2.0 ** -13)
-        cp(T.M[:], T.xb[:, 0:2048].indirect(offm), ["xb0", "xb1", koffm], ["M"])
-        ts(H(256, 384), B, -TOP, A_.add, [kB], ["pH:B"])
-        tt(T.ge[:], T.Zb[:], T.M[:], A_.is_ge, ["Zb", "M"], ["ge"])
-        tt(T.xs[:], Xt.indirect(T.offc[:]), T.M[:], A_.add, ["X", "offc", "M"], ["xs"])
+        act(T.M[:, 64:128], T.xb[:, 0:2048].indirect(T.offm[:, 16 * t + 4:16 * t + 8]), AF.Copy, ["xb0", "xb1", koffm], ["M_1"])
+        cp(T.M[:, 0:64], T.xb[:, 0:2048].indirect(T.offm[:, 16 * t:16 * t + 4]), ["xb0", "xb1", koffm], ["M_0"])
+
+        def count():
+            act(T.junk[:], Cst, AF.Identity, ["pU:C"], ["junk", "K"], scale=32.0, acc=T.K32[:, 2:3])
+            act(T.K32[:, 0:1], T.K32[:, 2:3], AF.Identity, ["K"], ["K32"], bias=KO)
+            act(T.K32[:, 1:2], T.K32[:, 2:3], AF.Identity, ["K"], ["Kq"], scale=2.0 ** -17, bias=KQ)
+
         if t == 0:
-            consts_f()
+            minus(1)
+            minus(2)
+        elif not last:
+            count()
+        ts(H(256, 384), B, -TOP, A_.add, [kB], ["pH:B", "pH:I_0"])
+        if t == 0:
+            cp(T.offc[:], T.pS[:, 128:136], ["pS:b"], ["offc"])
+            tt(T.fil[:], T.f4[:], Cst, A_.add, ["f4", "pU:C"], ["fil"])
+        tt(T.ge[:], T.Zb[:], T.M[:], A_.is_ge, ["Zb"] + allp("M"), ["ge"])
+        tt(T.xs[:], Xt.indirect(T.offc[:]), T.M[:], A_.add, ["X", "offc"] + allp("M"), ["xs"])
+        if t == 0:
+            ts(H(128, 256), A, 12288.0 - TOP, A_.add, kA, ["pH:A"])
 
         cnt = (T.Blk[:], T.ge[:], ["ge", "Blk"])
-        mm(T.pYA[:, 0:384], T.M[:], T.Wy[:], False, True, ["M", "Wy"], [yname[0]])
-        mm(T.pYB[:, 0:384], T.M[:], T.Wy[:], False, True, ["M", "Wy"], [yname[1]])
+        for b in range(2):
+            mm(YB_[b][:, 0:384], T.M[:], T.Wy[:], False, True, allp("M") + ["Wy"], [yname[b]])
         lin(T.pS[:, 0:128], "pS:a", [cnt])
         lin(T.pS[:, 128:256], "pS:b", [(nl, Id[-256.0], knl + [In(-256)]), cnt])
+        if t == 0:
+            lin(Cst, "pU:C", [(ones, nl, ["ones"] + knl)])
         rekey(2)
         act(T.sY[:, :, :, 0], T.pYA[:, 0:384], AF.Sign, [yname[0]], ["sY0"])
         ts(T.sY[:, :, :, 1], T.pYB[:, 0:384], 1.0, A_.min, [yname[1]], ["sY1"], -1.0, A_.max)
         act(T.fT[:], T.pS[:, 0:128], AF.Sign, ["pS:a"], ["fT"], bias=-5.5)
-        act(T.lsT[:], T.pS[:, 128:256], AF.Sign, ["pS:b"], ["lsT"], bias=128.0)
-        act(T.nlf[:], T.pS[:, 128:256], AF.Sign, ["pS:b"], ["nlf"], bias=5.5, scale=-1.0)
         weight = lambda l: (Id[2.0 ** (5 - l)], In(2 ** (5 - l)))
-        valB, xA, LA, xB, valA = T.pYA[:, 0:128], T.pYB[:, 0:128], T.pYB[:, 128:256], T.pT[:, 384:512], T.pS[:, 384:512]
-        lin(valB, yname[0], [(T.sY[:, l], weight(l)[0], ["sY0", "sY1", weight(l)[1]]) for l in range(6)]
-            + [(Id[64.0], T.fT[:], [In(64), "fT"])], final=False)
+        valB, xA, LA, xB, valA = T.pT[:, 256:384], T.pYB[:, 0:128], T.pYB[:, 128:256], T.pT[:, 384:512], T.pS[:, 384:512]
+        terms = [(T.sY[:, l], weight(l)[0], ["sY0", "sY1", weight(l)[1]]) for l in range(6)] + [(Id[64.0], T.fT[:], [In(64), "fT"])]
+        lin(valB, "pT:v", [(nlB, Id[-256.0], [knlB, In(-256)])] + terms)
         ts(T.xh[:], T.xs[:], 1, A_.arith_shift_right, ["xs"], ["xh"])
-        if t == 0:
-            consts_d()
         cp(Xt.indirect(T.offc[:]), T.xh[:], ["xh", "offc"], ["X"])
-        if last:
-            ts(T.orev[:], T.ioj[:, 0:8], 16.0, A_.mult, ["ioj", "col9"], ["orev"], col(9), A_.add)
-            cp(T.IdH[:], Id[1.0], [In(1)], ["IdH"])
+        ts(T.kT[:], valB, -64.5, A_.is_ge, ["pT:v"], ["kT"], 0.5, A_.subtract)
+        ts(T.nfT[:], valB, 0.0, A_.is_lt, ["pT:v"], ["nfT"], 0.5, A_.subtract)
 
         def yx_part(c, ps, key):
             for q in range(4):
@@ -560,19 +589,6 @@ def rank_program(g, core, T, topo):
         def yx_out(c, ps, key):
             act(T.yxo[:, 256 * c:256 * c + 256], ps, AF.Copy, [key], ["yxo%d" % c])
             dma("s", T.yx[:, 256 * c:256 * c + 256], T.yxo[:, 256 * c:256 * c + 256], "stx%d" % c, ["yxo%d" % c], [])
-
-        def k_sum():
-            lin(valB, yname[0], [(nlB, Id[-256.0], [knlB, In(-256)])], first=False)
-
-        def k_flags():
-            ts(T.kT[:], valB, -64.5, A_.is_ge, [yname[0]], ["kT"], 0.5, A_.subtract)
-            ts(T.nfT[:], valB, 0.0, A_.is_lt, [yname[0]], ["nfT"], 0.5, A_.subtract)
-
-        def a_sum():
-            lin(xA, yname[1], ranks(T.lsT[:], "lsT") + [Bk(T.kT[:], "kT", 1), Bk(T.nfT[:], "nfT", 1)])
-
-        def b_sum():
-            lin(xB, "pT:x", ranks(T.kT[:], "kT"), final=False)
 
         def cut(i, L, j, s, v):
             ix = [slice(None), slice(8 * L + 4 * j, 8 * L + 4 * j + 4)] + [slice(None)] * 4
@@ -594,8 +610,7 @@ def rank_program(g, core, T, topo):
                                        [n + "4_%d" % j, kn], wkeys(L, 0, j))] + [stage(s) for s in range(4)]
 
         a_steps = steps(0, "a", T.pYB, 0, yname[1], 0.5, 47.0, 128, "pH:A", T.a3, T.a4) + [
-            lambda j, a, b: tt(T.a1[:, a:b], T.W0[:, 4 * j:4 * j + 4], T.pYB[:, 128 + a:128 + b], A_.min, wkeys(0, 0, j) + ["pYB:l"], ["a1_%d" % j]),
-            lambda j, a, b: tt(T.a1[:, a:b], T.a1[:, a:b], H(a, b), A_.max, ["a1_%d" % j, "pH:m1_%d" % j], ["a1_%d" % j]),
+            lambda j, a, b: tt(T.a1[:, a:b], T.W0[:, 4 * j:4 * j + 4], T.pKB[:, a:b], A_.max, wkeys(0, 0, j) + [kname[1]], ["a1_%d" % j]),
             lambda j, a, b: tt(H(a, b), T.a1[:, a:b], T.pKA[:, a:b], A_.min, ["a1_%d" % j, kname[0]], ["pH:m1_%d" % j])]
         b_steps = steps(1, "e", T.pT, 384, "pT:x", 1.0, 15.5, 256, "pH:B", T.e3, T.e4)
 
@@ -604,60 +619,50 @@ def rank_program(g, core, T, topo):
                 for x in parts:
                     fn(*x)
 
-        yx_early = [(0, T.pYB[:, 256:512], "pYB:x")][:YX0] if last else []
-        for x in yx_early:
-            yx_part(*x)
-        if K_EARLY:
-            k_sum()
-            k_flags()
-        if K_EARLY == 1:
-            a_sum()
-
-        act(T.y0[:], T.yb[:, 0:2048].indirect(offb), AF.Copy, ["yb", "yb2", koffb], ["y0"])
+        act(T.y0[:], T.yb[:, 0:2048].indirect(offb), AF.Copy, ["yb0", "yb1", "yb2", koffb], ["y0"])
+        act(T.lsT[:], T.pS[:, 128:256], AF.Sign, ["pS:b"], ["lsT"], bias=128.0)
+        act(T.nlf[:], T.pS[:, 128:256], AF.Sign, ["pS:b"], ["nlf"], bias=5.5, scale=-1.0)
         for b in range(3):
-            mm(KB_[b][:, 0:256], T.y0[:], blk(T.Wn, b, 256), False, True, ["y0", "Wn"], [kname[b]])
-        if K_EARLY == 2:
-            a_sum()
-        if K_EARLY:
-            run(a_steps[:EARLY])
-            b_sum()
-        else:
-            k_sum()
-        lin(T.pYA[:, 256:384], "pYA:z", [(Id[1.0], T.Zb[:], ["Zb"]), (Id[-1.0], T.y0[:], ["y0", In(-1)])])
+            mm(KB_[b][:, 0:256], T.y0[:], blk(T.Wn, b, 256), False, True, ["y0", "Wn%d" % b], [kname[b]])
         act(blk(T.sX, 1, 256), T.pKB[:, 0:256], AF.Sign, [kname[1]], ["sX1"])
         for b in (0, 2):
             ts(blk(T.sX, b, 256), KB_[b][:, 0:256], 1.0, A_.min, [kname[b]], ["sX%d" % b], -1.0, A_.max)
-        if not K_EARLY:
-            k_flags()
+        lin(xA, yname[1], [(T.lsT[:], T.nLin[:], ["lsT", "nLin"]), Bk(T.kT[:], "kT", 1), Bk(T.nfT[:], "nfT", 1)])
+        lin(xB, "pT:x", [(T.kT[:], T.nLin[:], ["kT", "nLin"])], final=False)
         lin(valA, "pS:d", [(Id[-256.0], T.nlf[:], [In(-256), "nlf"])]
             + [(blk(T.sX, l), weight(l)[0], ["sX%d" % (l // 2), weight(l)[1]]) for l in range(6)])
+        lin(T.pYA[:, 256:384], "pYA:z", [(Id[1.0], T.Zb[:], ["Zb"]), (Id[-1.0], T.y0[:], ["y0", In(-1)])])
         if last:
             act(T.Zf[:], T.pYA[:, 256:384], AF.Abs, ["pYA:z"], ["Zf"])
             dma("s", T.yz[:], T.Zf[:], "stz", ["Zf"], [])
         else:
             act(T.Zb[:], T.pYA[:, 256:384], AF.Abs, ["pYA:z"], ["Zb"])
-        if not K_EARLY:
-            b_sum()
-            a_sum()
-        if not last:
-            u0()
-        run(a_steps[EARLY if K_EARLY else 0:max(EARLY, 1)])
-        lin(LA, "pYB:l", [Cc(0), Bk(T.kT[:], "kT", 3), Bk(T.nfT[:], "nfT", 3), Bk(T.lsT[:], "lsT", 2), Bk(T.nlf[:], "nlf", 2)], final=False)
-        run(a_steps[max(EARLY, 1):LEAD])
-        act(T.gT[:], valA, AF.Sign, ["pS:d"], ["gT"], bias=-255.5)
+        if t == 0:
+            count()
+        for n in range(GT):
+            run(a_steps[n:n + 1])
+            if t == 0 and n < 2:
+                consts_g(n)
+        ts(T.gT[:], valA, 255.5, A_.is_ge, ["pS:d"], ["gT"], 0.5, A_.subtract)
+        run(a_steps[GT:LEAD])
         lin(xB, "pT:x", [Bk(T.gT[:], "gT", 0)], first=False)
 
-        lin(LA, "pYB:l", [Bk(T.gT[:], "gT", 2)], first=False)
-        lin(T.pS[:, 0:128], "pS:a", [Cc(1), Bk(T.kT[:], "kT", 2), Bk(T.gT[:], "gT", 2)])
+        lin(LA, "pYB:l", [Cc(0), Bk(T.kT[:], "kT", 3), Bk(T.lsT[:], "lsT", 2), Bk(T.nlf[:], "nlf", 2), Bk(T.gT[:], "gT", 3)])
+        lin(T.pS[:, 0:128], "pS:a", [Cc(1), Bk(T.kT[:], "kT", 2), Bk(T.gT[:], "gT", 3)])
+        act(T.sT[:], LA, AF.Sign, ["pYB:l"], ["sT"], scale=-1.0)
         act(T.ab[:], T.pS[:, 0:128], AF.Abs, ["pS:a"], ["ab"], scale=2.0)
+        lin(T.pKB[:, 0:128], kname[1], [(T.If[:], T.fil[:], ["If", "fil"]), (Id[8192.0], T.sT[:], [In(8192), "sT"])])
+        if not last:
+            u0()
+        rest = [(0, T.pU[:, 0:256], "pU:U"), (1, T.pYA[:, 0:256], yname[0]), (2, T.pS[:, 128:384], "pS:b"), (3, T.pYB[:, 256:512], "pYB:x")]
         if not last:
             u1()
+        else:
+            yx_part(*rest[0])
         lin(T.pKA[:, 0:128], kname[0], [Cc(2), Bk(T.kT[:], "kT", 4), (Id[1.0], T.ab[:], ["ab"])])
         if last:
-            for x in yx_early:
-                yx_out(*x)
-            rest = [(0, T.pU[:, 0:256], "pU:U"), (1, T.pKB[:, 0:256], kname[1]), (2, T.pYA[:, 0:256], yname[0]), (3, T.pS[:, 128:384], "pS:b")]
-            for x in rest[YX0:]:
+            yx_out(*rest[0])
+            for x in rest[1:]:
                 yx_part(*x)
                 yx_out(*x)
         else:
@@ -668,8 +673,8 @@ def rank_program(g, core, T, topo):
 
         for n in range(len(b_steps)):
             run(b_steps[n:n + 1])
-            run(a_steps[LEAD + n:LEAD + n + 1])
-        run(a_steps[LEAD + len(b_steps):])
+            for m in FILL[n]:
+                a_steps[m // 2](*parts[m % 2])
         An, kAn = blk(T.A, t + 1), allp("A%d" % (t + 1))
         for j, a, b in parts:
             tt(T.m2[:, a:b], T.W0[:, 8 + 4 * j:12 + 4 * j], H(a, b), A_.max, wkeys(1, 0, j) + ["pH:m1_%d" % j], ["m2_%d" % j])
@@ -678,10 +683,13 @@ def rank_program(g, core, T, topo):
         if not last:
             send(t + 1, An, blk(T.B, t + 1), "rn%d" % (t + 1), kAn)
         else:
-            ts(T.yaf[:], An.indirect(T.orev[:]), -2048.0, A_.add, kAn + ["orev"], ["yaf"])
-            mm(T.pT[:, 0:128], T.yaf[:], T.IdH[:], True, True, ["yaf", "IdH"], ["pT:a"])
-            ts(T.yao[:], T.pT[:, 0:128], 2048.0, A_.add, ["pT:a"], ["yao"])
-            dma("a", T.ya[:], T.yao[:], "sta", ["yao"], [])
+            ends = [(T.pT[0:64, 0:128], "pT:a", "a"), (T.pKA[0:64, 0:128], kname[0], "s")]
+            for j, a, b in parts:
+                ts(T.yaf[:, a:b], T.A[:, 128 * RO + a:128 * RO + b].indirect(T.orev[:, 0:4]), -2048.0, A_.add, [kAn[j], "orev"], ["yaf%d" % j])
+                mm(ends[j][0], T.yaf[:, a:b], T.IdH[:], True, True, ["yaf%d" % j, "IdH"], [ends[j][1]])
+            for j, a, b in parts:
+                ts(T.yao[0:64, 128 * j:128 * j + 128], ends[j][0], 2048.0, A_.add, [ends[j][1]], ["yao%d" % j])
+                dma(ends[j][2], T.ya[a:b, :], T.yao[0:64, 128 * j:128 * j + 128], "sta%d" % j, ["yao%d" % j], [])
 
     for s in sorted(total):
         wait("g", (s, total[s]))

from concourse.mybir import AluOpType, ActivationFunctionType

RO = 4
SHIFTS = (9, 14, 19, 24)
MAGIC = sum(1 << s for s in SHIFTS)
EMASK = (1 << 12) | (1 << 16) | (1 << 20) | (1 << 24)
TOP = float(1 << 24)
BIG = 2.0 ** 26
CUT = 64
YCUT = 112
SLOTS = (-1, -1, 2, 3, 5, 6)
SLOTS0 = (1, 1, 2, 3, 5, 6, 7)
REKEY = (3, 4)
GT = 3
GORD = "abcCAB"
COPY_ACT = (1, 2)
LEAD = 5
FILL = ((10,), (11,), (12,), (13,), (14, 15), (16, 17), ())
ORDER = [1, 0, 2, 3, 4, 5]


def _sb(n, d):
    return ("sbuf", [128, n], d)


F, BF, HF, I32, U16 = "float32", "bfloat16", "float16", "int32", "uint16"
CUBE = [128, 16, 2, 2, 2, 2]
SCRATCH = {
    "X": _sb(4112, BF), "xb": _sb(2048, BF), "yb": _sb(2048, BF),
    "am_i": _sb(128, I32), "am_f": _sb(128, F), "Zb": _sb(128, BF), "Zf": _sb(128, F), "w_i": _sb(4, I32),
    "cols": _sb(16, F), "coli": _sb(8, I32),
    "ioj": _sb(128, F), "iog": _sb(128, F), "tvec": _sb(128, F), "c0": _sb(128, F),
    "If": _sb(128, F), "Rf": _sb(128, F), "Is": _sb(128 * 12, BF), "sT": _sb(128, BF), "fil": _sb(128, F), "CQ": _sb(128, BF), "Cs": _sb(128 * 4, BF),
    "Blk": _sb(128, BF), "Wblk": _sb(128, BF), "Wblk2": _sb(128, BF), "mask": _sb(128, F), "maskS": _sb(128, F), "mask16": _sb(128, BF),
    "l1": _sb(128, BF), "l2": _sb(128, BF), "nLin": _sb(128, BF), "Bs": _sb(128 * 5, BF),
    "Sel": _sb(8, BF), "nSel": _sb(8, F), "Sel2": _sb(8, BF), "SelH": _sb(8, HF), "ones": _sb(128, BF), "c33": _sb(128, BF),
    "wv": _sb(48, F), "wg": _sb(48, F), "wa": _sb(48, F), "wb": _sb(48, F), "wc": _sb(48, F), "Wp": _sb(48, BF), "Wk": _sb(48, BF), "Kc": _sb(768, BF),
    "Wn": _sb(768, BF), "Wy": _sb(384, BF), "orep": _sb(48, U16), "orep8": _sb(24, U16),
    "oend": _sb(8, U16), "orev": _sb(8, U16), "Cf": _sb(128, F), "c1": _sb(128, F),
    "K32": _sb(4, F), "junk": _sb(128, F),
    "P1": _sb(128, F), "qp": _sb(128, BF), "offx": _sb(128, U16), "offy": _sb(128, U16),
    "q1": _sb(128, BF), "q2": _sb(128, BF), "r1": _sb(128, BF), "r2": _sb(128, BF),
    "Gu": _sb(128, BF), "offc": _sb(8, U16), "f2": _sb(128, I32), "f4": _sb(128, I32),
    "D": _sb(256, F), "I0": _sb(260, F), "I1": _sb(260, F), "Qr": _sb(128, F), "Hs": _sb(128, F),
    "G1": _sb(128, F), "G2": _sb(128, HF), "M": _sb(128, BF), "ge": _sb(128, BF), "y0": _sb(128, BF),
    "sX": _sb(768, BF), "sY": ("sbuf", [128, 6, 8, 2, 8], BF),
    "fT": _sb(128, BF), "lsT": _sb(128, BF), "nlf": _sb(128, BF), "kT": _sb(128, BF), "nfT": _sb(128, BF), "gT": _sb(128, BF),
    "ab": _sb(128, BF), "a1": _sb(128, F), "a3": _sb(128, I32), "a4": _sb(128, I32), "e3": _sb(128, I32), "e4": _sb(128, I32),
    "W0": ("sbuf", CUBE, F), "W1": ("sbuf", CUBE, F), "m2": _sb(128, I32),
    "xs": _sb(128, I32), "xh": _sb(128, I32),
    "yaf": _sb(128, HF), "IdH": _sb(128, HF), "yao": _sb(256, F), "yxo": _sb(1024, F),
    "A": _sb(128 * (RO + 1), I32), "B": _sb(128 * RO, I32),
    "nl": _sb(128 * RO, BF), "nlB": _sb(128 * RO, BF), "offm": _sb(16 * RO, U16), "offb": _sb(16 * RO, U16),
    "pKA": ("psum", [128, 512], F), "pKB": ("psum", [128, 512], F), "pYA": ("psum", [128, 512], F), "pYB": ("psum", [128, 512], F),
    "pH": ("psum", [128, 512], F), "pU": ("psum", [128, 512], F), "pT": ("psum", [128, 512], F), "pS": ("psum", [128, 512], F),
}
SEMAPHORES = (["cv", "ca", "cp", "cg", "ls", "ldx", "lda", "ldz", "ldw", "ldp", "sta0", "sta1", "stz", "stx0", "stx1", "stx2", "stx3"]
              + ["rn%d" % t for t in range(RO)] + ["rl%d" % t for t in range(RO)] + ["ro%d" % t for t in range(RO)])


def rank_program(g, core, T, topo):
    rank = T.rank_of(core)
    if rank is None:
        return
    N = len(T.cores)
    A_ = AluOpType
    AF = ActivationFunctionType
    Q = {"v": g.vector, "a": g.scalar, "p": g.tensor, "g": g, "s": g.sync}
    own = {"v": "cv", "a": "ca", "p": "cp", "g": "cg"}
    total = {}
    known = {e: {} for e in Q}
    clock = {}
    lastw, readers, bank = {}, {}, {}

    def wait(e, ev):
        s, n = ev
        if known[e].get(s, 0) >= n:
            return
        Q[e].wait_ge(T.sem[s], n)
        known[e][s] = n
        for s2, n2 in clock.get(ev, {}).items():
            if known[e].get(s2, 0) < n2:
                known[e][s2] = n2

    def op(e, fn, r, w, inc=True, sem=None, by=1):
        me = own.get(e) if sem is None else sem
        need = {}

        def add(ev, same_ok):
            if ev is None:
                return
            if ev[0] == me and sem is None and (same_ok or e == "p"):
                return
            if need.get(ev[0], 0) < ev[1]:
                need[ev[0]] = ev[1]
        for k in r:
            add(lastw.get(k), False)
        for k in w:
            add(lastw.get(k), False)
            for s, n in readers.get(k, {}).items():
                add((s, n), False)
        banks = set(k.split(":")[0] for k in list(r) + list(w) if ":" in k)
        for b in banks:
            for s, n in bank.get(b, {}).items():
                add((s, n), True)
        for s, n in sorted(need.items(), key=lambda x: x[0] == me):
            wait(e, (s, n))
        ins = fn()
        ev = (me, total.get(me, 0) + by)
        if inc:
            if ins is not None:
                ins.then_inc(T.sem[me], by)
            total[me] = ev[1]
            clock[ev] = dict(known[e])
        for k in r:
            readers.setdefault(k, {})[me] = ev[1]
        for k in w:
            lastw[k] = ev
            readers[k] = {}
        for b in banks:
            bank.setdefault(b, {})[me] = ev[1]

    V, S_, PE = g.vector, g.scalar, g.tensor

    def tt(out, a, b, o, r, w):
        op("v", lambda: V.tensor_tensor(out, a, b, o), r, w)

    def ts(out, a, s1, o1, r, w, s2=None, o2=None):
        if o2 is None:
            op("v", lambda: V.tensor_scalar(out, a, s1, None, o1), r, w)
        else:
            op("v", lambda: V.tensor_scalar(out, a, s1, s2, o1, o2), r, w)

    def cp(out, a, r, w):
        op("v", lambda: V.tensor_copy(out, a), r, w)

    def scan(out, a, b, o1, o2, r, w):
        op("v", lambda: V.tensor_tensor_scan(out, a, b, 0.0, o1, o2), r, w)

    def ms(out, c, w):
        op("v", lambda: V.memset(out, c), [], w)

    def act(out, a, f, r, w, bias=0.0, scale=1.0, acc=None):
        if acc is None:
            op("a", lambda: S_.activation(out, a, f, bias=bias, scale=scale), r, w)
        else:
            op("a", lambda: S_.activation(out, a, f, bias=bias, scale=scale, accum_out=acc), r, w)

    def mm(out, l, rh, st, sp, r, w, inc=True):
        op("p", lambda: PE.matmul(out, l, rh, st, sp), r, w, inc=inc)

    def lin(out, w, terms, first=True, final=True):
        for j, (l, rh, r) in enumerate(terms):
            end = j == len(terms) - 1
            mm(out, l, rh, first and j == 0, final and end, r, [w], inc=end)

    def iota(out, pat, base, cm, w, fl=True):
        if fl:
            op("g", lambda: g.iota(out, pat, base, cm, allow_small_or_imprecise_dtypes=True), [], w)
        else:
            op("g", lambda: g.iota(out, pat, base, cm), [], w)

    def dma(e, out, a, sem, r, w):
        op(e, lambda: Q[e].dma_start(out, a), r, w, sem=sem, by=16)

    def peer(t, sign):
        return T.cores[(rank + sign * (1 + t % (N - 1))) % N]

    def width(src, dst):
        return len(topo.engines(src, dst))

    def send(t, src, dst, sem, r):
        d = peer(t, 1)
        rid, pid = topo.addr(d, core)

        def fn():
            g.remote_dma(dst, src, T.sem[sem], T.sem.ls, pid, rid, topo.mask(core, d))
            return None
        op("g", fn, r, [], sem="ls", by=width(core, d))

    def landed(t, key, sem):
        n = width(peer(t, -1), core)
        total[sem] = n
        lastw[key] = (sem, n)

    def blk(buf, t, n=128):
        return buf[:, n * t:n * t + n]

    dma("s", T.w_i[:, 0:1], T.wt[:], "ldw", [], ["w_i"])
    dma("a", T.Zb[:], T.zv[:], "ldz", [], ["Zb"])
    dma("s", T.am_i[:], T.am[:], "lda", [], ["am_i"])
    dma("a", T.X[:, 4096:4112], T.xt[:, 0:16], "ldp", [], ["Xpad"])
    dma("s", T.X[:, 0:4096], T.xt[:], "ldx", [], ["X"])
    for t in range(RO):
        landed(t, "B%d" % t, "rn%d" % t)
        landed(t, "nlB%d" % t, "rl%d" % t)
        landed(t, "offb%d" % t, "ro%d" % t)

    col = lambda j: T.cols[:, j:j + 1]
    iota(T.coli[:, 0:1], [[0, 1]], 0, 1, ["coli0"], fl=False)
    iota(T.ioj[:], [[1, 128]], 0, 0, ["ioj"])
    iota(T.iog[:], [[1, 8], [0, 16]], 0, 0, ["iog"])
    iota(T.wv[:], [[-3, 6], [-16, 8]], 0, 1, ["wv"])
    iota(T.wg[:], [[0, 6], [1, 8]], 0, 0, ["wg"])
    iota(T.tvec[:], [[0, 8], [1, 16]], 0, 0, ["tvec"])
    iota(T.c1[:], [[0, 8], [-37, 16]], 37 * 15 + 12288 - (1 << 24), 0, ["c1"])
    iota(T.D[:, 0:256:2], [[0, 128]], 0, 0, ["D_0", "D_1"])
    iota(T.CQ[:], [[0, 128]], 62 * 1024, 0, ["CQ0"])

    U, Uu, Cst, Um = (blk(T.pU, j) for j in range(4))
    KB_, kname = [T.pKA, T.pKB, T.pU], ["pKA:k", "pKB:k", "pU:U"]
    YB_, yname = [T.pYA, T.pYB], ["pYA:k", "pYB:k"]
    LB, lname = [T.pKA, T.pKB, T.pYA], ["pKA:k", "pKB:k", "pYA:k"]
    SC = [1.0, -2048.0, -131072.0, 2.0, 4.0, 8.0, 16.0, 32.0, 64.0, -256.0, -1.0, 8192.0]
    Id = {x: blk(T.Is, j) for j, x in enumerate(SC)}
    In = lambda x: "I%d" % x
    BS = [-1.0, -2.0, BIG / 2, BIG, -BIG]
    Bk = lambda x, name, j: (x, blk(T.Bs, j), [name, "Bs%d" % j])
    Cc = lambda j: (Id[1.0], blk(T.Cs, j), [In(1), "Cs%d" % j])
    ones = T.ones[:]
    unit = lambda l: 2.0 ** (60 - 25 * l)
    KQ, KO = 129.5 - 2.0 ** -14, 68.0 * 2 ** 17 - 16

    ms(T.ones[:], 1.0, ["ones"])
    ms(T.I0[:, 1:260:130], 0.0, ["I0_0", "I0_1"])
    ms(T.I1[:, 1:260:130], 0.0, ["I1_0", "I1_1"])
    ms(T.offc[:], 0, ["offc"])
    for j, l in enumerate(ORDER):
        act(blk(T.Kc, j), ones, AF.Identity, ["ones"], ["Kc%d" % l], scale=-(TOP if l < 5 else 65536.0) * unit(l))
    ts(T.coli[:, 1:2], T.coli[:, 0:1], 15, A_.bitwise_and, ["coli0"], ["coli1"])
    ts(T.coli[:, 2:3], T.coli[:, 0:1], 4, A_.arith_shift_right, ["coli0"], ["coli2"])
    ms(T.K32[:, 0:1], KO, ["K32"])
    ms(T.K32[:, 1:2], KQ, ["Kq"])
    cp(T.cols[:, 0:3], T.coli[:, 0:3], ["coli0", "coli1", "coli2"], ["cols"])
    ms(T.c33[0:64, :], 129.0 * 32, ["c33a"])
    ms(T.c33[64:128, :], 33.0 / 64, ["c33b"])
    ms(T.offm[:], 0, ["offm%d" % t for t in range(RO)])
    ts(col(3), col(1), -2.0, A_.mult, ["cols"], ["col3a"], 15.0, A_.add)
    ts(T.If[:], T.ioj[:], col(0), A_.is_equal, ["ioj", "cols"], ["If"])
    tt(col(4), col(3), col(0), A_.add, ["col3a", "cols"], ["col4"])
    ts(T.Blk[:], T.iog[:], col(2), A_.is_equal, ["iog", "cols"], ["Blk"])
    ts(T.Rf[:], T.ioj[:], col(4), A_.is_equal, ["ioj", "col4"], ["Rf"])
    ts(T.wa[:], T.wv[:], 0.0, A_.is_equal, ["wv"], ["wa"], 65536.0, A_.mult)
    ts(T.wb[:], T.wv[:], 1.0, A_.is_equal, ["wv"], ["wb"], 256.0, A_.mult)
    ts(T.wc[:], T.wv[:], 2.0, A_.is_equal, ["wv"], ["wc"])

    for x in SC[:5]:
        act(Id[x], T.If[:], AF.Identity, ["If"], [In(x)], scale=x)

    tt(T.Wblk[:], T.w_i[:, 0:1].indirect(T.offc[:]), T.Blk[:], A_.mult, ["w_i", "offc", "Blk"], ["Wblk"])
    cp(T.am_f[:], T.am_i[:], ["am_i"], ["am_f"])
    tt(T.wa[:], T.wa[:], T.wb[:], A_.add, ["wa", "wb"], ["wa"])
    ts(T.Wblk2[:], T.Wblk[:], 2.0, A_.mult, ["Wblk"], ["Wblk2"])
    ts(T.wg[:], T.wg[:], col(2), A_.is_equal, ["wg", "cols"], ["wg"])
    ts(col(7), col(1), 8.0, A_.is_ge, ["cols"], ["col7"])
    tt(T.wa[:], T.wa[:], T.wc[:], A_.add, ["wa", "wc"], ["wa"])
    ts(T.orep8[:], T.ioj[:, 0:24], 2.0, A_.mult, ["ioj", "col7"], ["orep8"], col(7), A_.add)
    ts(T.orep[:], T.ioj[:, 0:48], 1.0, A_.mult, ["ioj"], ["orep"])
    tt(T.Wp[:], T.wa[:], T.wg[:], A_.mult, ["wa", "wg"], ["Wp"])

    def level_weights(a, b):
        for j in range(a, b):
            l = ORDER[j]
            act(T.Wk[:, 8 * j:8 * j + 8], T.Wp[:, 8 * l:8 * l + 8], AF.Identity, ["Wp"], ["Wk%d" % j], scale=unit(l) / (1 if l < 5 else 512))

    def init_keys():
        for b in range(3):
            mm(LB[b][:, 1:512:2], Id[1.0], T.Kc[:, 256 * b:256 * b + 256], True, False, [In(1)] + ["Kc%d" % l for l in range(6)], [lname[b]], inc=False)
        mm(T.pYA[:, 257:512:2], Id[1.0], blk(T.Cs, 3), False, False, ["Cs3"], [lname[2]], inc=False)

    zw, qq = (T.Zb[:], T.Wblk[:], ["Zb", "Wblk"]), (Id[1.0], T.q2[:], [In(1), "q2"])

    def u0():
        lin(T.pYA[:, 256:384], "pYA:z", [zw])

    def u1():
        act(T.q1[:], T.pYA[:, 256:384], AF.Identity, ["pYA:z"], ["q1"], scale=2.0 ** -10, bias=128.5 + 2.0 ** -11)
        act(T.q2[:], T.q1[:], AF.Identity, ["q1"], ["q2"], scale=-1024.0, bias=129.0 * 1024.0)

    def u2():
        lin(U, "pU:U", [(T.Zb[:], T.Wblk2[:], ["Zb", "Wblk2"]), (ones, T.c33[:], ["ones", "c33a", "c33b"]),
                        (Id[-2048.0], T.q1[:], [In(-2048), "q1"])])

    def u2b():
        lin(Uu, "pU:V", [zw, qq])

    def u3():
        act(T.r1[:], Uu, AF.Identity, ["pU:V"], ["r1"], scale=2.0 ** -5, bias=128.5 + 2.0 ** -6)
        act(T.r2[:], T.r1[:], AF.Identity, ["r1"], ["r2"], scale=-32.0, bias=129.0 * 32.0)

    def u4():
        lin(Um, "pU:m", [zw, qq, (Id[1.0], T.r2[:], [In(1), "r2"])])
        lin(Cst, "pU:C", [zw, qq, (T.If[:], T.Cf[:], ["If", "Cf"])])

    lin(T.pYB[:, 0:128], "pYB:k", [(T.Wblk[:], T.Zb[:], ["Zb", "Wblk"])])
    mm(T.pT[:, 0:128], T.am_f[:], T.Rf[:], True, True, ["am_f", "Rf"], ["pT:a"])
    act(T.r1[:], T.pYB[:, 0:128], AF.Identity, ["pYB:k"], ["r1"], scale=2.0 ** -10, bias=128.5 + 2.0 ** -11)
    mm(T.pS[:, 0:128], T.Rf[:], T.am_f[:], True, True, ["am_f", "Rf"], ["pS:a"])
    level_weights(0, 3)
    u0()
    lin(T.pYB[:, 128:256], "pYB:l", [(T.Wblk2[:], T.Zb[:], ["Zb", "Wblk2"]), (ones, T.c33[:], ["ones", "c33a", "c33b"]),
                                     (Id[-2048.0], T.r1[:], [In(-2048), "r1"])])
    u1()
    for j in (1, 2, 3, 4):
        ts(blk(T.Bs, j), T.Blk[:], BS[j], A_.mult, ["Blk"], ["Bs%d" % j])
    cp(blk(T.A, 0), T.pT[:, 0:128], ["pT:a"], ["A0_0", "A0_1"])
    send(0, blk(T.A, 0), blk(T.B, 0), "rn0", ["A0_0", "A0_1"])
    cp(T.P1[:], T.pS[:, 0:128], ["pS:a"], ["P1_0", "P1_1"])
    for x in SC[7:]:
        iota(Id[x], [[0, 128]], int(x), 0, [In(x)])
        op("g", lambda x=x: g.affine_select(Id[x], Id[x], [[-1, 128]], A_.is_equal, 0.0, 0, 1), [In(x)], [In(x)])
    op("g", lambda: g.affine_select(T.l1[:], T.Blk[:], [[-1, 128]], A_.is_gt, 0.0, 0, 1), ["Blk"], ["l1"])
    lanes = [(1, CUT, 128), (0, 0, CUT)]
    for j, a, b in lanes:
        tt(T.e3[:, a:b], T.P1[:, a:b], T.pYB[:, 128 + a:128 + b], A_.mult, ["P1_0", "P1_1", "pYB:l"], ["e3_%d" % j])
    ts(blk(T.Cs, 3), T.tvec[:], 64.0, A_.add, ["tvec"], ["Cs3"], unit(5), A_.mult)
    for j, a, b in lanes:
        ts(T.e4[:, a:b], T.e3[:, a:b], 5, A_.arith_shift_right, ["e3_%d" % j], ["e4_%d" % j], 4095, A_.bitwise_and)
    ts(Id[8.0], Id[1.0], 8.0, A_.mult, [In(1)], [In(8)])
    for j, a, b in lanes:
        cp(T.offx[:, a:b], T.e4[:, a:b], ["e4_%d" % j], ["offx%d" % j])
    ts(T.a3[:], T.tvec[:], float(MAGIC), A_.mult, ["tvec"], ["a3_0", "a3_1"])
    ts(Id[16.0], Id[1.0], 16.0, A_.mult, [In(1)], [In(16)])
    u2()
    u2b()
    level_weights(3, 6)

    def consts_a():
        ts(T.mask[:], T.tvec[:], col(1), A_.is_equal, ["tvec", "cols"], ["mask"])
        ts(T.Sel[:], T.ioj[:, 0:8], col(2), A_.is_equal, ["ioj", "cols"], ["Sel"])
        ts(T.a4[:], T.a3[:], EMASK, A_.bitwise_and, ["a3_0", "a3_1"], ["a4_0", "a4_1"])
        tt(T.f2[:], blk(T.A, 0), Uu, A_.mult, ["A0_0", "A0_1", "pU:V"], ["f2"])

    def consts_b():
        act(col(6), col(0), AF.Identity, ["cols"], ["col6"], scale=16.0)
        act(T.l2[:], T.If[:], AF.Identity, ["If", "cols"], ["l2"], scale=col(1))
        act(blk(T.Bs, 0), T.Blk[:], AF.Identity, ["Blk"], ["Bs0"], scale=BS[0])
        u3()
        act(T.Sel2[:], T.Sel[:], AF.Identity, ["Sel"], ["Sel2"], scale=2.0)
        act(T.mask16[:], T.mask[:], AF.Identity, ["mask", "col6"], ["mask16"], scale=col(6))
        act(T.maskS[:], T.mask[:], AF.Identity, ["mask"], ["maskS"], scale=-1.0 / unit(5))
        act(T.nSel[:], T.Sel[:], AF.Identity, ["Sel"], ["nSel"], scale=-1.0)
        act(T.Wy[:], T.Wp[:].indirect(T.orep8[:]), AF.Identity, ["Wp", "orep8"], ["Wy"], scale=-1.0)
        minus(0)

    def minus(b):
        act(blk(T.Wn, b, 256), T.Wp[:].indirect(blk(T.orep, b, 16)), AF.Identity, ["Wp", "orep"], ["Wn%d" % b], scale=-1.0)

    def consts_c():
        ts(T.c0[:], T.tvec[:], 0.5, A_.is_lt, ["tvec"], ["c0"], -2.0 ** 88, A_.mult)
        tt(T.Cf[:], T.a4[:], T.c1[:], A_.add, ["a4_0", "a4_1", "c1"], ["Cf"])

    def consts_e():
        ts(T.oend[:], T.ioj[:, 0:8], 16.0, A_.mult, ["ioj"], ["oend"], 15.0, A_.add)
        cp(T.SelH[:], T.Sel[:], ["Sel"], ["SelH"])

    def consts_f():
        tt(T.nLin[:], T.l2[:], T.l1[:], A_.subtract, ["l1", "l2"], ["nLin"])
        ms(blk(T.Cs, 2), -7.5 * BIG, ["Cs2"])
        ts(T.f4[:], T.f2[:], 5, A_.arith_shift_right, ["f2"], ["f4"], 4095, A_.bitwise_and)

    def consts_g(n):
        ts(blk(T.Cs, n), T.tvec[:], [0.5, -3.5][n], A_.add, ["tvec"], ["Cs%d" % n], BIG, A_.mult)

    parts = [(j, 64 * j, 64 * j + 64) for j in range(2)]
    allp = lambda n: [n + "_0", n + "_1"]
    H = lambda a, b: T.pH[:, a:b]
    WW = [T.W0, T.W1]
    II = [T.I0, T.I1]
    Xw, Xt = T.X[:, 0:4112], T.X[:, 0:4096]

    for t in range(RO):
        last = t == RO - 1
        A, B = blk(T.A, t), blk(T.B, t)
        kA, kB = allp("A%d" % t), "B%d" % t
        nl, nlB = blk(T.nl, t), blk(T.nlB, t)
        knl, knlB = allp("nl%d" % t), "nlB%d" % t
        offm, offb = T.offm[:, 16 * t:16 * t + 8], T.offb[:, 16 * t:16 * t + 8]
        koffm, koffb = "offm%d" % t, "offb%d" % t

        def turn(ps, key, a, b):
            lin(ps, key, [(T.P1[:], T.If[:, a:b], allp("P1") + ["If"]), (ones, T.CQ[:, a:b], ["ones", "CQ0"])], final=False)

        def unwrap(ps, key, a, b):
            lin(ps, key, [(T.qp[:], T.Is[:, 256 + a:256 + b], allp("qp") + [In(SC[2])])], first=False)

        def offsets(out, okey, ps, key):
            ts(out, ps, T.K32[:, 0:1], A_.add, [key, "K32"], [okey], 2.0 ** -5 + 2.0 ** -25, A_.mult)

        if t > 0:
            for j, a, b in parts:
                tt(T.P1[:, a:b], T.A[:, 128 * t + a:128 * t + b], T.pU[:, a:b], A_.mult, [kA[j], "pU:U"], ["P1_%d" % j])
            turn(T.pT[:, 0:128 - CUT], "pT:a", CUT, 128)
            turn(T.pS[:, 0:CUT], "pS:a", 0, CUT)
            for j, a, b in parts:
                ts(T.qp[:, a:b], T.P1[:, a:b], 2.0 ** -17, A_.mult, ["P1_%d" % j, "Kq"], ["qp_%d" % j], T.K32[:, 1:2], A_.add)
            unwrap(T.pT[:, 0:128 - CUT], "pT:a", CUT, 128)
            tt(T.f2[:], A, Uu, A_.mult, kA + ["pU:V"], ["f2"])
            unwrap(T.pS[:, 0:CUT], "pS:a", 0, CUT)
            ts(T.f4[:], T.f2[:], 5, A_.arith_shift_right, ["f2"], ["f4"], 4095, A_.bitwise_and)
        init_keys()
        if t > 0:
            u4()
            offsets(T.offx[:, CUT:128], "offx1", T.pT[:, 0:128 - CUT], "pT:a")
            offsets(T.offx[:, 0:CUT], "offx0", T.pS[:, 0:CUT], "pS:a")
        act(T.xb[:, 16 * CUT:2048], Xw.indirect(T.offx[:, CUT:128]), AF.Copy, ["X", "Xpad", "offx1"], ["xb1"])
        cp(T.xb[:, 0:16 * CUT], Xw.indirect(T.offx[:, 0:CUT]), ["X", "Xpad", "offx0"], ["xb0"])
        if t == 0:
            consts_a()
            consts_c()
            consts_b()

        def keys(b):
            for j in range(16):
                mm(LB[b][:, 1 + 2 * j:2 + 2 * j + 480:32], T.xb[:, j:2048:16], T.Wk[:, 16 * b:16 * b + 16], False, j == 15,
                   ["xb0", "xb1", "Wk%d" % (2 * b), "Wk%d" % (2 * b + 1)], [lname[b]], inc=j == 15)

        def rekey(b):
            for j in range(16):
                mm(KB_[b][:, j:j + 241:16], T.xb[:, j:2048:16], T.Wp[:, 16 * b:16 * b + 16], j == 0, False, ["xb0", "xb1", "Wp"], [kname[b]], inc=False)

        for b in range(3):
            keys(b)

        def from_u():
            tt(T.Gu[:], Um, T.mask[:], A_.mult, ["pU:m", "mask"], ["Gu"])
            tt(T.fil[:], T.f4[:], Cst, A_.add, ["f4", "pU:C"], ["fil"])

        def column():
            lin(T.pS[:, 128:136], "pS:b", [(T.mask16[:], T.Sel2[:], ["mask16", "Sel2"]), (T.Gu[:], T.Sel[:], ["Gu", "Sel"])])

        def b1(j, a, b):
            tt(T.P1[:, a:b], T.B[:, 128 * t + a:128 * t + b], T.pU[:, a:b], A_.mult, [kB, "pU:U"], ["P1_%d" % j])
            if j:
                turn(T.pT[:, 0:128], "pT:a", 0, 128)

        def b2(j, a, b):
            ts(T.qp[:, a:b], T.P1[:, a:b], 2.0 ** -17, A_.mult, ["P1_%d" % j, "Kq"], ["qp_%d" % j], T.K32[:, 1:2], A_.add)
            if j:
                unwrap(T.pT[:, 0:128], "pT:a", 0, 128)
                if t > 0:
                    column()

        def b3(j, a, b):
            offsets(T.offy[:, a:b], "offy%d" % j, T.pT[:, a:b], "pT:a")
            b = min(b, YCUT if t else 128)
            act(T.yb[:, 16 * a:16 * b], Xw.indirect(T.offy[:, a:b]), AF.Copy, ["X", "Xpad", "offy%d" % j], ["yb%d" % j])
            if j:
                mm(T.pT[:, 128:136], T.mask16[:], T.Sel[:], True, False, ["mask16", "Sel"], ["pT:m"], inc=False)

        if t > 0:
            from_u()
            ts(H(128, 256), A, 12288.0 - TOP, A_.add, kA, ["pH:A"])
        if t == 0:
            consts_e()
        if t == 1:
            ts(col(9), col(1), -1.0, A_.mult, ["cols"], ["col9"], 15.0, A_.add)
            cp(T.IdH[:], Id[1.0], [In(1)], ["IdH"])
        if t == 2:
            ts(T.orev[:], T.ioj[:, 0:8], 16.0, A_.mult, ["ioj", "col9"], ["orev"], col(9), A_.add)
        pieces = [(fn, x) for fn in (b1, b2, b3) for x in parts]
        slots = list(zip(SLOTS if t else SLOTS0, pieces + [(u4, ())]))

        def slot(n):
            for m, (fn, x) in slots:
                if m == n:
                    fn(*x)

        slot(-1)

        def region(l, a, b, first, step):
            c = 256 * (ORDER.index(l) % 2) + 2 * a + first
            return LB[l // 2][:, c:c + 2 * (b - a) - (step - 1):step]

        def dcol(l, j, a, b, shift):
            if l == 0:
                return region(0, a, b, 1 - 2 * shift, 2), lname[0]
            if l == 5:
                return T.pH[:, 257 + 2 * a:256 + 2 * b:2], "pH:I_%d" % j
            c = 130 * j + 3 - 2 * shift
            return II[l % 2][:, c:c + 127:2], "I%d_%d" % (l % 2, j)

        for l in range(6):
            if l > 0:
                for j, a, b in parts:
                    hk = lname[l // 2] + "h%d_%d" % (l, j)
                    out = II[l % 2][:, 130 * j + 2:130 * j + 130] if l < 5 else H(256 + 2 * a, 256 + 2 * b)
                    scan(out, T.D[:, 2 * a:2 * b], region(l, a, b, 0, 1), A_.subtract, A_.min,
                         ["D_%d" % j, hk, lname[l // 2]], [dcol(l, j, a, b, 0)[1]] + ["pH:B"] * (l == 5 and j == 0))
                    if l > 1:
                        d, kd = dcol(l - 1, j, a, b, 0)
                    else:
                        d, kd = T.D[:, 2 * a + 1:2 * b:2], "D_%d" % j
                    tt(T.Qr[:, a:b], region(l, a, b, 0, 2), d, A_.subtract, [hk, kd], ["Q_%d" % j])
            if l in REKEY:
                rekey(REKEY.index(l))
            for j, a, b in parts:
                q, kq = (T.Qr[:, a:b], "Q_%d" % j) if l else (T.c0[:, a:b], "c0")
                if l == 5:
                    d, kd = dcol(l, j, a, b, 0)
                    scan(T.Hs[:, a:b], q, d, A_.min, A_.max, [kd, kq], ["Hs_%d" % j])
                    continue
                d, kd = dcol(l, j, a, b, 1)
                if l in COPY_ACT and t > 0:
                    act(T.D[:, 2 * a + 1:2 * b:2], dcol(l, j, a, b, 0)[0], AF.Copy, [kd], ["D_%d" % j])
                else:
                    cp(T.D[:, 2 * a + 1:2 * b:2], dcol(l, j, a, b, 0)[0], [kd], ["D_%d" % j])
                scan(region(l + 1, a, b, 0, 2), d, q, A_.max, A_.min, [kd, kq], [lname[(l + 1) // 2] + "h%d_%d" % (l + 1, j)])
                slot(2 * l + j)

        def dead(j, a, b):
            d, kd = dcol(5, j, a, b, 0)
            tt(T.nl[:, 128 * t + a:128 * t + b], d, T.Hs[:, a:b], A_.is_lt, [kd, "Hs_%d" % j], [knl[j]])

        def ends(G, n, j, a, b):
            tt(G[:, a:b], T.Hs[:, a:b].indirect(T.oend[:, 0:4]), T.maskS[:, a:b], A_.mult, ["Hs_%d" % j, "oend", "maskS"], [n + "_%d" % j])

        if t > 0:
            cp(T.offc[:], T.pS[:, 128:136], ["pS:b"], ["offc"])
        for c in GORD:
            x = parts[c in "ABC"]
            if c in "aA":
                ends(T.G1, "G1", *x)
            elif c in "bB":
                ends(T.G2, "G2", *x)
            else:
                dead(*x)
        send(t, nl, nlB, "rl%d" % t, knl)
        lin(T.pT[:, 128:136], "pT:m", [(T.G1[:], T.nSel[:], allp("G1") + ["nSel"]), (T.G2[:], T.SelH[:], allp("G2") + ["SelH"])], first=False)
        if t == 0:
            tt(T.Gu[:], Um, T.mask[:], A_.mult, ["pU:m", "mask"], ["Gu"])
            column()
            consts_f()
        else:
            cp(T.yb[:, 16 * YCUT:2048], Xw.indirect(T.offy[:, YCUT:128]), ["X", "Xpad", "offy1"], ["yb2"])
        if 0 < t < RO - 1:
            lin(Cst, "pU:C", [(ones, nl, ["ones"] + knl)])
        for j in range(16):
            mm(YB_[j // 8][:, j % 8:j % 8 + 377:8], T.yb[:, j:2048:16], T.Wp[:], j % 8 == 0, False,
               ["yb0", "yb1", "yb2", "Wp"], [yname[j // 8]], inc=False)
        cp(offm, T.pT[:, 128:136], ["pT:m"], [koffm])
        send(t, T.offm[:, 16 * t:16 * t + 16], T.offb[:, 16 * t:16 * t + 16], "ro%d" % t, [koffm])
        act(T.M[:, 64:128], T.xb[:, 0:2048].indirect(T.offm[:, 16 * t + 4:16 * t + 8]), AF.Copy, ["xb0", "xb1", koffm], ["M_1"])
        cp(T.M[:, 0:64], T.xb[:, 0:2048].indirect(T.offm[:, 16 * t:16 * t + 4]), ["xb0", "xb1", koffm], ["M_0"])

        def count():
            act(T.junk[:], Cst, AF.Identity, ["pU:C"], ["junk", "K"], scale=32.0, acc=T.K32[:, 2:3])
            act(T.K32[:, 0:1], T.K32[:, 2:3], AF.Identity, ["K"], ["K32"], bias=KO)
            act(T.K32[:, 1:2], T.K32[:, 2:3], AF.Identity, ["K"], ["Kq"], scale=2.0 ** -17, bias=KQ)

        if t == 0:
            minus(1)
            minus(2)
        elif not last:
            count()
        ts(H(256, 384), B, -TOP, A_.add, [kB], ["pH:B", "pH:I_0"])
        if t == 0:
            cp(T.offc[:], T.pS[:, 128:136], ["pS:b"], ["offc"])
            tt(T.fil[:], T.f4[:], Cst, A_.add, ["f4", "pU:C"], ["fil"])
        tt(T.ge[:], T.Zb[:], T.M[:], A_.is_ge, ["Zb"] + allp("M"), ["ge"])
        tt(T.xs[:], Xt.indirect(T.offc[:]), T.M[:], A_.add, ["X", "offc"] + allp("M"), ["xs"])
        if t == 0:
            ts(H(128, 256), A, 12288.0 - TOP, A_.add, kA, ["pH:A"])

        cnt = (T.Blk[:], T.ge[:], ["ge", "Blk"])
        for b in range(2):
            mm(YB_[b][:, 0:384], T.M[:], T.Wy[:], False, True, allp("M") + ["Wy"], [yname[b]])
        lin(T.pS[:, 0:128], "pS:a", [cnt])
        lin(T.pS[:, 128:256], "pS:b", [(nl, Id[-256.0], knl + [In(-256)]), cnt])
        if t == 0:
            lin(Cst, "pU:C", [(ones, nl, ["ones"] + knl)])
        rekey(2)
        act(T.sY[:, :, :, 0], T.pYA[:, 0:384], AF.Sign, [yname[0]], ["sY0"])
        ts(T.sY[:, :, :, 1], T.pYB[:, 0:384], 1.0, A_.min, [yname[1]], ["sY1"], -1.0, A_.max)
        act(T.fT[:], T.pS[:, 0:128], AF.Sign, ["pS:a"], ["fT"], bias=-5.5)
        weight = lambda l: (Id[2.0 ** (5 - l)], In(2 ** (5 - l)))
        valB, xA, LA, xB, valA = T.pT[:, 256:384], T.pYB[:, 0:128], T.pYB[:, 128:256], T.pT[:, 384:512], T.pS[:, 384:512]
        terms = [(T.sY[:, l], weight(l)[0], ["sY0", "sY1", weight(l)[1]]) for l in range(6)] + [(Id[64.0], T.fT[:], [In(64), "fT"])]
        lin(valB, "pT:v", [(nlB, Id[-256.0], [knlB, In(-256)])] + terms)
        ts(T.xh[:], T.xs[:], 1, A_.arith_shift_right, ["xs"], ["xh"])
        cp(Xt.indirect(T.offc[:]), T.xh[:], ["xh", "offc"], ["X"])
        ts(T.kT[:], valB, -64.5, A_.is_ge, ["pT:v"], ["kT"], 0.5, A_.subtract)
        ts(T.nfT[:], valB, 0.0, A_.is_lt, ["pT:v"], ["nfT"], 0.5, A_.subtract)

        def yx_part(c, ps, key):
            for q in range(4):
                mm(ps, Id[1.0], T.X[:, 1024 * q + 256 * c:1024 * q + 256 * c + 256], q == 0, q == 3, ["X"], [key], inc=q == 3)

        def yx_out(c, ps, key):
            act(T.yxo[:, 256 * c:256 * c + 256], ps, AF.Copy, [key], ["yxo%d" % c])
            dma("s", T.yx[:, 256 * c:256 * c + 256], T.yxo[:, 256 * c:256 * c + 256], "stx%d" % c, ["yxo%d" % c], [])

        def cut(i, L, j, s, v):
            ix = [slice(None), slice(8 * L + 4 * j, 8 * L + 4 * j + 4)] + [slice(None)] * 4
            ix[5 - s] = v
            return WW[i][tuple(ix)]

        wkeys = lambda L, i, j: ["W%d%d%d_0" % (L, i, j), "W%d%d%d_1" % (L, i, j)]

        def steps(L, n, ps, c, kx, scale, shift, cn, kn, e3, e4):
            def stage(s):
                def fn(j, a, b):
                    for v, alu in enumerate([A_.min, A_.max]):
                        tt(cut(1 - s % 2, L, j, s, v), cut(s % 2, L, j, s, 0), cut(s % 2, L, j, s, 1), alu,
                           wkeys(L, s % 2, j), [wkeys(L, 1 - s % 2, j)[v]])
                return fn
            return [lambda j, a, b: ts(e3[:, a:b], ps[:, c + a:c + b], shift, A_.add, [kx], [n + "3_%d" % j], scale * MAGIC, A_.mult),
                    lambda j, a, b: ts(e4[:, a:b], e3[:, a:b], EMASK, A_.bitwise_and, [n + "3_%d" % j], [n + "4_%d" % j]),
                    lambda j, a, b: tt(T.W0[:, 8 * L + 4 * j:8 * L + 4 * j + 4], e4[:, a:b], H(cn + a, cn + b), A_.add,
                                       [n + "4_%d" % j, kn], wkeys(L, 0, j))] + [stage(s) for s in range(4)]

        a_steps = steps(0, "a", T.pYB, 0, yname[1], 0.5, 47.0, 128, "pH:A", T.a3, T.a4) + [
            lambda j, a, b: tt(T.a1[:, a:b], T.W0[:, 4 * j:4 * j + 4], T.pKB[:, a:b], A_.max, wkeys(0, 0, j) + [kname[1]], ["a1_%d" % j]),
            lambda j, a, b: tt(H(a, b), T.a1[:, a:b], T.pKA[:, a:b], A_.min, ["a1_%d" % j, kname[0]], ["pH:m1_%d" % j])]
        b_steps = steps(1, "e", T.pT, 384, "pT:x", 1.0, 15.5, 256, "pH:B", T.e3, T.e4)

        def run(todo):
            for fn in todo:
                for x in parts:
                    fn(*x)

        act(T.y0[:], T.yb[:, 0:2048].indirect(offb), AF.Copy, ["yb0", "yb1", "yb2", koffb], ["y0"])
        act(T.lsT[:], T.pS[:, 128:256], AF.Sign, ["pS:b"], ["lsT"], bias=128.0)
        act(T.nlf[:], T.pS[:, 128:256], AF.Sign, ["pS:b"], ["nlf"], bias=5.5, scale=-1.0)
        for b in range(3):
            mm(KB_[b][:, 0:256], T.y0[:], blk(T.Wn, b, 256), False, True, ["y0", "Wn%d" % b], [kname[b]])
        act(blk(T.sX, 1, 256), T.pKB[:, 0:256], AF.Sign, [kname[1]], ["sX1"])
        for b in (0, 2):
            ts(blk(T.sX, b, 256), KB_[b][:, 0:256], 1.0, A_.min, [kname[b]], ["sX%d" % b], -1.0, A_.max)
        lin(xA, yname[1], [(T.lsT[:], T.nLin[:], ["lsT", "nLin"]), Bk(T.kT[:], "kT", 1), Bk(T.nfT[:], "nfT", 1)])
        lin(xB, "pT:x", [(T.kT[:], T.nLin[:], ["kT", "nLin"])], final=False)
        lin(valA, "pS:d", [(Id[-256.0], T.nlf[:], [In(-256), "nlf"])]
            + [(blk(T.sX, l), weight(l)[0], ["sX%d" % (l // 2), weight(l)[1]]) for l in range(6)])
        lin(T.pYA[:, 256:384], "pYA:z", [(Id[1.0], T.Zb[:], ["Zb"]), (Id[-1.0], T.y0[:], ["y0", In(-1)])])
        if last:
            act(T.Zf[:], T.pYA[:, 256:384], AF.Abs, ["pYA:z"], ["Zf"])
            dma("s", T.yz[:], T.Zf[:], "stz", ["Zf"], [])
        else:
            act(T.Zb[:], T.pYA[:, 256:384], AF.Abs, ["pYA:z"], ["Zb"])
        if t == 0:
            count()
        for n in range(GT):
            run(a_steps[n:n + 1])
            if t == 0 and n < 2:
                consts_g(n)
        ts(T.gT[:], valA, 255.5, A_.is_ge, ["pS:d"], ["gT"], 0.5, A_.subtract)
        run(a_steps[GT:LEAD])
        lin(xB, "pT:x", [Bk(T.gT[:], "gT", 0)], first=False)

        lin(LA, "pYB:l", [Cc(0), Bk(T.kT[:], "kT", 3), Bk(T.lsT[:], "lsT", 2), Bk(T.nlf[:], "nlf", 2), Bk(T.gT[:], "gT", 3)])
        lin(T.pS[:, 0:128], "pS:a", [Cc(1), Bk(T.kT[:], "kT", 2), Bk(T.gT[:], "gT", 3)])
        act(T.sT[:], LA, AF.Sign, ["pYB:l"], ["sT"], scale=-1.0)
        act(T.ab[:], T.pS[:, 0:128], AF.Abs, ["pS:a"], ["ab"], scale=2.0)
        lin(T.pKB[:, 0:128], kname[1], [(T.If[:], T.fil[:], ["If", "fil"]), (Id[8192.0], T.sT[:], [In(8192), "sT"])])
        if not last:
            u0()
        rest = [(0, T.pU[:, 0:256], "pU:U"), (1, T.pYA[:, 0:256], yname[0]), (2, T.pS[:, 128:384], "pS:b"), (3, T.pYB[:, 256:512], "pYB:x")]
        if not last:
            u1()
        else:
            yx_part(*rest[0])
        lin(T.pKA[:, 0:128], kname[0], [Cc(2), Bk(T.kT[:], "kT", 4), (Id[1.0], T.ab[:], ["ab"])])
        if last:
            yx_out(*rest[0])
            for x in rest[1:]:
                yx_part(*x)
                yx_out(*x)
        else:
            act(T.X[:, 4096:4112], T.X[:, 0:16], AF.Copy, ["X"], ["Xpad"])
            u2()
            u2b()
            u3()

        for n in range(len(b_steps)):
            run(b_steps[n:n + 1])
            for m in FILL[n]:
                a_steps[m // 2](*parts[m % 2])
        An, kAn = blk(T.A, t + 1), allp("A%d" % (t + 1))
        for j, a, b in parts:
            tt(T.m2[:, a:b], T.W0[:, 8 + 4 * j:12 + 4 * j], H(a, b), A_.max, wkeys(1, 0, j) + ["pH:m1_%d" % j], ["m2_%d" % j])
        for j, a, b in parts:
            ts(T.A[:, 128 * t + 128 + a:128 * t + 128 + b], T.m2[:, a:b], 4095, A_.bitwise_and, ["m2_%d" % j], [kAn[j]])
        if not last:
            send(t + 1, An, blk(T.B, t + 1), "rn%d" % (t + 1), kAn)
        else:
            ends = [(T.pT[0:64, 0:128], "pT:a", "a"), (T.pKA[0:64, 0:128], kname[0], "s")]
            for j, a, b in parts:
                ts(T.yaf[:, a:b], T.A[:, 128 * RO + a:128 * RO + b].indirect(T.orev[:, 0:4]), -2048.0, A_.add, [kAn[j], "orev"], ["yaf%d" % j])
                mm(ends[j][0], T.yaf[:, a:b], T.IdH[:], True, True, ["yaf%d" % j, "IdH"], [ends[j][1]])
            for j, a, b in parts:
                ts(T.yao[0:64, 128 * j:128 * j + 128], ends[j][0], 2048.0, A_.add, [ends[j][1]], ["yao%d" % j])
                dma(ends[j][2], T.ya[a:b, :], T.yao[0:64, 128 * j:128 * j + 128], "sta%d" % j, ["yao%d" % j], [])

    for s in sorted(total):
        wait("g", (s, total[s]))
